import numpy as np
import ml_dtypes


def mxq(x, axis, fmt="e4m3"):
    dtype, down = {"e4m3": (ml_dtypes.float8_e4m3fn, 7), "e5m2": (ml_dtypes.float8_e5m2, 14)}[fmt]
    v = np.moveaxis(np.asarray(x, np.float32).astype(ml_dtypes.bfloat16).astype(np.float64), axis, -1)
    blocks = v.reshape(v.shape[:-1] + (-1, 32))
    amax = np.abs(blocks).max(-1, keepdims=True)
    byte = np.maximum(np.where(amax > 0, np.frexp(amax)[1] - 1 + 127, 0) - down, 1)
    scale = np.exp2(byte - 127.0)
    codes = (blocks / scale).astype(np.float32).astype(dtype).astype(np.float64)
    return np.moveaxis((codes * scale).reshape(v.shape), -1, axis)


WIDE = False


def mx_kscale(k):
    if not WIDE:
        return np.ones(k)
    levels = np.array([10, -10, 5, -5, 0])
    if k % 512:
        return np.exp2(np.random.permutation(np.resize(levels, k // 32))).repeat(32)
    a = np.empty((k // 512, 16))
    for p in range(k // 512):
        a[p, :8] = np.random.permutation(np.resize(levels, 8))
        for g in range(8):
            far = levels[np.abs(levels - a[p, g]) >= 10]
            a[p, g + 8] = far[np.random.randint(len(far))]
    return np.exp2(a.ravel()).repeat(32)


def f64(x):
    return np.asarray(x).astype(np.float64)


def striped(idx):
    return np.tile(idx.reshape(-1, 16).T, (8, 1)).astype(np.uint16)


def unstriped(offs):
    return offs[:16].T.reshape(-1).astype(np.int64)


E2M1 = np.array([0.0, 0.5, 1.0, 1.5, 2.0, 3.0, 4.0, 6.0, -0.0, -0.5, -1.0, -1.5, -2.0, -3.0, -4.0, -6.0])


def pack_weight(w, fmt):
    k, n = w.shape
    w = f64(np.asarray(w, np.float32).astype(ml_dtypes.bfloat16)).reshape(k // 32, 32, n)
    amax = np.abs(w).max(1)
    if fmt == "e4m3":
        byte = np.frexp(amax)[1] - 1 + 127 - 7
    else:
        mant, ex = np.frexp(amax / 6.0)
        byte = np.where(mant > 0.5, ex, ex - 1) + 127
    byte = np.clip(np.where(amax > 0, byte, 1), 1, 254)
    scaled = (w * np.exp2(127.0 - byte)[:, None, :]).reshape(k, n).astype(np.float32)
    by_word = np.ascontiguousarray(scaled.reshape(k // 512, 128, 4, n).transpose(0, 1, 3, 2))
    if fmt == "e4m3":
        words = by_word.astype(ml_dtypes.float8_e4m3fn).view(np.uint8)
    else:
        c = by_word.astype(ml_dtypes.float4_e2m1fn).view(np.uint8) & 0xF
        words = (c[..., 0::2] | (c[..., 1::2] << 4)).reshape(k // 512, 128, 2 * n)
    return np.ascontiguousarray(words), np.ascontiguousarray(byte.astype(np.uint8).reshape(k // 512, 16, n))


def unpack_weight(words, scales, fmt):
    g, _, n = scales.shape
    words = np.ascontiguousarray(words).reshape(g, 128, n, -1)
    if fmt == "e4m3":
        vals = words.view(ml_dtypes.float8_e4m3fn).astype(np.float64)
    else:
        nib = np.empty((g, 128, n, 4), np.uint8)
        nib[..., 0::2] = words & 0xF
        nib[..., 1::2] = words >> 4
        vals = E2M1[nib]
    vals = vals * np.repeat(np.exp2(scales.astype(np.float64) - 127.0), 8, axis=1)[..., None]
    return vals.transpose(0, 1, 3, 2).reshape(g * 512, n)


def gelu(v):
    return 0.5 * v * (1.0 + np.tanh(np.sqrt(2.0 / np.pi) * (v + 0.044715 * v**3)))


K, H, N, T, S, T2 = 1024, 1536, 512, 2048, 1024, 2048

def setup_inputs():
    n = np.random.standard_normal
    s = mx_kscale(K)[:, None]
    u = mx_kscale(H)[:, None]
    tab_words, tab_scales = pack_weight(n((K, T)) * s, "e4m3")
    w4_words, w4_scales = pack_weight(n((H, N)) / np.sqrt(H) / u, "e2m1")
    return {
        "tab_words": tab_words,
        "tab_scales": tab_scales,
        "offs": striped(np.random.permutation(T)[:S]),
        "w1": (n((K, H)) / np.sqrt(K) / s).astype(np.float32),
        "cd": (np.exp(0.3 * n(H)) * u[:, 0]).astype(np.float32),
        "w4_words": w4_words,
        "w4_scales": w4_scales,
        "offs2": striped(np.random.permutation(T2)[:S]),
        "wgo": np.exp(0.3 * n((128, S))).astype(np.float32),
    }

def reference(tab_words, tab_scales, offs, w1, cd, w4_words, w4_scales, offs2, wgo):
    v = unpack_weight(tab_words, tab_scales, "e4m3")[:, unstriped(offs)]
    a = mxq(f64(w1), 0, "e4m3").T @ v
    h = f64(cd)[:, None] * (a * np.abs(a))
    w4 = unpack_weight(w4_words, w4_scales, "e2m1")
    y = -(w4.T @ mxq(h, 0, "e4m3"))
    out = np.zeros((N, T2))
    out[:, unstriped(offs2)] = np.tile(f64(wgo), (N // 128, 1)) * y
    return out

@@ -1,0 +1,201 @@
+from contextlib import ExitStack
+
+import concourse.mybir as mybir
+
+K, H, N, T, S, T2 = 1024, 1536, 512, 2048, 1024, 2048
+FLOPS = 2 * S * H * (K + N)
+
+F32 = mybir.dt.float32
+BF16 = mybir.dt.bfloat16
+I32 = mybir.dt.int32
+U32 = mybir.dt.uint32
+U16 = mybir.dt.uint16
+U8 = mybir.dt.uint8
+FP8X4 = mybir.dt.float8_e4m3fn_x4
+FP4X4 = mybir.dt.float4_e2m1fn_x4
+ACT = mybir.ActivationFunctionType
+MULT = mybir.AluOpType.mult
+
+P = 128
+PACK = 4
+PASS = P * PACK
+KP = K // PASS
+HP = H // PASS
+NT = N // P
+HALF = 512
+HALVES = S // HALF
+LIST_COLS = HALF // 16
+TOK = 128
+
+
+def tile_list_contact_drag_store_kernel(
+    tc, tab_words, tab_scales, offs, w1, cd, w4_words, w4_scales, offs2, wgo, out
+):
+    nc = tc.nc
+    with ExitStack() as ctx:
+        keep = ctx.enter_context(tc.tile_pool(name="keep", bufs=1))
+        ring = ctx.enter_context(tc.tile_pool(name="ring", bufs=4))
+        psum_a = ctx.enter_context(tc.psum_pool(name="psum_a", bufs=4))
+        psum_y = ctx.enter_context(tc.psum_pool(name="psum_y", bufs=1))
+
+        def kept(shape, dtype, name):
+            return keep.tile(shape, dtype, name=name, align_bytes=64)
+
+        pick = keep.tile([P, S // 16], U16, name="pick")
+        place = keep.tile([P, S // 16], U16, name="place")
+        tab_w = [kept([P, T], I32, f"tab_w{a}") for a in range(KP)]
+        tab_s = kept([P, T], U8, "tab_s")
+        w1_raw = [[kept([P, PACK, PASS], F32, f"w1_raw{b}{a}") for a in range(KP)] for b in range(HP)]
+        cd_sb = kept([P, HP, PACK], F32, "cd_sb")
+        w4_w = kept([P, HP, 2 * N], U8, "w4_w")
+        w4_s = kept([P, HP, N], U8, "w4_s")
+        wgo_sb = kept([P, S], F32, "wgo_sb")
+        pages = [kept([P, T2], F32, f"page{n}") for n in range(NT)]
+
+        nc.gpsimd.memset(tab_s[:].bitcast(I32), 0)
+        nc.gpsimd.memset(w4_s[:].bitcast(I32), 0)
+        for page in pages:
+            nc.gpsimd.memset(page[:], 0.0)
+
+        def load_w1(b, a):
+            rows = w1[PASS * a : PASS * (a + 1), PASS * b : PASS * (b + 1)]
+            nc.sync.dma_start(w1_raw[b][a][:], rows.rearrange("(p j) c -> p j c", j=PACK))
+
+        def load_tab(a):
+            nc.sync.dma_start(tab_w[a][:], tab_words[a].rearrange("p t i -> p (t i)").bitcast(I32))
+
+        nc.sync.dma_start(pick[:], offs)
+        load_tab(0)
+        for q in range(4):
+            nc.sync.dma_start(
+                tab_s[32 * q : 32 * q + 4 * KP, :].bitcast(I32), tab_scales[:, 4 * q : 4 * q + 4, :].bitcast(I32)
+            )
+        load_w1(0, 0)
+        load_tab(1)
+        nc.sync.dma_start(cd_sb[:], cd.rearrange("(b p t) -> p b t", b=HP, t=PACK))
+        load_w1(0, 1)
+        for a in range(KP):
+            load_w1(1, a)
+        for q in range(4):
+            nc.sync.dma_start(
+                w4_s[32 * q : 32 * q + 4, :, :].bitcast(I32),
+                w4_scales[:, 4 * q : 4 * q + 4, :].rearrange("a r n -> r a n").bitcast(I32),
+            )
+        nc.sync.dma_start(w4_w[:].bitcast(I32), w4_words.rearrange("a p c -> p a c").bitcast(I32))
+        for a in range(KP):
+            load_w1(2, a)
+        nc.sync.dma_start(place[:], offs2)
+        nc.sync.dma_start(wgo_sb[:], wgo)
+
+        v_w = [[kept([P, HALF], U32, f"v_w{g}{a}") for a in range(KP)] for g in range(HALVES)]
+        v_s = [kept([P, HALF], U8, f"v_s{g}") for g in range(HALVES)]
+
+        def list_half(lst, g):
+            return lst[:, LIST_COLS * g : LIST_COLS * (g + 1)]
+
+        def gather_words(g, a):
+            nc.vector.tensor_copy(v_w[g][a][:], tab_w[a][:].bitcast(U32).indirect(list_half(pick, g)))
+
+        def gather_scales(g):
+            nc.vector.tensor_copy(v_s[g][:], tab_s[:].indirect(list_half(pick, g)))
+
+        for g in range(HALVES):
+            gather_words(g, 0)
+        for g in range(HALVES):
+            gather_scales(g)
+        for g in range(HALVES):
+            gather_words(g, 1)
+
+        w1_w = {}
+        w1_s = {}
+
+        def quantise_w1(b, a, u, on_vector):
+            src = w1_raw[b][a][:].rearrange("p j (m t) -> p m j t", t=PACK)[:, :, :, 2 * u : 2 * u + 2]
+            grouped = ring.tile([P, 2 * PASS], BF16, name="w1_grouped", align_bytes=64)
+            dst = grouped[:].rearrange("p (t m j) -> p m j t", t=2, j=PACK)
+            if on_vector:
+                nc.vector.tensor_copy(dst, src)
+            else:
+                nc.scalar.copy(dst, src)
+            w1_w[b, a, u] = kept([P, 2 * P], U32, f"w1_w{b}{a}{u}")
+            w1_s[b, a, u] = kept([P, 2 * P], U8, f"w1_s{b}{a}{u}")
+            nc.vector.quantize_mx(w1_w[b, a, u][:].bitcast(FP8X4), w1_s[b, a, u][:], grouped[:])
+
+        def drag(b, g, mags):
+            h_bf = ring.tile([P, PACK * HALF], BF16, name="h_bf", align_bytes=64, bufs=3)
+            for s in range(HALF // TOK):
+                cols = slice(TOK * s, TOK * (s + 1))
+                bank = psum_a.tile([P, PACK, TOK], F32, name="bank")
+                for t in range(PACK):
+                    wcols = slice(P * (t % 2), P * (t % 2 + 1))
+                    for a in range(KP):
+                        nc.tensor.matmul_mx(
+                            bank[:, t, :],
+                            lhsT=w1_w[b, a, t // 2][:, wcols].bitcast(FP8X4),
+                            lhsT_scale=w1_s[b, a, t // 2][:, wcols],
+                            rhs=v_w[g][a][:, cols].bitcast(FP8X4),
+                            rhs_scale=v_s[g][4 * a : P, cols],
+                            start=(a == 0),
+                            stop=(a == KP - 1),
+                        )
+                mag = mags[s] if s in mags else ring.tile([P, HALF], F32, name="mag")
+                mag = mag[:].rearrange("p (t c) -> p t c", t=PACK)
+                for t in range(PACK):
+                    nc.scalar.activation(mag[:, t, :], bank[:, t, :], ACT.Abs, scale=cd_sb[:, b, t : t + 1])
+                dst = h_bf[:, PACK * TOK * s : PACK * TOK * (s + 1)]
+                nc.vector.tensor_tensor(
+                    dst.rearrange("p (c i t) -> p c t i", i=2, t=PACK),
+                    bank[:].rearrange("p t (c i) -> p c t i", i=2),
+                    mag.rearrange("p t (c i) -> p c t i", i=2),
+                    MULT,
+                )
+            h_w = kept([P, HALF], U32, f"h_w{b}{g}")
+            h_s = kept([P, HALF], U8, f"h_s{b}{g}")
+            nc.vector.quantize_mx(h_w[:].bitcast(FP8X4), h_s[:], h_bf[:])
+            return h_w, h_s
+
+        def project(b, y_banks, h_w, h_s):
+            for n in range(NT):
+                nc.tensor.matmul_mx(
+                    y_banks[n][:],
+                    lhsT=w4_w[:, b, 2 * P * n : 2 * P * (n + 1)].bitcast(FP4X4),
+                    lhsT_scale=w4_s[:, b, P * n : P * (n + 1)],
+                    rhs=h_w[:].bitcast(FP8X4),
+                    rhs_scale=h_s[:],
+                    start=(b == 0),
+                    stop=(b == HP - 1),
+                )
+
+        forces = [[kept([P, HALF], F32, f"force{g}{n}") for n in range(NT)] for g in range(HALVES)]
+
+        def negate(g, y_banks):
+            for n in range(NT):
+                nc.scalar.activation(forces[g][n][:], y_banks[n][:], ACT.Copy, scale=-1.0)
+
+        def scatter(g, n):
+            nc.vector.tensor_tensor(
+                pages[n][:].indirect(list_half(place, g)), forces[g][n][:], wgo_sb[:, HALF * g : HALF * (g + 1)], MULT
+            )
+
+        def new_y_banks():
+            return [psum_y.tile([P, HALF], F32, name=f"y_bank{n}") for n in range(NT)]
+
+        y_first = new_y_banks()
+        h_second = []
+        for b in range(HP):
+            for a in range(KP):
+                for u in range(2):
+                    quantise_w1(b, a, u, on_vector=(u == 0 and (b, a) != (0, 0)))
+            project(b, y_first, *drag(b, 0, {}))
+            lent = {n: forces[0][n] for n in (2, 3)} if b == HP - 1 else {}
+            h_second.append(drag(b, 1, lent))
+        negate(0, y_first)
+        y_second = new_y_banks()
+        for b in range(HP):
+            project(b, y_second, *h_second[b])
+        for n in range(NT):
+            scatter(0, n)
+        negate(1, y_second)
+        for n in range(NT):
+            scatter(1, n)
+            nc.sync.dma_start(out[P * n : P * (n + 1), :], pages[n][:])

@@ -52,10 +52,10 @@ def tile_list_contact_drag_store_kernel(
         wgo_sb = kept([P, S], F32, "wgo_sb")
         pages = [kept([P, T2], F32, f"page{n}") for n in range(NT)]
 
-        nc.gpsimd.memset(tab_s[:].bitcast(I32), 0)
-        nc.gpsimd.memset(w4_s[:].bitcast(I32), 0)
+        nc.vector.memset(tab_s[:].bitcast(I32), 0)
+        nc.vector.memset(w4_s[:].bitcast(I32), 0)
         for page in pages:
-            nc.gpsimd.memset(page[:], 0.0)
+            nc.vector.memset(page[:], 0.0)
 
         def load_w1(b, a):
             rows = w1[PASS * a : PASS * (a + 1), PASS * b : PASS * (b + 1)]
@@ -65,15 +65,15 @@ def tile_list_contact_drag_store_kernel(
             nc.sync.dma_start(tab_w[a][:], tab_words[a].rearrange("p t i -> p (t i)").bitcast(I32))
 
         nc.sync.dma_start(pick[:], offs)
+        nc.sync.dma_start(cd_sb[:], cd.rearrange("(b p t) -> p b t", b=HP, t=PACK))
         load_tab(0)
         for q in range(4):
             nc.sync.dma_start(
                 tab_s[32 * q : 32 * q + 4 * KP, :].bitcast(I32), tab_scales[:, 4 * q : 4 * q + 4, :].bitcast(I32)
             )
         load_w1(0, 0)
-        load_tab(1)
-        nc.sync.dma_start(cd_sb[:], cd.rearrange("(b p t) -> p b t", b=HP, t=PACK))
         load_w1(0, 1)
+        load_tab(1)
         for a in range(KP):
             load_w1(1, a)
         for q in range(4):
@@ -93,8 +93,9 @@ def tile_list_contact_drag_store_kernel(
         def list_half(lst, g):
             return lst[:, LIST_COLS * g : LIST_COLS * (g + 1)]
 
-        def gather_words(g, a):
-            nc.vector.tensor_copy(v_w[g][a][:], tab_w[a][:].bitcast(U32).indirect(list_half(pick, g)))
+        def gather_words(g, a, lo=0, hi=HALF):
+            entries = pick[:, (HALF * g + lo) // 16 : (HALF * g + hi) // 16]
+            nc.vector.tensor_copy(v_w[g][a][:, lo:hi], tab_w[a][:].bitcast(U32).indirect(entries))
 
         def gather_scales(g):
             nc.vector.tensor_copy(v_s[g][:], tab_s[:].indirect(list_half(pick, g)))
@@ -103,70 +104,67 @@ def tile_list_contact_drag_store_kernel(
             gather_words(g, 0)
         for g in range(HALVES):
             gather_scales(g)
-        for g in range(HALVES):
-            gather_words(g, 1)
 
-        w1_w = {}
-        w1_s = {}
+        w1_bf, w1_w, w1_s = {}, {}, {}
+        h_bf, h_w, h_s = {}, {}, {}
+        forces = [[kept([P, HALF], F32, f"force{g}{n}") for n in range(NT)] for g in range(HALVES)]
 
-        def quantise_w1(b, a, u, on_vector):
+        def round_w1(b, a, u, engine_copy):
             src = w1_raw[b][a][:].rearrange("p j (m t) -> p m j t", t=PACK)[:, :, :, 2 * u : 2 * u + 2]
-            grouped = ring.tile([P, 2 * PASS], BF16, name="w1_grouped", align_bytes=64)
-            dst = grouped[:].rearrange("p (t m j) -> p m j t", t=2, j=PACK)
-            if on_vector:
-                nc.vector.tensor_copy(dst, src)
-            else:
-                nc.scalar.copy(dst, src)
+            w1_bf[b, a, u] = ring.tile([P, 2 * PASS], BF16, name="w1_bf", align_bytes=64)
+            engine_copy(w1_bf[b, a, u][:].rearrange("p (t m j) -> p m j t", t=2, j=PACK), src)
+
+        def quantise_w1(b, a, u):
             w1_w[b, a, u] = kept([P, 2 * P], U32, f"w1_w{b}{a}{u}")
             w1_s[b, a, u] = kept([P, 2 * P], U8, f"w1_s{b}{a}{u}")
-            nc.vector.quantize_mx(w1_w[b, a, u][:].bitcast(FP8X4), w1_s[b, a, u][:], grouped[:])
+            nc.vector.quantize_mx(w1_w[b, a, u][:].bitcast(FP8X4), w1_s[b, a, u][:], w1_bf[b, a, u][:])
 
-        def drag(b, g, mags):
-            h_bf = ring.tile([P, PACK * HALF], BF16, name="h_bf", align_bytes=64, bufs=3)
-            for s in range(HALF // TOK):
-                cols = slice(TOK * s, TOK * (s + 1))
-                bank = psum_a.tile([P, PACK, TOK], F32, name="bank")
+        def drag(b, g, s):
+            if s == 0:
+                h_bf[b, g] = ring.tile([P, PACK * HALF], BF16, name="h_bf", align_bytes=64, bufs=3)
+            cols = slice(TOK * s, TOK * (s + 1))
+            bank = psum_a.tile([P, PACK, TOK], F32, name="bank")
+            for a in range(KP):
                 for t in range(PACK):
                     wcols = slice(P * (t % 2), P * (t % 2 + 1))
-                    for a in range(KP):
-                        nc.tensor.matmul_mx(
-                            bank[:, t, :],
-                            lhsT=w1_w[b, a, t // 2][:, wcols].bitcast(FP8X4),
-                            lhsT_scale=w1_s[b, a, t // 2][:, wcols],
-                            rhs=v_w[g][a][:, cols].bitcast(FP8X4),
-                            rhs_scale=v_s[g][4 * a : P, cols],
-                            start=(a == 0),
-                            stop=(a == KP - 1),
-                        )
-                mag = mags[s] if s in mags else ring.tile([P, HALF], F32, name="mag")
-                mag = mag[:].rearrange("p (t c) -> p t c", t=PACK)
-                for t in range(PACK):
-                    nc.scalar.activation(mag[:, t, :], bank[:, t, :], ACT.Abs, scale=cd_sb[:, b, t : t + 1])
-                dst = h_bf[:, PACK * TOK * s : PACK * TOK * (s + 1)]
-                nc.vector.tensor_tensor(
-                    dst.rearrange("p (c i t) -> p c t i", i=2, t=PACK),
-                    bank[:].rearrange("p t (c i) -> p c t i", i=2),
-                    mag.rearrange("p t (c i) -> p c t i", i=2),
-                    MULT,
-                )
-            h_w = kept([P, HALF], U32, f"h_w{b}{g}")
-            h_s = kept([P, HALF], U8, f"h_s{b}{g}")
-            nc.vector.quantize_mx(h_w[:].bitcast(FP8X4), h_s[:], h_bf[:])
-            return h_w, h_s
+                    nc.tensor.matmul_mx(
+                        bank[:, t, :],
+                        lhsT=w1_w[b, a, t // 2][:, wcols].bitcast(FP8X4),
+                        lhsT_scale=w1_s[b, a, t // 2][:, wcols],
+                        rhs=v_w[g][a][:, cols].bitcast(FP8X4),
+                        rhs_scale=v_s[g][4 * a : P, cols],
+                        start=(a == 0 and t == 0),
+                        stop=(a == KP - 1 and t == PACK - 1),
+                    )
+            lent = (b, g) == (HP - 1, HALVES - 1) and s >= 2
+            mag = forces[0][s] if lent else ring.tile([P, HALF], F32, name="mag")
+            mag = mag[:].rearrange("p (t c) -> p t c", t=PACK)
+            for t in range(PACK):
+                nc.scalar.activation(mag[:, t, :], bank[:, t, :], ACT.Abs, scale=cd_sb[:, b, t : t + 1])
+            dst = h_bf[b, g][:, PACK * TOK * s : PACK * TOK * (s + 1)]
+            nc.vector.tensor_tensor(
+                dst.rearrange("p (c i t) -> p c t i", i=2, t=PACK),
+                bank[:].rearrange("p t (c i) -> p c t i", i=2),
+                mag.rearrange("p t (c i) -> p c t i", i=2),
+                MULT,
+            )
 
-        def project(b, y_banks, h_w, h_s):
+        def quantise_h(b, g):
+            h_w[b, g] = kept([P, HALF], U32, f"h_w{b}{g}")
+            h_s[b, g] = kept([P, HALF], U8, f"h_s{b}{g}")
+            nc.vector.quantize_mx(h_w[b, g][:].bitcast(FP8X4), h_s[b, g][:], h_bf[b, g][:])
+
+        def project(b, g, y_banks):
             for n in range(NT):
                 nc.tensor.matmul_mx(
                     y_banks[n][:],
                     lhsT=w4_w[:, b, 2 * P * n : 2 * P * (n + 1)].bitcast(FP4X4),
                     lhsT_scale=w4_s[:, b, P * n : P * (n + 1)],
-                    rhs=h_w[:].bitcast(FP8X4),
-                    rhs_scale=h_s[:],
+                    rhs=h_w[b, g][:].bitcast(FP8X4),
+                    rhs_scale=h_s[b, g][:],
                     start=(b == 0),
                     stop=(b == HP - 1),
                 )
-
-        forces = [[kept([P, HALF], F32, f"force{g}{n}") for n in range(NT)] for g in range(HALVES)]
 
         def negate(g, y_banks):
             for n in range(NT):
@@ -180,19 +178,40 @@ def tile_list_contact_drag_store_kernel(
         def new_y_banks():
             return [psum_y.tile([P, HALF], F32, name=f"y_bank{n}") for n in range(NT)]
 
+        round_w1(0, 0, 0, nc.scalar.copy)
+        round_w1(0, 0, 1, nc.scalar.copy)
+        round_w1(0, 1, 0, nc.vector.tensor_copy)
+        round_w1(0, 1, 1, nc.scalar.copy)
+        quantise_w1(0, 0, 0)
+        quantise_w1(0, 0, 1)
+        quantise_w1(0, 1, 0)
+        gather_words(0, 1, 0, HALF // 2)
+        quantise_w1(0, 1, 1)
+        gather_words(0, 1, HALF // 2, HALF)
+        gather_words(1, 1)
+
         y_first = new_y_banks()
-        h_second = []
+        steps = HALF // TOK
         for b in range(HP):
-            for a in range(KP):
-                for u in range(2):
-                    quantise_w1(b, a, u, on_vector=(u == 0 and (b, a) != (0, 0)))
-            project(b, y_first, *drag(b, 0, {}))
-            lent = {n: forces[0][n] for n in (2, 3)} if b == HP - 1 else {}
-            h_second.append(drag(b, 1, lent))
+            for g in range(HALVES):
+                for s in range(steps):
+                    drag(b, g, s)
+                    if s == 0 and g == 1:
+                        quantise_h(b, 0)
+                        project(b, 0, y_first)
+                    if s == 0 and g == 0 and b > 0:
+                        quantise_h(b - 1, 1)
+                    if b + 1 < HP and s == 1:
+                        round_w1(b + 1, g, 0, nc.vector.tensor_copy)
+                        round_w1(b + 1, g, 1, nc.scalar.copy)
+                    if b + 1 < HP and s == 2:
+                        quantise_w1(b + 1, g, 0)
+                        quantise_w1(b + 1, g, 1)
+        quantise_h(HP - 1, 1)
         negate(0, y_first)
         y_second = new_y_banks()
         for b in range(HP):
-            project(b, y_second, *h_second[b])
+            project(b, 1, y_second)
         for n in range(NT):
             scatter(0, n)
         negate(1, y_second)

@@ -35,8 +35,7 @@ def tile_list_contact_drag_store_kernel(
     with ExitStack() as ctx:
         keep = ctx.enter_context(tc.tile_pool(name="keep", bufs=1))
         ring = ctx.enter_context(tc.tile_pool(name="ring", bufs=4))
-        psum_a = ctx.enter_context(tc.psum_pool(name="psum_a", bufs=4))
-        psum_y = ctx.enter_context(tc.psum_pool(name="psum_y", bufs=1))
+        psum = ctx.enter_context(tc.psum_pool(name="psum", bufs=8))
 
         def kept(shape, dtype, name):
             return keep.tile(shape, dtype, name=name, align_bytes=64)
@@ -55,7 +54,7 @@ def tile_list_contact_drag_store_kernel(
         nc.vector.memset(tab_s[:].bitcast(I32), 0)
         nc.vector.memset(w4_s[:].bitcast(I32), 0)
         for page in pages:
-            nc.vector.memset(page[:], 0.0)
+            nc.vector.memset(page[:].bitcast(I32), 0)
 
         def load_w1(b, a):
             rows = w1[PASS * a : PASS * (a + 1), PASS * b : PASS * (b + 1)]
@@ -110,41 +109,45 @@ def tile_list_contact_drag_store_kernel(
         forces = [[kept([P, HALF], F32, f"force{g}{n}") for n in range(NT)] for g in range(HALVES)]
 
         def round_w1(b, a, u, engine_copy):
-            src = w1_raw[b][a][:].rearrange("p j (m t) -> p m j t", t=PACK)[:, :, :, 2 * u : 2 * u + 2]
-            w1_bf[b, a, u] = ring.tile([P, 2 * PASS], BF16, name="w1_bf", align_bytes=64)
-            engine_copy(w1_bf[b, a, u][:].rearrange("p (t m j) -> p m j t", t=2, j=PACK), src)
+            if u == 0:
+                w1_bf[b, a] = ring.tile([P, PACK * PASS], BF16, name="w1_bf", align_bytes=64, bufs=2)
+            half = slice(P // 2 * u, P // 2 * (u + 1))
+            src = w1_raw[b][a][:].rearrange("p j (m t) -> p m t j", t=PACK)
+            dst = w1_bf[b, a][:].rearrange("p (t m j) -> p m t j", t=PACK, j=PACK)
+            engine_copy(dst[:, half, :, :], src[:, half, :, :])
 
-        def quantise_w1(b, a, u):
-            w1_w[b, a, u] = kept([P, 2 * P], U32, f"w1_w{b}{a}{u}")
-            w1_s[b, a, u] = kept([P, 2 * P], U8, f"w1_s{b}{a}{u}")
-            nc.vector.quantize_mx(w1_w[b, a, u][:].bitcast(FP8X4), w1_s[b, a, u][:], w1_bf[b, a, u][:])
+        def quantise_w1(b, a):
+            w1_w[b, a] = kept([P, PASS], U32, f"w1_w{b}{a}")
+            w1_s[b, a] = kept([P, PASS], U8, f"w1_s{b}{a}")
+            nc.vector.quantize_mx(w1_w[b, a][:].bitcast(FP8X4), w1_s[b, a][:], w1_bf[b, a][:])
 
         def drag(b, g, s):
             if s == 0:
                 h_bf[b, g] = ring.tile([P, PACK * HALF], BF16, name="h_bf", align_bytes=64, bufs=3)
             cols = slice(TOK * s, TOK * (s + 1))
-            bank = psum_a.tile([P, PACK, TOK], F32, name="bank")
+            bank = psum.tile([P, HALF], F32, name="bank")
+            bank = bank[:].rearrange("p (t c) -> p t c", t=PACK)
             for a in range(KP):
                 for t in range(PACK):
-                    wcols = slice(P * (t % 2), P * (t % 2 + 1))
+                    wcols = slice(P * t, P * (t + 1))
                     nc.tensor.matmul_mx(
                         bank[:, t, :],
-                        lhsT=w1_w[b, a, t // 2][:, wcols].bitcast(FP8X4),
-                        lhsT_scale=w1_s[b, a, t // 2][:, wcols],
+                        lhsT=w1_w[b, a][:, wcols].bitcast(FP8X4),
+                        lhsT_scale=w1_s[b, a][:, wcols],
                         rhs=v_w[g][a][:, cols].bitcast(FP8X4),
                         rhs_scale=v_s[g][4 * a : P, cols],
                         start=(a == 0 and t == 0),
                         stop=(a == KP - 1 and t == PACK - 1),
                     )
             lent = (b, g) == (HP - 1, HALVES - 1) and s >= 2
-            mag = forces[0][s] if lent else ring.tile([P, HALF], F32, name="mag")
+            mag = forces[0][s] if lent else ring.tile([P, HALF], F32, name="mag", bufs=8)
             mag = mag[:].rearrange("p (t c) -> p t c", t=PACK)
             for t in range(PACK):
                 nc.scalar.activation(mag[:, t, :], bank[:, t, :], ACT.Abs, scale=cd_sb[:, b, t : t + 1])
             dst = h_bf[b, g][:, PACK * TOK * s : PACK * TOK * (s + 1)]
             nc.vector.tensor_tensor(
                 dst.rearrange("p (c i t) -> p c t i", i=2, t=PACK),
-                bank[:].rearrange("p t (c i) -> p c t i", i=2),
+                bank.rearrange("p t (c i) -> p c t i", i=2),
                 mag.rearrange("p t (c i) -> p c t i", i=2),
                 MULT,
             )
@@ -154,10 +157,11 @@ def tile_list_contact_drag_store_kernel(
             h_s[b, g] = kept([P, HALF], U8, f"h_s{b}{g}")
             nc.vector.quantize_mx(h_w[b, g][:].bitcast(FP8X4), h_s[b, g][:], h_bf[b, g][:])
 
-        def project(b, g, y_banks):
-            for n in range(NT):
+        def project(g, n):
+            y_bank = psum.tile([P, HALF], F32, name="bank")
+            for b in range(HP):
                 nc.tensor.matmul_mx(
-                    y_banks[n][:],
+                    y_bank[:],
                     lhsT=w4_w[:, b, 2 * P * n : 2 * P * (n + 1)].bitcast(FP4X4),
                     lhsT_scale=w4_s[:, b, P * n : P * (n + 1)],
                     rhs=h_w[b, g][:].bitcast(FP8X4),
@@ -165,32 +169,26 @@ def tile_list_contact_drag_store_kernel(
                     start=(b == 0),
                     stop=(b == HP - 1),
                 )
+            return y_bank
 
-        def negate(g, y_banks):
-            for n in range(NT):
-                nc.scalar.activation(forces[g][n][:], y_banks[n][:], ACT.Copy, scale=-1.0)
+        def negate(g, n, y_bank):
+            nc.scalar.activation(forces[g][n][:], y_bank[:], ACT.Copy, scale=-1.0)
 
         def scatter(g, n):
             nc.vector.tensor_tensor(
                 pages[n][:].indirect(list_half(place, g)), forces[g][n][:], wgo_sb[:, HALF * g : HALF * (g + 1)], MULT
             )
 
-        def new_y_banks():
-            return [psum_y.tile([P, HALF], F32, name=f"y_bank{n}") for n in range(NT)]
-
         round_w1(0, 0, 0, nc.scalar.copy)
         round_w1(0, 0, 1, nc.scalar.copy)
         round_w1(0, 1, 0, nc.vector.tensor_copy)
         round_w1(0, 1, 1, nc.scalar.copy)
-        quantise_w1(0, 0, 0)
-        quantise_w1(0, 0, 1)
-        quantise_w1(0, 1, 0)
+        quantise_w1(0, 0)
         gather_words(0, 1, 0, HALF // 2)
-        quantise_w1(0, 1, 1)
+        quantise_w1(0, 1)
         gather_words(0, 1, HALF // 2, HALF)
         gather_words(1, 1)
 
-        y_first = new_y_banks()
         steps = HALF // TOK
         for b in range(HP):
             for g in range(HALVES):
@@ -198,23 +196,22 @@ def tile_list_contact_drag_store_kernel(
                     drag(b, g, s)
                     if s == 0 and g == 1:
                         quantise_h(b, 0)
-                        project(b, 0, y_first)
                     if s == 0 and g == 0 and b > 0:
                         quantise_h(b - 1, 1)
-                    if b + 1 < HP and s == 1:
-                        round_w1(b + 1, g, 0, nc.vector.tensor_copy)
-                        round_w1(b + 1, g, 1, nc.scalar.copy)
-                    if b + 1 < HP and s == 2:
-                        quantise_w1(b + 1, g, 0)
-                        quantise_w1(b + 1, g, 1)
+                    if b + 1 < HP and g == 0:
+                        if s % 2 == 0:
+                            round_w1(b + 1, s // 2, 0, nc.vector.tensor_copy)
+                            round_w1(b + 1, s // 2, 1, nc.scalar.copy)
+                        else:
+                            quantise_w1(b + 1, s // 2)
         quantise_h(HP - 1, 1)
-        negate(0, y_first)
-        y_second = new_y_banks()
-        for b in range(HP):
-            project(b, 1, y_second)
+        for n in range(NT):
+            negate(0, n, project(0, n))
+        y_second = [project(1, n) for n in range(NT)]
         for n in range(NT):
             scatter(0, n)
-        negate(1, y_second)
+        for n in range(NT):
+            negate(1, n, y_second[n])
         for n in range(NT):
             scatter(1, n)
             nc.sync.dma_start(out[P * n : P * (n + 1), :], pages[n][:])

@@ -15,6 +15,7 @@ FP8X4 = mybir.dt.float8_e4m3fn_x4
 FP4X4 = mybir.dt.float4_e2m1fn_x4
 ACT = mybir.ActivationFunctionType
 MULT = mybir.AluOpType.mult
+ADD = mybir.AluOpType.add
 
 P = 128
 PACK = 4
@@ -26,6 +27,7 @@ HALF = 512
 HALVES = S // HALF
 LIST_COLS = HALF // 16
 TOK = 128
+SPLIT = 96
 
 
 def tile_list_contact_drag_store_kernel(
@@ -73,16 +75,15 @@ def tile_list_contact_drag_store_kernel(
         load_w1(0, 0)
         load_w1(0, 1)
         load_tab(1)
-        for a in range(KP):
-            load_w1(1, a)
+        for b in range(1, HP):
+            for a in range(KP):
+                load_w1(b, a)
         for q in range(4):
             nc.sync.dma_start(
                 w4_s[32 * q : 32 * q + 4, :, :].bitcast(I32),
                 w4_scales[:, 4 * q : 4 * q + 4, :].rearrange("a r n -> r a n").bitcast(I32),
             )
         nc.sync.dma_start(w4_w[:].bitcast(I32), w4_words.rearrange("a p c -> p a c").bitcast(I32))
-        for a in range(KP):
-            load_w1(2, a)
         nc.sync.dma_start(place[:], offs2)
         nc.sync.dma_start(wgo_sb[:], wgo)
 
@@ -108,13 +109,22 @@ def tile_list_contact_drag_store_kernel(
         h_bf, h_w, h_s = {}, {}, {}
         forces = [[kept([P, HALF], F32, f"force{g}{n}") for n in range(NT)] for g in range(HALVES)]
 
-        def round_w1(b, a, u, engine_copy):
-            if u == 0:
-                w1_bf[b, a] = ring.tile([P, PACK * PASS], BF16, name="w1_bf", align_bytes=64, bufs=2)
-            half = slice(P // 2 * u, P // 2 * (u + 1))
+        def round_w1(b, a, lo, hi, engine_copy):
+            if (b, a) not in w1_bf:
+                if b == 0:
+                    w1_bf[b, a] = kept([P, PACK * PASS], BF16, f"w1_first{a}")
+                else:
+                    w1_bf[b, a] = ring.tile([P, PACK * PASS], BF16, name="w1_bf", align_bytes=64, bufs=1)
             src = w1_raw[b][a][:].rearrange("p j (m t) -> p m t j", t=PACK)
             dst = w1_bf[b, a][:].rearrange("p (t m j) -> p m t j", t=PACK, j=PACK)
-            engine_copy(dst[:, half, :, :], src[:, half, :, :])
+            engine_copy(dst[:, lo:hi, :, :], src[:, lo:hi, :, :])
+
+        def gpsimd_copy(dst, src):
+            nc.gpsimd.tensor_scalar(dst, src, 1.0, 0.0, MULT, ADD)
+
+        def round_shared(b, a):
+            round_w1(b, a, 0, SPLIT, gpsimd_copy)
+            round_w1(b, a, SPLIT, P, nc.scalar.copy)
 
         def quantise_w1(b, a):
             w1_w[b, a] = kept([P, PASS], U32, f"w1_w{b}{a}")
@@ -179,31 +189,32 @@ def tile_list_contact_drag_store_kernel(
                 pages[n][:].indirect(list_half(place, g)), forces[g][n][:], wgo_sb[:, HALF * g : HALF * (g + 1)], MULT
             )
 
-        round_w1(0, 0, 0, nc.scalar.copy)
-        round_w1(0, 0, 1, nc.scalar.copy)
-        round_w1(0, 1, 0, nc.vector.tensor_copy)
-        round_w1(0, 1, 1, nc.scalar.copy)
+        round_w1(0, 0, 0, P, nc.scalar.copy)
+        round_w1(0, 1, P // 4, P, nc.scalar.copy)
         quantise_w1(0, 0)
+        round_w1(0, 1, 0, P // 4, nc.vector.tensor_copy)
         gather_words(0, 1, 0, HALF // 2)
         quantise_w1(0, 1)
         gather_words(0, 1, HALF // 2, HALF)
         gather_words(1, 1)
 
-        steps = HALF // TOK
+        round_shared(1, 0)
         for b in range(HP):
-            for g in range(HALVES):
-                for s in range(steps):
-                    drag(b, g, s)
-                    if s == 0 and g == 1:
-                        quantise_h(b, 0)
-                    if s == 0 and g == 0 and b > 0:
+            more = b + 1 < HP
+            for step in range(8):
+                drag(b, step // 4, step % 4)
+                if step == 1:
+                    if more:
+                        quantise_w1(b + 1, 0)
+                        round_shared(b + 1, 1)
+                    if b > 0:
                         quantise_h(b - 1, 1)
-                    if b + 1 < HP and g == 0:
-                        if s % 2 == 0:
-                            round_w1(b + 1, s // 2, 0, nc.vector.tensor_copy)
-                            round_w1(b + 1, s // 2, 1, nc.scalar.copy)
-                        else:
-                            quantise_w1(b + 1, s // 2)
+                if step == (5 if more else 4):
+                    if more:
+                        quantise_w1(b + 1, 1)
+                    if b + 2 < HP:
+                        round_shared(b + 2, 0)
+                    quantise_h(b, 0)
         quantise_h(HP - 1, 1)
         for n in range(NT):
             negate(0, n, project(0, n))

@@ -36,6 +36,7 @@ def tile_list_contact_drag_store_kernel(
     nc = tc.nc
     with ExitStack() as ctx:
         keep = ctx.enter_context(tc.tile_pool(name="keep", bufs=1))
+        shared = ctx.enter_context(tc.tile_pool(name="shared", bufs=1))
         ring = ctx.enter_context(tc.tile_pool(name="ring", bufs=4))
         psum = ctx.enter_context(tc.psum_pool(name="psum", bufs=8))
 
@@ -46,8 +47,12 @@ def tile_list_contact_drag_store_kernel(
         place = keep.tile([P, S // 16], U16, name="place")
         tab_w = [kept([P, T], I32, f"tab_w{a}") for a in range(KP)]
         tab_s = kept([P, T], U8, "tab_s")
-        w1_raw = [[kept([P, PACK, PASS], F32, f"w1_raw{b}{a}") for a in range(KP)] for b in range(HP)]
-        cd_sb = kept([P, HP, PACK], F32, "cd_sb")
+
+        def over_piece(shape, dtype, name, piece):
+            return shared.tile(shape, dtype, name=name, align_bytes=64, offset=4 * PACK * PASS * piece)
+
+        w1_raw = [[over_piece([P, PACK, PASS], F32, f"w1_raw{b}{a}", KP * b + a) for a in range(KP)] for b in range(HP)]
+        cd_sb = [kept([P, PACK], F32, f"cd_sb{b}") for b in range(HP)]
         w4_w = kept([P, HP, 2 * N], U8, "w4_w")
         w4_s = kept([P, HP, N], U8, "w4_s")
         wgo_sb = kept([P, S], F32, "wgo_sb")
@@ -65,9 +70,8 @@ def tile_list_contact_drag_store_kernel(
         def load_tab(a):
             nc.sync.dma_start(tab_w[a][:], tab_words[a].rearrange("p t i -> p (t i)").bitcast(I32))
 
-        nc.sync.dma_start(pick[:], offs)
-        nc.sync.dma_start(cd_sb[:], cd.rearrange("(b p t) -> p b t", b=HP, t=PACK))
         load_tab(0)
+        nc.sync.dma_start(pick[:], offs)
         for q in range(4):
             nc.sync.dma_start(
                 tab_s[32 * q : 32 * q + 4 * KP, :].bitcast(I32), tab_scales[:, 4 * q : 4 * q + 4, :].bitcast(I32)
@@ -75,9 +79,11 @@ def tile_list_contact_drag_store_kernel(
         load_w1(0, 0)
         load_w1(0, 1)
         load_tab(1)
-        for b in range(1, HP):
-            for a in range(KP):
-                load_w1(b, a)
+        for b in range(HP):
+            nc.sync.dma_start(cd_sb[b][:], cd[PASS * b : PASS * (b + 1)].rearrange("(p t) -> p t", t=PACK))
+            if b + 1 < HP:
+                for a in range(KP):
+                    load_w1(b + 1, a)
         for q in range(4):
             nc.sync.dma_start(
                 w4_s[32 * q : 32 * q + 4, :, :].bitcast(I32),
@@ -123,37 +129,46 @@ def tile_list_contact_drag_store_kernel(
             nc.gpsimd.tensor_scalar(dst, src, 1.0, 0.0, MULT, ADD)
 
         def round_shared(b, a):
-            round_w1(b, a, 0, SPLIT, gpsimd_copy)
-            round_w1(b, a, SPLIT, P, nc.scalar.copy)
+            split = P // 2 if b == 1 else SPLIT
+            round_w1(b, a, 0, split, gpsimd_copy)
+            round_w1(b, a, split, P, nc.scalar.copy)
 
         def quantise_w1(b, a):
             w1_w[b, a] = kept([P, PASS], U32, f"w1_w{b}{a}")
             w1_s[b, a] = kept([P, PASS], U8, f"w1_s{b}{a}")
             nc.vector.quantize_mx(w1_w[b, a][:].bitcast(FP8X4), w1_s[b, a][:], w1_bf[b, a][:])
 
+        banks = {}
+
+        def product(b, g, s, a):
+            if a == 0:
+                tile = psum.tile([P, HALF], F32, name="bank")
+                banks[b, g, s] = tile[:].rearrange("p (t c) -> p t c", t=PACK)
+            cols = slice(TOK * s, TOK * (s + 1))
+            for t in range(PACK):
+                wcols = slice(P * t, P * (t + 1))
+                nc.tensor.matmul_mx(
+                    banks[b, g, s][:, t, :],
+                    lhsT=w1_w[b, a][:, wcols].bitcast(FP8X4),
+                    lhsT_scale=w1_s[b, a][:, wcols],
+                    rhs=v_w[g][a][:, cols].bitcast(FP8X4),
+                    rhs_scale=v_s[g][4 * a : P, cols],
+                    start=(a == 0 and t == 0),
+                    stop=(a == KP - 1 and t == PACK - 1),
+                )
+
         def drag(b, g, s):
             if s == 0:
                 h_bf[b, g] = ring.tile([P, PACK * HALF], BF16, name="h_bf", align_bytes=64, bufs=3)
-            cols = slice(TOK * s, TOK * (s + 1))
-            bank = psum.tile([P, HALF], F32, name="bank")
-            bank = bank[:].rearrange("p (t c) -> p t c", t=PACK)
-            for a in range(KP):
-                for t in range(PACK):
-                    wcols = slice(P * t, P * (t + 1))
-                    nc.tensor.matmul_mx(
-                        bank[:, t, :],
-                        lhsT=w1_w[b, a][:, wcols].bitcast(FP8X4),
-                        lhsT_scale=w1_s[b, a][:, wcols],
-                        rhs=v_w[g][a][:, cols].bitcast(FP8X4),
-                        rhs_scale=v_s[g][4 * a : P, cols],
-                        start=(a == 0 and t == 0),
-                        stop=(a == KP - 1 and t == PACK - 1),
-                    )
+            if (b, g, s) not in banks:
+                product(b, g, s, 0)
+            product(b, g, s, 1)
+            bank = banks[b, g, s]
             lent = (b, g) == (HP - 1, HALVES - 1) and s >= 2
             mag = forces[0][s] if lent else ring.tile([P, HALF], F32, name="mag", bufs=8)
             mag = mag[:].rearrange("p (t c) -> p t c", t=PACK)
             for t in range(PACK):
-                nc.scalar.activation(mag[:, t, :], bank[:, t, :], ACT.Abs, scale=cd_sb[:, b, t : t + 1])
+                nc.scalar.activation(mag[:, t, :], bank[:, t, :], ACT.Abs, scale=cd_sb[b][:, t : t + 1])
             dst = h_bf[b, g][:, PACK * TOK * s : PACK * TOK * (s + 1)]
             nc.vector.tensor_tensor(
                 dst.rearrange("p (c i t) -> p c t i", i=2, t=PACK),
@@ -164,7 +179,11 @@ def tile_list_contact_drag_store_kernel(
 
         def quantise_h(b, g):
             h_w[b, g] = kept([P, HALF], U32, f"h_w{b}{g}")
-            h_s[b, g] = kept([P, HALF], U8, f"h_s{b}{g}")
+            piece = KP * b + g + 3
+            if piece < KP * HP:
+                h_s[b, g] = over_piece([P, HALF], U8, f"h_s{b}{g}", piece)
+            else:
+                h_s[b, g] = kept([P, HALF], U8, f"h_s{b}{g}")
             nc.vector.quantize_mx(h_w[b, g][:].bitcast(FP8X4), h_s[b, g][:], h_bf[b, g][:])
 
         def project(g, n):
@@ -190,15 +209,17 @@ def tile_list_contact_drag_store_kernel(
             )
 
         round_w1(0, 0, 0, P, nc.scalar.copy)
-        round_w1(0, 1, P // 4, P, nc.scalar.copy)
+        round_w1(0, 1, P // 2, P, nc.scalar.copy)
         quantise_w1(0, 0)
-        round_w1(0, 1, 0, P // 4, nc.vector.tensor_copy)
-        gather_words(0, 1, 0, HALF // 2)
+        for s in range(HALF // TOK):
+            product(0, 0, s, 0)
+        round_w1(0, 1, 0, P // 2, nc.vector.tensor_copy)
         quantise_w1(0, 1)
+        gather_words(0, 1, 0, HALF // 2)
         gather_words(0, 1, HALF // 2, HALF)
         gather_words(1, 1)
 
-        round_shared(1, 0)
+        round_w1(1, 0, 0, P, gpsimd_copy)
         for b in range(HP):
             more = b + 1 < HP
             for step in range(8):
@@ -215,8 +236,11 @@ def tile_list_contact_drag_store_kernel(
                     if b + 2 < HP:
                         round_shared(b + 2, 0)
                     quantise_h(b, 0)
+                if step == 5 and not more:
+                    for n in range(2):
+                        negate(0, n, project(0, n))
         quantise_h(HP - 1, 1)
-        for n in range(NT):
+        for n in range(2, NT):
             negate(0, n, project(0, n))
         y_second = [project(1, n) for n in range(NT)]
         for n in range(NT):

@@ -15,7 +15,6 @@ FP8X4 = mybir.dt.float8_e4m3fn_x4
 FP4X4 = mybir.dt.float4_e2m1fn_x4
 ACT = mybir.ActivationFunctionType
 MULT = mybir.AluOpType.mult
-ADD = mybir.AluOpType.add
 
 P = 128
 PACK = 4
@@ -27,7 +26,6 @@ HALF = 512
 HALVES = S // HALF
 LIST_COLS = HALF // 16
 TOK = 128
-SPLIT = 96
 
 
 def tile_list_contact_drag_store_kernel(
@@ -115,23 +113,20 @@ def tile_list_contact_drag_store_kernel(
         h_bf, h_w, h_s = {}, {}, {}
         forces = [[kept([P, HALF], F32, f"force{g}{n}") for n in range(NT)] for g in range(HALVES)]
 
-        def round_w1(b, a, lo, hi, engine_copy):
+        def round_w1(b, a, pair, lo, hi, engine_copy):
             if (b, a) not in w1_bf:
                 if b == 0:
                     w1_bf[b, a] = kept([P, PACK * PASS], BF16, f"w1_first{a}")
                 else:
-                    w1_bf[b, a] = ring.tile([P, PACK * PASS], BF16, name="w1_bf", align_bytes=64, bufs=1)
-            src = w1_raw[b][a][:].rearrange("p j (m t) -> p m t j", t=PACK)
-            dst = w1_bf[b, a][:].rearrange("p (t m j) -> p m t j", t=PACK, j=PACK)
-            engine_copy(dst[:, lo:hi, :, :], src[:, lo:hi, :, :])
-
-        def gpsimd_copy(dst, src):
-            nc.gpsimd.tensor_scalar(dst, src, 1.0, 0.0, MULT, ADD)
+                    w1_bf[b, a] = over_piece([P, PACK * PASS], BF16, f"w1_bf{b}{a}", a)
+            slots = slice(2 * pair, 2 * pair + 2)
+            src = w1_raw[b][a][:].rearrange("p j (m t) -> p m j t", t=PACK)
+            dst = w1_bf[b, a][:].rearrange("p (t m j) -> p m j t", t=PACK, j=PACK)
+            engine_copy(dst[:, lo:hi, :, slots], src[:, lo:hi, :, slots])
 
         def round_shared(b, a):
-            split = P // 2 if b == 1 else SPLIT
-            round_w1(b, a, 0, split, gpsimd_copy)
-            round_w1(b, a, split, P, nc.scalar.copy)
+            round_w1(b, a, 0, 0, P, nc.vector.tensor_copy)
+            round_w1(b, a, 1, 0, P, nc.scalar.copy)
 
         def quantise_w1(b, a):
             w1_w[b, a] = kept([P, PASS], U32, f"w1_w{b}{a}")
@@ -159,13 +154,21 @@ def tile_list_contact_drag_store_kernel(
 
         def drag(b, g, s):
             if s == 0:
-                h_bf[b, g] = ring.tile([P, PACK * HALF], BF16, name="h_bf", align_bytes=64, bufs=3)
+                if (b, g) == (HP - 1, 0):
+                    h_bf[b, g] = over_piece([P, PACK * HALF], BF16, "h_last", 2)
+                else:
+                    h_bf[b, g] = ring.tile([P, PACK * HALF], BF16, name="h_bf", align_bytes=64, bufs=3)
             if (b, g, s) not in banks:
                 product(b, g, s, 0)
             product(b, g, s, 1)
             bank = banks[b, g, s]
             lent = (b, g) == (HP - 1, HALVES - 1) and s >= 2
-            mag = forces[0][s] if lent else ring.tile([P, HALF], F32, name="mag", bufs=8)
+            if lent:
+                mag = forces[0][s]
+            elif b + 1 < HP and g == 0 and s % 2 == 1:
+                mag = over_piece([P, HALF], F32, f"mag{b}{s}", s // 2)
+            else:
+                mag = ring.tile([P, HALF], F32, name="mag", bufs=8)
             mag = mag[:].rearrange("p (t c) -> p t c", t=PACK)
             for t in range(PACK):
                 nc.scalar.activation(mag[:, t, :], bank[:, t, :], ACT.Abs, scale=cd_sb[b][:, t : t + 1])
@@ -179,9 +182,8 @@ def tile_list_contact_drag_store_kernel(
 
         def quantise_h(b, g):
             h_w[b, g] = kept([P, HALF], U32, f"h_w{b}{g}")
-            piece = KP * b + g + 3
-            if piece < KP * HP:
-                h_s[b, g] = over_piece([P, HALF], U8, f"h_s{b}{g}", piece)
+            if (b, g) == (HP - 2, 1):
+                h_s[b, g] = over_piece([P, HALF], U8, f"h_s{b}{g}", 2)
             else:
                 h_s[b, g] = kept([P, HALF], U8, f"h_s{b}{g}")
             nc.vector.quantize_mx(h_w[b, g][:].bitcast(FP8X4), h_s[b, g][:], h_bf[b, g][:])
@@ -208,33 +210,29 @@ def tile_list_contact_drag_store_kernel(
                 pages[n][:].indirect(list_half(place, g)), forces[g][n][:], wgo_sb[:, HALF * g : HALF * (g + 1)], MULT
             )
 
-        round_w1(0, 0, 0, P, nc.scalar.copy)
-        round_w1(0, 1, P // 2, P, nc.scalar.copy)
+        round_w1(0, 0, 0, 0, P, nc.scalar.copy)
+        round_w1(0, 0, 1, 0, P, nc.scalar.copy)
+        round_w1(0, 1, 1, 0, P, nc.scalar.copy)
         quantise_w1(0, 0)
         for s in range(HALF // TOK):
             product(0, 0, s, 0)
-        round_w1(0, 1, 0, P // 2, nc.vector.tensor_copy)
+        round_w1(0, 1, 0, 0, P, nc.vector.tensor_copy)
         quantise_w1(0, 1)
         gather_words(0, 1, 0, HALF // 2)
         gather_words(0, 1, HALF // 2, HALF)
         gather_words(1, 1)
 
-        round_w1(1, 0, 0, P, gpsimd_copy)
         for b in range(HP):
             more = b + 1 < HP
             for step in range(8):
                 drag(b, step // 4, step % 4)
-                if step == 1:
-                    if more:
-                        quantise_w1(b + 1, 0)
-                        round_shared(b + 1, 1)
-                    if b > 0:
-                        quantise_h(b - 1, 1)
-                if step == (5 if more else 4):
-                    if more:
-                        quantise_w1(b + 1, 1)
-                    if b + 2 < HP:
-                        round_shared(b + 2, 0)
+                if step == (0 if more else 5) and b > 0:
+                    quantise_h(b - 1, 1)
+                if more and step in (1, 3):
+                    round_shared(b + 1, step // 2)
+                if more and step in (2, 4):
+                    quantise_w1(b + 1, step // 2 - 1)
+                if step == 4:
                     quantise_h(b, 0)
                 if step == 5 and not more:
                     for n in range(2):

@@ -26,6 +26,7 @@ HALF = 512
 HALVES = S // HALF
 LIST_COLS = HALF // 16
 TOK = 128
+PAGES = 2
 
 
 def tile_list_contact_drag_store_kernel(
@@ -54,12 +55,12 @@ def tile_list_contact_drag_store_kernel(
         w4_w = kept([P, HP, 2 * N], U8, "w4_w")
         w4_s = kept([P, HP, N], U8, "w4_s")
         wgo_sb = kept([P, S], F32, "wgo_sb")
-        pages = [kept([P, T2], F32, f"page{n}") for n in range(NT)]
+        pages = [kept([P, T2], F32, f"page{n}") for n in range(PAGES)]
 
         nc.vector.memset(tab_s[:].bitcast(I32), 0)
-        nc.vector.memset(w4_s[:].bitcast(I32), 0)
         for page in pages:
             nc.vector.memset(page[:].bitcast(I32), 0)
+        nc.vector.memset(w4_s[:].bitcast(I32), 0)
 
         def load_w1(b, a):
             rows = w1[PASS * a : PASS * (a + 1), PASS * b : PASS * (b + 1)]
@@ -111,7 +112,7 @@ def tile_list_contact_drag_store_kernel(
 
         w1_bf, w1_w, w1_s = {}, {}, {}
         h_bf, h_w, h_s = {}, {}, {}
-        forces = [[kept([P, HALF], F32, f"force{g}{n}") for n in range(NT)] for g in range(HALVES)]
+        forces = [kept([P, S], F32, f"force{n}") for n in range(NT)]
 
         def round_w1(b, a, pair, lo, hi, engine_copy):
             if (b, a) not in w1_bf:
@@ -162,14 +163,14 @@ def tile_list_contact_drag_store_kernel(
                 product(b, g, s, 0)
             product(b, g, s, 1)
             bank = banks[b, g, s]
-            lent = (b, g) == (HP - 1, HALVES - 1) and s >= 2
+            lent = (b, g) == (HP - 1, HALVES - 1) and s == 2
             if lent:
-                mag = forces[0][s]
+                mag = forces[1][:, 0:HALF]
             elif b + 1 < HP and g == 0 and s % 2 == 1:
-                mag = over_piece([P, HALF], F32, f"mag{b}{s}", s // 2)
+                mag = over_piece([P, HALF], F32, f"mag{b}{s}", s // 2)[:]
             else:
-                mag = ring.tile([P, HALF], F32, name="mag", bufs=8)
-            mag = mag[:].rearrange("p (t c) -> p t c", t=PACK)
+                mag = ring.tile([P, HALF], F32, name="mag", bufs=8)[:]
+            mag = mag.rearrange("p (t c) -> p t c", t=PACK)
             for t in range(PACK):
                 nc.scalar.activation(mag[:, t, :], bank[:, t, :], ACT.Abs, scale=cd_sb[b][:, t : t + 1])
             dst = h_bf[b, g][:, PACK * TOK * s : PACK * TOK * (s + 1)]
@@ -203,12 +204,15 @@ def tile_list_contact_drag_store_kernel(
             return y_bank
 
         def negate(g, n, y_bank):
-            nc.scalar.activation(forces[g][n][:], y_bank[:], ACT.Copy, scale=-1.0)
+            nc.scalar.activation(forces[n][:, HALF * g : HALF * (g + 1)], y_bank[:], ACT.Copy, scale=-1.0)
 
-        def scatter(g, n):
+        def scatter(n, lo, hi):
+            page = pages[n % PAGES]
             nc.vector.tensor_tensor(
-                pages[n][:].indirect(list_half(place, g)), forces[g][n][:], wgo_sb[:, HALF * g : HALF * (g + 1)], MULT
+                page[:].indirect(place[:, lo // 16 : hi // 16]), forces[n][:, lo:hi], wgo_sb[:, lo:hi], MULT
             )
+            if hi == S:
+                nc.sync.dma_start(out[P * n : P * (n + 1), :], page[:])
 
         round_w1(0, 0, 0, 0, P, nc.scalar.copy)
         round_w1(0, 0, 1, 0, P, nc.scalar.copy)
@@ -235,16 +239,16 @@ def tile_list_contact_drag_store_kernel(
                 if step == 4:
                     quantise_h(b, 0)
                 if step == 5 and not more:
-                    for n in range(2):
-                        negate(0, n, project(0, n))
+                    negate(0, 0, project(0, 0))
+        scatter(0, 0, HALF)
         quantise_h(HP - 1, 1)
-        for n in range(2, NT):
-            negate(0, n, project(0, n))
-        y_second = [project(1, n) for n in range(NT)]
-        for n in range(NT):
-            scatter(0, n)
-        for n in range(NT):
-            negate(1, n, y_second[n])
-        for n in range(NT):
-            scatter(1, n)
-            nc.sync.dma_start(out[P * n : P * (n + 1), :], pages[n][:])
+        negate(0, 1, project(0, 1))
+        scatter(1, 0, HALF // 2)
+        negate(1, 0, project(1, 0))
+        scatter(0, HALF, S)
+        negate(1, 1, project(1, 1))
+        scatter(1, HALF // 2, S)
+        for n in range(PAGES, NT):
+            for g in range(HALVES):
+                negate(g, n, project(g, n))
+            scatter(n, 0, S)

@@ -15,6 +15,7 @@ FP8X4 = mybir.dt.float8_e4m3fn_x4
 FP4X4 = mybir.dt.float4_e2m1fn_x4
 ACT = mybir.ActivationFunctionType
 MULT = mybir.AluOpType.mult
+ADD = mybir.AluOpType.add
 
 P = 128
 PACK = 4
@@ -26,7 +27,8 @@ HALF = 512
 HALVES = S // HALF
 LIST_COLS = HALF // 16
 TOK = 128
-PAGES = 2
+WIDE = 256
+ROTA = 4
 
 
 def tile_list_contact_drag_store_kernel(
@@ -37,7 +39,7 @@ def tile_list_contact_drag_store_kernel(
         keep = ctx.enter_context(tc.tile_pool(name="keep", bufs=1))
         shared = ctx.enter_context(tc.tile_pool(name="shared", bufs=1))
         ring = ctx.enter_context(tc.tile_pool(name="ring", bufs=4))
-        psum = ctx.enter_context(tc.psum_pool(name="psum", bufs=8))
+        psum = ctx.enter_context(tc.psum_pool(name="psum", bufs=1))
 
         def kept(shape, dtype, name):
             return keep.tile(shape, dtype, name=name, align_bytes=64)
@@ -47,15 +49,21 @@ def tile_list_contact_drag_store_kernel(
         tab_w = [kept([P, T], I32, f"tab_w{a}") for a in range(KP)]
         tab_s = kept([P, T], U8, "tab_s")
 
-        def over_piece(shape, dtype, name, piece):
-            return shared.tile(shape, dtype, name=name, align_bytes=64, offset=4 * PACK * PASS * piece)
+        def over_piece(shape, dtype, name, piece, skip=0):
+            return shared.tile(shape, dtype, name=name, align_bytes=64, offset=4 * PACK * PASS * piece + skip)
 
         w1_raw = [[over_piece([P, PACK, PASS], F32, f"w1_raw{b}{a}", KP * b + a) for a in range(KP)] for b in range(HP)]
-        cd_sb = [kept([P, PACK], F32, f"cd_sb{b}") for b in range(HP)]
+        cd_all = kept([P, HP, PACK], F32, "cd_all")
+        cd_sb = [cd_all[:, b, :] for b in range(HP)]
+        cd_root = kept([P, HP * PACK], F32, "cd_root")
+        guess = kept([P, HP * PACK], F32, "guess")
+        inverse = kept([P, HP * PACK], F32, "inverse")
+        quotient = kept([P, HP * PACK], F32, "quotient")
+        psum_banks = [psum.tile([P, HALF], F32, name=f"bank{i}") for i in range(2 * ROTA)]
         w4_w = kept([P, HP, 2 * N], U8, "w4_w")
         w4_s = kept([P, HP, N], U8, "w4_s")
         wgo_sb = kept([P, S], F32, "wgo_sb")
-        pages = [kept([P, T2], F32, f"page{n}") for n in range(PAGES)]
+        pages = [kept([P, T2], F32, f"page{n}") for n in range(NT)]
 
         nc.vector.memset(tab_s[:].bitcast(I32), 0)
         for page in pages:
@@ -71,25 +79,24 @@ def tile_list_contact_drag_store_kernel(
 
         load_tab(0)
         nc.sync.dma_start(pick[:], offs)
-        for q in range(4):
-            nc.sync.dma_start(
-                tab_s[32 * q : 32 * q + 4 * KP, :].bitcast(I32), tab_scales[:, 4 * q : 4 * q + 4, :].bitcast(I32)
-            )
-        load_w1(0, 0)
+        nc.sync.dma_start(place[:], offs2)
+        for i in range(4 * KP):
+            if i == 3:
+                load_w1(0, 0)
+            r, a = divmod(i, KP)
+            nc.sync.dma_start(tab_s[4 * a + r : P : 32, :].bitcast(I32), tab_scales[a, r:16:4, :].bitcast(I32))
         load_w1(0, 1)
         load_tab(1)
-        for b in range(HP):
-            nc.sync.dma_start(cd_sb[b][:], cd[PASS * b : PASS * (b + 1)].rearrange("(p t) -> p t", t=PACK))
-            if b + 1 < HP:
-                for a in range(KP):
-                    load_w1(b + 1, a)
+        nc.sync.dma_start(cd_all[:], cd.rearrange("(b p t) -> p b t", p=P, t=PACK))
+        for b in range(1, HP):
+            for a in range(KP):
+                load_w1(b, a)
         for q in range(4):
             nc.sync.dma_start(
                 w4_s[32 * q : 32 * q + 4, :, :].bitcast(I32),
                 w4_scales[:, 4 * q : 4 * q + 4, :].rearrange("a r n -> r a n").bitcast(I32),
             )
         nc.sync.dma_start(w4_w[:].bitcast(I32), w4_words.rearrange("a p c -> p a c").bitcast(I32))
-        nc.sync.dma_start(place[:], offs2)
         nc.sync.dma_start(wgo_sb[:], wgo)
 
         v_w = [[kept([P, HALF], U32, f"v_w{g}{a}") for a in range(KP)] for g in range(HALVES)]
@@ -105,6 +112,8 @@ def tile_list_contact_drag_store_kernel(
         def gather_scales(g):
             nc.vector.tensor_copy(v_s[g][:], tab_s[:].indirect(list_half(pick, g)))
 
+        cd_flat = cd_all[:].rearrange("p b t -> p (b t)")
+        nc.scalar.activation(guess[:], cd_flat, ACT.Sqrt)
         for g in range(HALVES):
             gather_words(g, 0)
         for g in range(HALVES):
@@ -134,12 +143,12 @@ def tile_list_contact_drag_store_kernel(
             w1_s[b, a] = kept([P, PASS], U8, f"w1_s{b}{a}")
             nc.vector.quantize_mx(w1_w[b, a][:].bitcast(FP8X4), w1_s[b, a][:], w1_bf[b, a][:])
 
-        banks = {}
+        banks, mags = {}, {}
+        piece_of = {(0, 0, 0): 0, (0, 0, 3): 0, (0, 0, 1): 1, (1, 0, 0): 1, (2, 0, 3): 1}
 
         def product(b, g, s, a):
             if a == 0:
-                tile = psum.tile([P, HALF], F32, name="bank")
-                banks[b, g, s] = tile[:].rearrange("p (t c) -> p t c", t=PACK)
+                banks[b, g, s] = psum_banks[4 * (b % 2) + s][:].rearrange("p (t c) -> p t c", t=PACK)
             cols = slice(TOK * s, TOK * (s + 1))
             for t in range(PACK):
                 wcols = slice(P * t, P * (t + 1))
@@ -153,66 +162,102 @@ def tile_list_contact_drag_store_kernel(
                     stop=(a == KP - 1 and t == PACK - 1),
                 )
 
-        def drag(b, g, s):
-            if s == 0:
-                if (b, g) == (HP - 1, 0):
-                    h_bf[b, g] = over_piece([P, PACK * HALF], BF16, "h_last", 2)
-                else:
-                    h_bf[b, g] = ring.tile([P, PACK * HALF], BF16, name="h_bf", align_bytes=64, bufs=3)
+        def magnitude(b, g, s):
             if (b, g, s) not in banks:
                 product(b, g, s, 0)
             product(b, g, s, 1)
-            bank = banks[b, g, s]
-            lent = (b, g) == (HP - 1, HALVES - 1) and s == 2
-            if lent:
-                mag = forces[1][:, 0:HALF]
-            elif b + 1 < HP and g == 0 and s % 2 == 1:
-                mag = over_piece([P, HALF], F32, f"mag{b}{s}", s // 2)[:]
+            if (b, g, s) in piece_of:
+                mag = over_piece([P, HALF], F32, f"mag{b}{g}{s}", piece_of[b, g, s], 3072)[:]
             else:
-                mag = ring.tile([P, HALF], F32, name="mag", bufs=8)[:]
-            mag = mag.rearrange("p (t c) -> p t c", t=PACK)
+                mag = ring.tile([P, HALF], F32, name="mag", bufs=4)[:]
+            mags[b, g, s] = mag.rearrange("p (t c) -> p t c", t=PACK)
             for t in range(PACK):
-                nc.scalar.activation(mag[:, t, :], bank[:, t, :], ACT.Abs, scale=cd_sb[b][:, t : t + 1])
-            dst = h_bf[b, g][:, PACK * TOK * s : PACK * TOK * (s + 1)]
+                nc.scalar.activation(
+                    mags[b, g, s][:, t, :], banks[b, g, s][:, t, :], ACT.Abs, scale=cd_sb[b][:, t : t + 1]
+                )
+
+        def h_tile(b, g):
+            if (b, g) not in h_bf:
+                h_bf[b, g] = kept([P, PACK * HALF], BF16, f"h_bf{b}{g}")
+            return h_bf[b, g]
+
+        def multiply(b, g, s):
+            dst = h_tile(b, g)[:, PACK * TOK * s : PACK * TOK * (s + 1)]
             nc.vector.tensor_tensor(
                 dst.rearrange("p (c i t) -> p c t i", i=2, t=PACK),
-                bank.rearrange("p t (c i) -> p c t i", i=2),
-                mag.rearrange("p t (c i) -> p c t i", i=2),
+                banks[b, g, s].rearrange("p t (c i) -> p c t i", i=2),
+                mags[b, g, s].rearrange("p t (c i) -> p c t i", i=2),
                 MULT,
             )
 
-        def quantise_h(b, g):
-            h_w[b, g] = kept([P, HALF], U32, f"h_w{b}{g}")
-            if (b, g) == (HP - 2, 1):
-                h_s[b, g] = over_piece([P, HALF], U8, f"h_s{b}{g}", 2)
-            else:
-                h_s[b, g] = kept([P, HALF], U8, f"h_s{b}{g}")
-            nc.vector.quantize_mx(h_w[b, g][:].bitcast(FP8X4), h_s[b, g][:], h_bf[b, g][:])
+        def drag(b, g, s):
+            magnitude(b, g, s)
+            multiply(b, g, s)
 
-        def project(g, n):
-            y_bank = psum.tile([P, HALF], F32, name="bank")
-            for b in range(HP):
+        def drag_by_sign(b, s):
+            cols = slice(WIDE * s, WIDE * (s + 1))
+            squares = over_piece([P, 2, WIDE, 2], BF16, f"squares{b}{s}", 2 + b, 4096 * s)
+            signs = over_piece([P, 2, WIDE, 2], BF16, f"signs{b}{s}", 2 + b, 4096 * s + 2048)
+            for u in range(2):
+                bank = psum_banks[(0, 4, 5)[(2 * (HP * s + b) + u) % 3]][:].rearrange("p (e c) -> p e c", e=2)
+                for e in range(2):
+                    wcols = slice(P * (2 * u + e), P * (2 * u + e + 1))
+                    for a in range(KP):
+                        nc.tensor.matmul_mx(
+                            bank[:, e, :],
+                            lhsT=w1_w[b, a][:, wcols].bitcast(FP8X4),
+                            lhsT_scale=w1_s[b, a][:, wcols],
+                            rhs=(v_late[:] if (a, s) == (1, 1) else v_w[1][a][:, cols]).bitcast(FP8X4),
+                            rhs_scale=v_s[1][4 * a : P, cols],
+                            start=(a == 0),
+                            stop=(a == KP - 1),
+                        )
+                for e in range(2):
+                    t = 2 * u + e
+                    nc.scalar.activation(
+                        squares[:, u, :, e], bank[:, e, :], ACT.Square, scale=cd_root[:, PACK * b + t : PACK * b + t + 1]
+                    )
+                nc.scalar.activation(
+                    signs[:, u, :, :].rearrange("p (c i) e -> p c e i", i=2),
+                    bank.rearrange("p e (c i) -> p c e i", i=2),
+                    ACT.Sign,
+                )
+            dst = h_tile(b, 1)[:, PACK * WIDE * s : PACK * WIDE * (s + 1)]
+            nc.vector.tensor_tensor(
+                dst.rearrange("p (c u e) -> p c u e", u=2, e=2),
+                squares[:].rearrange("p u c e -> p c u e"),
+                signs[:].rearrange("p u c e -> p c u e"),
+                MULT,
+            )
+
+        def quantise_h(b, g, lo=0, hi=HALF):
+            if (b, g) not in h_w:
+                h_w[b, g] = kept([P, HALF], U32, f"h_w{b}{g}")
+                h_s[b, g] = kept([P, HALF], U8, f"h_s{b}{g}")
+            nc.vector.quantize_mx(
+                h_w[b, g][:, lo:hi].bitcast(FP8X4), h_s[b, g][:, lo:hi], h_bf[b, g][:, PACK * lo : PACK * hi]
+            )
+
+        def project(g, n, y_bank, order, lo=0, hi=HALF):
+            width = HALF if hi - lo == HALF else TOK
+            passes = [(b, c) for b in order for c in range(lo, hi, width)]
+            for b, c in passes:
                 nc.tensor.matmul_mx(
-                    y_bank[:],
+                    y_bank[:, c - lo : c - lo + width],
                     lhsT=w4_w[:, b, 2 * P * n : 2 * P * (n + 1)].bitcast(FP4X4),
                     lhsT_scale=w4_s[:, b, P * n : P * (n + 1)],
-                    rhs=h_w[b, g][:].bitcast(FP8X4),
-                    rhs_scale=h_s[b, g][:],
-                    start=(b == 0),
-                    stop=(b == HP - 1),
+                    rhs=h_w[b, g][:, c : c + width].bitcast(FP8X4),
+                    rhs_scale=h_s[b, g][:, c : c + width],
+                    start=((b, c) == passes[0]),
+                    stop=((b, c) == passes[-1]),
                 )
-            return y_bank
 
-        def negate(g, n, y_bank):
-            nc.scalar.activation(forces[n][:, HALF * g : HALF * (g + 1)], y_bank[:], ACT.Copy, scale=-1.0)
-
-        def scatter(n, lo, hi):
-            page = pages[n % PAGES]
-            nc.vector.tensor_tensor(
-                page[:].indirect(place[:, lo // 16 : hi // 16]), forces[n][:, lo:hi], wgo_sb[:, lo:hi], MULT
-            )
+        def scatter(n, lo, hi, y_bank):
+            values = forces[n][:, lo:hi]
+            nc.scalar.activation(values, y_bank[:, 0 : hi - lo], ACT.Copy, scale=-1.0)
+            nc.vector.tensor_tensor(pages[n][:].indirect(place[:, lo // 16 : hi // 16]), values, wgo_sb[:, lo:hi], MULT)
             if hi == S:
-                nc.sync.dma_start(out[P * n : P * (n + 1), :], page[:])
+                nc.sync.dma_start(out[P * n : P * (n + 1), :], pages[n][:])
 
         round_w1(0, 0, 0, 0, P, nc.scalar.copy)
         round_w1(0, 0, 1, 0, P, nc.scalar.copy)
@@ -224,31 +269,70 @@ def tile_list_contact_drag_store_kernel(
         quantise_w1(0, 1)
         gather_words(0, 1, 0, HALF // 2)
         gather_words(0, 1, HALF // 2, HALF)
-        gather_words(1, 1)
+        nc.vector.reciprocal(inverse[:], guess[:])
+        gather_words(1, 1, 0, WIDE)
+        nc.vector.scalar_tensor_tensor(quotient[:], cd_flat, 0.5, inverse[:], MULT, MULT)
 
-        for b in range(HP):
-            more = b + 1 < HP
-            for step in range(8):
-                drag(b, step // 4, step % 4)
-                if step == (0 if more else 5) and b > 0:
-                    quantise_h(b - 1, 1)
-                if more and step in (1, 3):
-                    round_shared(b + 1, step // 2)
-                if more and step in (2, 4):
-                    quantise_w1(b + 1, step // 2 - 1)
-                if step == 4:
-                    quantise_h(b, 0)
-                if step == 5 and not more:
-                    negate(0, 0, project(0, 0))
-        scatter(0, 0, HALF)
-        quantise_h(HP - 1, 1)
-        negate(0, 1, project(0, 1))
-        scatter(1, 0, HALF // 2)
-        negate(1, 0, project(1, 0))
-        scatter(0, HALF, S)
-        negate(1, 1, project(1, 1))
-        scatter(1, HALF // 2, S)
-        for n in range(PAGES, NT):
-            for g in range(HALVES):
-                negate(g, n, project(g, n))
-            scatter(n, 0, S)
+        drag(0, 0, 0)
+        nc.vector.scalar_tensor_tensor(cd_root[:], guess[:], 0.5, quotient[:], MULT, ADD)
+        magnitude(0, 0, 1)
+        round_shared(1, 0)
+        multiply(0, 0, 1)
+        quantise_w1(1, 0)
+        drag(0, 0, 2)
+        round_w1(1, 1, 0, 0, P, nc.vector.tensor_copy)
+        round_w1(1, 1, 1, 0, P, nc.vector.tensor_copy)
+        magnitude(0, 0, 3)
+        quantise_w1(1, 1)
+        multiply(0, 0, 3)
+        magnitude(1, 0, 0)
+        quantise_h(0, 0)
+        multiply(1, 0, 0)
+        round_shared(2, 0)
+        drag(1, 0, 1)
+        quantise_w1(2, 0)
+        round_shared(2, 1)
+        drag(1, 0, 2)
+        quantise_w1(2, 1)
+        drag(1, 0, 3)
+        drag(2, 0, 0)
+        quantise_h(1, 0)
+        drag(2, 0, 1)
+        drag(2, 0, 2)
+        quantise_h(2, 0, 0, WIDE)
+        drag(2, 0, 3)
+        v_late = over_piece([P, WIDE], U32, "v_late", 1, 4096)
+        nc.vector.tensor_copy(v_late[:], tab_w[1][:].bitcast(U32).indirect(pick[:, (HALF + WIDE) // 16 : S // 16]))
+        quantise_h(2, 0, WIDE, HALF)
+        last = NT - 1
+        mid = HALF + WIDE
+
+        def deliver(n, lo, hi, bank, order):
+            g = lo // HALF
+            project(g, n, psum_banks[bank], order, lo - HALF * g, hi - HALF * g)
+            scatter(n, lo, hi, psum_banks[bank])
+
+        deliver(0, 0, WIDE, 6, (1, 0, 2))
+        deliver(0, WIDE, HALF, 4, (1, 0, 2))
+        deliver(1, 0, HALF, 5, (1, 0, 2))
+        drag_by_sign(0, 0)
+        deliver(2, 0, HALF, 0, (0, 1, 2))
+        quantise_h(0, 1, 0, WIDE)
+        drag_by_sign(1, 0)
+        deliver(last, 0, WIDE, 5, (0, 1, 2))
+        quantise_h(1, 1, 0, WIDE)
+        drag_by_sign(2, 0)
+        quantise_h(2, 1, 0, WIDE)
+        deliver(last, WIDE, HALF, 4, (0, 1, 2))
+        drag_by_sign(0, 1)
+        quantise_h(0, 1, WIDE, HALF)
+        drag_by_sign(1, 1)
+        deliver(0, HALF, mid, 5, (0, 1, 2))
+        quantise_h(1, 1, WIDE, HALF)
+        deliver(1, HALF, mid, 0, (0, 1, 2))
+        drag_by_sign(2, 1)
+        quantise_h(2, 1, WIDE, HALF)
+        deliver(2, HALF, mid, 5, (0, 1, 2))
+        for n in range(last):
+            deliver(n, mid, S, 1 + n, (1, 0, 2))
+        deliver(last, HALF, S, 6, (1, 0, 2))

@@ -25,7 +25,6 @@ HP = H // PASS
 NT = N // P
 HALF = 512
 HALVES = S // HALF
-LIST_COLS = HALF // 16
 TOK = 128
 WIDE = 256
 ROTA = 4
@@ -77,12 +76,12 @@ def tile_list_contact_drag_store_kernel(
         def load_tab(a):
             nc.sync.dma_start(tab_w[a][:], tab_words[a].rearrange("p t i -> p (t i)").bitcast(I32))
 
-        load_tab(0)
+        load_w1(0, 0)
         nc.sync.dma_start(pick[:], offs)
         nc.sync.dma_start(place[:], offs2)
         for i in range(4 * KP):
             if i == 3:
-                load_w1(0, 0)
+                load_tab(0)
             r, a = divmod(i, KP)
             nc.sync.dma_start(tab_s[4 * a + r : P : 32, :].bitcast(I32), tab_scales[a, r:16:4, :].bitcast(I32))
         load_w1(0, 1)
@@ -102,22 +101,16 @@ def tile_list_contact_drag_store_kernel(
         v_w = [[kept([P, HALF], U32, f"v_w{g}{a}") for a in range(KP)] for g in range(HALVES)]
         v_s = [kept([P, HALF], U8, f"v_s{g}") for g in range(HALVES)]
 
-        def list_half(lst, g):
-            return lst[:, LIST_COLS * g : LIST_COLS * (g + 1)]
-
         def gather_words(g, a, lo=0, hi=HALF):
             entries = pick[:, (HALF * g + lo) // 16 : (HALF * g + hi) // 16]
             nc.vector.tensor_copy(v_w[g][a][:, lo:hi], tab_w[a][:].bitcast(U32).indirect(entries))
 
-        def gather_scales(g):
-            nc.vector.tensor_copy(v_s[g][:], tab_s[:].indirect(list_half(pick, g)))
+        def gather_scales(g, lo=0, hi=HALF):
+            entries = pick[:, (HALF * g + lo) // 16 : (HALF * g + hi) // 16]
+            nc.vector.tensor_copy(v_s[g][:, lo:hi], tab_s[:].indirect(entries))
 
         cd_flat = cd_all[:].rearrange("p b t -> p (b t)")
         nc.scalar.activation(guess[:], cd_flat, ACT.Sqrt)
-        for g in range(HALVES):
-            gather_words(g, 0)
-        for g in range(HALVES):
-            gather_scales(g)
 
         w1_bf, w1_w, w1_s = {}, {}, {}
         h_bf, h_w, h_s = {}, {}, {}
@@ -184,9 +177,9 @@ def tile_list_contact_drag_store_kernel(
         def multiply(b, g, s):
             dst = h_tile(b, g)[:, PACK * TOK * s : PACK * TOK * (s + 1)]
             nc.vector.tensor_tensor(
-                dst.rearrange("p (c i t) -> p c t i", i=2, t=PACK),
-                banks[b, g, s].rearrange("p t (c i) -> p c t i", i=2),
-                mags[b, g, s].rearrange("p t (c i) -> p c t i", i=2),
+                dst.rearrange("p (c i t) -> p c t i", i=4, t=PACK),
+                banks[b, g, s].rearrange("p t (c i) -> p c t i", i=4),
+                mags[b, g, s].rearrange("p t (c i) -> p c t i", i=4),
                 MULT,
             )
 
@@ -253,7 +246,10 @@ def tile_list_contact_drag_store_kernel(
                 )
 
         def scatter(n, lo, hi, y_bank):
-            values = forces[n][:, lo:hi]
+            if (n, lo) == (NT - 2, HALF):
+                values = over_piece([P, WIDE], F32, "held", 1 + HP, 4096)[:]
+            else:
+                values = forces[n][:, lo:hi]
             nc.scalar.activation(values, y_bank[:, 0 : hi - lo], ACT.Copy, scale=-1.0)
             nc.vector.tensor_tensor(pages[n][:].indirect(place[:, lo // 16 : hi // 16]), values, wgo_sb[:, lo:hi], MULT)
             if hi == S:
@@ -261,11 +257,15 @@ def tile_list_contact_drag_store_kernel(
 
         round_w1(0, 0, 0, 0, P, nc.scalar.copy)
         round_w1(0, 0, 1, 0, P, nc.scalar.copy)
+        round_w1(0, 1, 0, 0, P, nc.scalar.copy)
         round_w1(0, 1, 1, 0, P, nc.scalar.copy)
+        gather_words(0, 0)
+        gather_scales(0)
         quantise_w1(0, 0)
         for s in range(HALF // TOK):
             product(0, 0, s, 0)
-        round_w1(0, 1, 0, 0, P, nc.vector.tensor_copy)
+        gather_words(1, 0)
+        gather_scales(1)
         quantise_w1(0, 1)
         gather_words(0, 1, 0, HALF // 2)
         gather_words(0, 1, HALF // 2, HALF)
@@ -332,7 +332,7 @@ def tile_list_contact_drag_store_kernel(
         deliver(1, HALF, mid, 0, (0, 1, 2))
         drag_by_sign(2, 1)
         quantise_h(2, 1, WIDE, HALF)
-        deliver(2, HALF, mid, 5, (0, 1, 2))
+        deliver(2, HALF, mid, 4, (0, 1, 2))
         for n in range(last):
             deliver(n, mid, S, 1 + n, (1, 0, 2))
         deliver(last, HALF, S, 6, (1, 0, 2))

@@ -113,6 +113,7 @@ def tile_list_contact_drag_store_kernel(
         nc.scalar.activation(guess[:], cd_flat, ACT.Sqrt)
 
         w1_bf, w1_w, w1_s = {}, {}, {}
+        staging = {(1, 0): (0, 0), (1, 1): (1, 0), (2, 0): (0, 4096), (2, 1): (1, 4096)}
         h_bf, h_w, h_s = {}, {}, {}
         forces = [kept([P, S], F32, f"force{n}") for n in range(NT)]
 
@@ -121,7 +122,7 @@ def tile_list_contact_drag_store_kernel(
                 if b == 0:
                     w1_bf[b, a] = kept([P, PACK * PASS], BF16, f"w1_first{a}")
                 else:
-                    w1_bf[b, a] = over_piece([P, PACK * PASS], BF16, f"w1_bf{b}{a}", a)
+                    w1_bf[b, a] = over_piece([P, PACK * PASS], BF16, f"w1_bf{b}{a}", *staging[b, a])
             slots = slice(2 * pair, 2 * pair + 2)
             src = w1_raw[b][a][:].rearrange("p j (m t) -> p m j t", t=PACK)
             dst = w1_bf[b, a][:].rearrange("p (t m j) -> p m j t", t=PACK, j=PACK)
@@ -137,11 +138,13 @@ def tile_list_contact_drag_store_kernel(
             nc.vector.quantize_mx(w1_w[b, a][:].bitcast(FP8X4), w1_s[b, a][:], w1_bf[b, a][:])
 
         banks, mags = {}, {}
-        piece_of = {(0, 0, 0): 0, (0, 0, 3): 0, (0, 0, 1): 1, (1, 0, 0): 1, (2, 0, 3): 1}
+        held_by = {(0, 0, 1): staging[1, 0], (0, 0, 3): staging[1, 1], (0, 1, 0): staging[2, 0], (1, 0, 0): staging[2, 1], (2, 0, 1): (2, 0)}
+        bank_of = {(0, 0, 0): 0, (0, 0, 1): 1, (0, 0, 2): 2, (0, 0, 3): 3, (0, 1, 0): 4, (0, 1, 1): 5}
+        bank_of.update({(1, 0, 0): 6, (1, 0, 1): 7, (1, 0, 2): 0, (1, 0, 3): 1, (2, 0, 0): 2, (2, 0, 1): 3})
 
         def product(b, g, s, a):
             if a == 0:
-                banks[b, g, s] = psum_banks[4 * (b % 2) + s][:].rearrange("p (t c) -> p t c", t=PACK)
+                banks[b, g, s] = psum_banks[bank_of[b, g, s]][:].rearrange("p (t c) -> p t c", t=PACK)
             cols = slice(TOK * s, TOK * (s + 1))
             for t in range(PACK):
                 wcols = slice(P * t, P * (t + 1))
@@ -159,8 +162,8 @@ def tile_list_contact_drag_store_kernel(
             if (b, g, s) not in banks:
                 product(b, g, s, 0)
             product(b, g, s, 1)
-            if (b, g, s) in piece_of:
-                mag = over_piece([P, HALF], F32, f"mag{b}{g}{s}", piece_of[b, g, s], 3072)[:]
+            if (b, g, s) in held_by:
+                mag = over_piece([P, HALF], F32, f"mag{b}{g}{s}", *held_by[b, g, s])[:]
             else:
                 mag = ring.tile([P, HALF], F32, name="mag", bufs=4)[:]
             mags[b, g, s] = mag.rearrange("p (t c) -> p t c", t=PACK)
@@ -187,35 +190,49 @@ def tile_list_contact_drag_store_kernel(
             magnitude(b, g, s)
             multiply(b, g, s)
 
-        def drag_by_sign(b, s):
+        halves = {}
+
+        def sign_bank(b, q, u, bank_number):
+            g, s = divmod(q, 2)
             cols = slice(WIDE * s, WIDE * (s + 1))
-            squares = over_piece([P, 2, WIDE, 2], BF16, f"squares{b}{s}", 2 + b, 4096 * s)
-            signs = over_piece([P, 2, WIDE, 2], BF16, f"signs{b}{s}", 2 + b, 4096 * s + 2048)
-            for u in range(2):
-                bank = psum_banks[(0, 4, 5)[(2 * (HP * s + b) + u) % 3]][:].rearrange("p (e c) -> p e c", e=2)
-                for e in range(2):
-                    wcols = slice(P * (2 * u + e), P * (2 * u + e + 1))
-                    for a in range(KP):
-                        nc.tensor.matmul_mx(
-                            bank[:, e, :],
-                            lhsT=w1_w[b, a][:, wcols].bitcast(FP8X4),
-                            lhsT_scale=w1_s[b, a][:, wcols],
-                            rhs=(v_late[:] if (a, s) == (1, 1) else v_w[1][a][:, cols]).bitcast(FP8X4),
-                            rhs_scale=v_s[1][4 * a : P, cols],
-                            start=(a == 0),
-                            stop=(a == KP - 1),
-                        )
-                for e in range(2):
-                    t = 2 * u + e
-                    nc.scalar.activation(
-                        squares[:, u, :, e], bank[:, e, :], ACT.Square, scale=cd_root[:, PACK * b + t : PACK * b + t + 1]
-                    )
-                nc.scalar.activation(
-                    signs[:, u, :, :].rearrange("p (c i) e -> p c e i", i=2),
-                    bank.rearrange("p e (c i) -> p c e i", i=2),
-                    ACT.Sign,
+            if u == 0:
+                halves[b, q] = (
+                    ring.tile([P, 2, WIDE, 2], BF16, name="squares", bufs=3),
+                    ring.tile([P, 2, WIDE, 2], BF16, name="signs", bufs=3),
                 )
-            dst = h_tile(b, 1)[:, PACK * WIDE * s : PACK * WIDE * (s + 1)]
+            squares, signs = halves[b, q]
+            bank = psum_banks[bank_number][:].rearrange("p (e c) -> p e c", e=2)
+            for e in range(2):
+                wcols = slice(P * (2 * u + e), P * (2 * u + e + 1))
+                for a in range(KP):
+                    nc.tensor.matmul_mx(
+                        bank[:, e, :],
+                        lhsT=w1_w[b, a][:, wcols].bitcast(FP8X4),
+                        lhsT_scale=w1_s[b, a][:, wcols],
+                        rhs=(v_late[:] if (a, q) == (1, 3) else v_w[g][a][:, cols]).bitcast(FP8X4),
+                        rhs_scale=v_s[g][4 * a : P, cols],
+                        start=(a == 0),
+                        stop=(a == KP - 1),
+                    )
+            for e in range(2):
+                t = 2 * u + e
+                nc.scalar.activation(
+                    squares[:, u, :, e], bank[:, e, :], ACT.Square, scale=cd_root[:, PACK * b + t : PACK * b + t + 1]
+                )
+            nc.scalar.activation(
+                signs[:, u, :, :].rearrange("p (c i) e -> p c e i", i=2),
+                bank.rearrange("p e (c i) -> p c e i", i=2),
+                ACT.Sign,
+            )
+
+        def sign_unit(b, q, first_bank):
+            sign_bank(b, q, 0, first_bank)
+            sign_bank(b, q, 1, first_bank + 1)
+
+        def sign_product(b, q):
+            g, s = divmod(q, 2)
+            squares, signs = halves[b, q]
+            dst = h_tile(b, g)[:, PACK * WIDE * s : PACK * WIDE * (s + 1)]
             nc.vector.tensor_tensor(
                 dst.rearrange("p (c u e) -> p c u e", u=2, e=2),
                 squares[:].rearrange("p u c e -> p c u e"),
@@ -225,7 +242,10 @@ def tile_list_contact_drag_store_kernel(
 
         def quantise_h(b, g, lo=0, hi=HALF):
             if (b, g) not in h_w:
-                h_w[b, g] = kept([P, HALF], U32, f"h_w{b}{g}")
+                if (b, g) == (0, 1):
+                    h_w[b, g] = over_piece([P, HALF], U32, "h_w01", 2, 1024)
+                else:
+                    h_w[b, g] = kept([P, HALF], U32, f"h_w{b}{g}")
                 h_s[b, g] = kept([P, HALF], U8, f"h_s{b}{g}")
             nc.vector.quantize_mx(
                 h_w[b, g][:, lo:hi].bitcast(FP8X4), h_s[b, g][:, lo:hi], h_bf[b, g][:, PACK * lo : PACK * hi]
@@ -245,15 +265,25 @@ def tile_list_contact_drag_store_kernel(
                     stop=((b, c) == passes[-1]),
                 )
 
-        def scatter(n, lo, hi, y_bank):
-            if (n, lo) == (NT - 2, HALF):
-                values = over_piece([P, WIDE], F32, "held", 1 + HP, 4096)[:]
-            else:
-                values = forces[n][:, lo:hi]
-            nc.scalar.activation(values, y_bank[:, 0 : hi - lo], ACT.Copy, scale=-1.0)
-            nc.vector.tensor_tensor(pages[n][:].indirect(place[:, lo // 16 : hi // 16]), values, wgo_sb[:, lo:hi], MULT)
+        def negate(n, lo, hi):
+            g = lo // HALF
+            y_bank = psum_banks[ROTA + n]
+            project(g, n, y_bank, range(HP), lo - HALF * g, hi - HALF * g)
+            nc.scalar.activation(forces[n][:, lo:hi], y_bank[:, 0 : hi - lo], ACT.Copy, scale=-1.0)
+
+        def scatter(n, lo, hi):
+            places = place[:, lo // 16 : hi // 16]
+            nc.vector.tensor_tensor(pages[n][:].indirect(places), forces[n][:, lo:hi], wgo_sb[:, lo:hi], MULT)
             if hi == S:
                 nc.sync.dma_start(out[P * n : P * (n + 1), :], pages[n][:])
+
+        def deliver(n, q, count=1):
+            negate(n, WIDE * q, WIDE * (q + count))
+            scatter(n, WIDE * q, WIDE * (q + count))
+
+        def quantise_quarter(b, q):
+            g, s = divmod(q, 2)
+            quantise_h(b, g, WIDE * s, WIDE * (s + 1))
 
         round_w1(0, 0, 0, 0, P, nc.scalar.copy)
         round_w1(0, 0, 1, 0, P, nc.scalar.copy)
@@ -275,64 +305,58 @@ def tile_list_contact_drag_store_kernel(
 
         drag(0, 0, 0)
         nc.vector.scalar_tensor_tensor(cd_root[:], guess[:], 0.5, quotient[:], MULT, ADD)
-        magnitude(0, 0, 1)
+        drag(0, 0, 1)
+        magnitude(0, 0, 2)
         round_shared(1, 0)
-        multiply(0, 0, 1)
-        quantise_w1(1, 0)
-        drag(0, 0, 2)
-        round_w1(1, 1, 0, 0, P, nc.vector.tensor_copy)
-        round_w1(1, 1, 1, 0, P, nc.vector.tensor_copy)
+        multiply(0, 0, 2)
         magnitude(0, 0, 3)
-        quantise_w1(1, 1)
+        quantise_w1(1, 0)
         multiply(0, 0, 3)
-        magnitude(1, 0, 0)
+        magnitude(0, 1, 0)
+        round_shared(1, 1)
         quantise_h(0, 0)
-        multiply(1, 0, 0)
+        magnitude(0, 1, 1)
+        quantise_w1(1, 1)
+        multiply(0, 1, 0)
+        magnitude(1, 0, 0)
         round_shared(2, 0)
-        drag(1, 0, 1)
+        multiply(0, 1, 1)
+        multiply(1, 0, 0)
+        magnitude(1, 0, 1)
         quantise_w1(2, 0)
         round_shared(2, 1)
-        drag(1, 0, 2)
+        multiply(1, 0, 1)
+        magnitude(1, 0, 2)
         quantise_w1(2, 1)
+        multiply(1, 0, 2)
         drag(1, 0, 3)
         drag(2, 0, 0)
         quantise_h(1, 0)
         drag(2, 0, 1)
-        drag(2, 0, 2)
-        quantise_h(2, 0, 0, WIDE)
-        drag(2, 0, 3)
-        v_late = over_piece([P, WIDE], U32, "v_late", 1, 4096)
+        quantise_quarter(2, 0)
+        v_late = over_piece([P, WIDE], U32, "v_late", 2, 0)
         nc.vector.tensor_copy(v_late[:], tab_w[1][:].bitcast(U32).indirect(pick[:, (HALF + WIDE) // 16 : S // 16]))
-        quantise_h(2, 0, WIDE, HALF)
-        last = NT - 1
-        mid = HALF + WIDE
+        quantise_quarter(0, 2)
 
-        def deliver(n, lo, hi, bank, order):
-            g = lo // HALF
-            project(g, n, psum_banks[bank], order, lo - HALF * g, hi - HALF * g)
-            scatter(n, lo, hi, psum_banks[bank])
-
-        deliver(0, 0, WIDE, 6, (1, 0, 2))
-        deliver(0, WIDE, HALF, 4, (1, 0, 2))
-        deliver(1, 0, HALF, 5, (1, 0, 2))
-        drag_by_sign(0, 0)
-        deliver(2, 0, HALF, 0, (0, 1, 2))
-        quantise_h(0, 1, 0, WIDE)
-        drag_by_sign(1, 0)
-        deliver(last, 0, WIDE, 5, (0, 1, 2))
-        quantise_h(1, 1, 0, WIDE)
-        drag_by_sign(2, 0)
-        quantise_h(2, 1, 0, WIDE)
-        deliver(last, WIDE, HALF, 4, (0, 1, 2))
-        drag_by_sign(0, 1)
-        quantise_h(0, 1, WIDE, HALF)
-        drag_by_sign(1, 1)
-        deliver(0, HALF, mid, 5, (0, 1, 2))
-        quantise_h(1, 1, WIDE, HALF)
-        deliver(1, HALF, mid, 0, (0, 1, 2))
-        drag_by_sign(2, 1)
-        quantise_h(2, 1, WIDE, HALF)
-        deliver(2, HALF, mid, 4, (0, 1, 2))
-        for n in range(last):
-            deliver(n, mid, S, 1 + n, (1, 0, 2))
-        deliver(last, HALF, S, 6, (1, 0, 2))
+        sign_bank(2, 1, 0, 0)
+        deliver(0, 0)
+        sign_bank(2, 1, 1, 1)
+        steps = [
+            ((2, 1), (1, 0), (2, 0)),
+            ((1, 2), (3, 0), (0, 1)),
+            ((2, 2), (1, 1), (2, 1)),
+            ((0, 3), (3, 1), None),
+            ((1, 3), (0, 2), None),
+            ((2, 3), (1, 2), (2, 2)),
+        ]
+        for i, (unit, cover, after) in enumerate(steps):
+            if i > 0:
+                sign_unit(*unit, 2 * (i % 2))
+            sign_product(*unit)
+            deliver(*cover)
+            quantise_quarter(*unit)
+            if after is not None:
+                deliver(*after)
+        for n in range(NT - 1):
+            deliver(n, 3)
+        deliver(NT - 1, 2, 2)

@@ -138,9 +138,9 @@ def tile_list_contact_drag_store_kernel(
             nc.vector.quantize_mx(w1_w[b, a][:].bitcast(FP8X4), w1_s[b, a][:], w1_bf[b, a][:])
 
         banks, mags = {}, {}
-        held_by = {(0, 0, 1): staging[1, 0], (0, 0, 3): staging[1, 1], (0, 1, 0): staging[2, 0], (1, 0, 0): staging[2, 1], (2, 0, 1): (2, 0)}
+        held_by = {(0, 0, 1): staging[1, 0], (0, 0, 3): staging[1, 1], (0, 1, 0): staging[2, 0], (1, 0, 1): staging[2, 1], (1, 0, 3): (2, 0)}
         bank_of = {(0, 0, 0): 0, (0, 0, 1): 1, (0, 0, 2): 2, (0, 0, 3): 3, (0, 1, 0): 4, (0, 1, 1): 5}
-        bank_of.update({(1, 0, 0): 6, (1, 0, 1): 7, (1, 0, 2): 0, (1, 0, 3): 1, (2, 0, 0): 2, (2, 0, 1): 3})
+        bank_of.update({(1, 0, 0): 6, (1, 0, 1): 7, (1, 0, 2): 0, (1, 0, 3): 1, (2, 0, 0): 2, (2, 0, 1): 3, (2, 0, 2): 6, (2, 0, 3): 7})
 
         def product(b, g, s, a):
             if a == 0:
@@ -192,7 +192,13 @@ def tile_list_contact_drag_store_kernel(
 
         halves = {}
 
-        def sign_bank(b, q, u, bank_number):
+        taken = []
+
+        def next_bank():
+            taken.append(psum_banks[(4, 6, 7)[len(taken) % 3]])
+            return taken[-1]
+
+        def sign_bank(b, q, u):
             g, s = divmod(q, 2)
             cols = slice(WIDE * s, WIDE * (s + 1))
             if u == 0:
@@ -201,7 +207,7 @@ def tile_list_contact_drag_store_kernel(
                     ring.tile([P, 2, WIDE, 2], BF16, name="signs", bufs=3),
                 )
             squares, signs = halves[b, q]
-            bank = psum_banks[bank_number][:].rearrange("p (e c) -> p e c", e=2)
+            bank = next_bank()[:].rearrange("p (e c) -> p e c", e=2)
             for e in range(2):
                 wcols = slice(P * (2 * u + e), P * (2 * u + e + 1))
                 for a in range(KP):
@@ -225,9 +231,9 @@ def tile_list_contact_drag_store_kernel(
                 ACT.Sign,
             )
 
-        def sign_unit(b, q, first_bank):
-            sign_bank(b, q, 0, first_bank)
-            sign_bank(b, q, 1, first_bank + 1)
+        def sign_unit(b, q):
+            sign_bank(b, q, 0)
+            sign_bank(b, q, 1)
 
         def sign_product(b, q):
             g, s = divmod(q, 2)
@@ -267,7 +273,7 @@ def tile_list_contact_drag_store_kernel(
 
         def negate(n, lo, hi):
             g = lo // HALF
-            y_bank = psum_banks[ROTA + n]
+            y_bank = next_bank()
             project(g, n, y_bank, range(HP), lo - HALF * g, hi - HALF * g)
             nc.scalar.activation(forces[n][:, lo:hi], y_bank[:, 0 : hi - lo], ACT.Copy, scale=-1.0)
 
@@ -324,39 +330,45 @@ def tile_list_contact_drag_store_kernel(
         multiply(1, 0, 0)
         magnitude(1, 0, 1)
         quantise_w1(2, 0)
-        round_shared(2, 1)
         multiply(1, 0, 1)
         magnitude(1, 0, 2)
-        quantise_w1(2, 1)
+        round_shared(2, 1)
         multiply(1, 0, 2)
-        drag(1, 0, 3)
-        drag(2, 0, 0)
+        magnitude(1, 0, 3)
+        quantise_w1(2, 1)
+        multiply(1, 0, 3)
         quantise_h(1, 0)
-        drag(2, 0, 1)
-        quantise_quarter(2, 0)
         v_late = over_piece([P, WIDE], U32, "v_late", 2, 0)
         nc.vector.tensor_copy(v_late[:], tab_w[1][:].bitcast(U32).indirect(pick[:, (HALF + WIDE) // 16 : S // 16]))
+        drag(2, 0, 0)
         quantise_quarter(0, 2)
+        drag(2, 0, 1)
+        quantise_quarter(2, 0)
+        drag(2, 0, 2)
+        negate(0, 0, WIDE)
+        drag(2, 0, 3)
+        scatter(0, 0, WIDE)
+        quantise_quarter(2, 1)
 
-        sign_bank(2, 1, 0, 0)
-        deliver(0, 0)
-        sign_bank(2, 1, 1, 1)
-        steps = [
-            ((2, 1), (1, 0), (2, 0)),
-            ((1, 2), (3, 0), (0, 1)),
-            ((2, 2), (1, 1), (2, 1)),
-            ((0, 3), (3, 1), None),
-            ((1, 3), (0, 2), None),
-            ((2, 3), (1, 2), (2, 2)),
-        ]
-        for i, (unit, cover, after) in enumerate(steps):
-            if i > 0:
-                sign_unit(*unit, 2 * (i % 2))
+        def finish(unit, cover=None, after=None):
             sign_product(*unit)
-            deliver(*cover)
+            if cover is not None:
+                deliver(*cover)
             quantise_quarter(*unit)
             if after is not None:
                 deliver(*after)
+
+        deliver(1, 0)
+        sign_unit(1, 2)
+        finish((1, 2), (0, 1), (2, 0, 2))
+        sign_unit(2, 2)
+        finish((2, 2), (1, 1))
+        sign_unit(0, 3)
+        finish((0, 3), (3, 0, 2))
+        sign_unit(1, 3)
+        finish((1, 3), (0, 2))
+        sign_unit(2, 3)
+        finish((2, 3), (1, 2), (2, 2))
         for n in range(NT - 1):
             deliver(n, 3)
         deliver(NT - 1, 2, 2)

@@ -52,12 +52,12 @@ def tile_list_contact_drag_store_kernel(
             return shared.tile(shape, dtype, name=name, align_bytes=64, offset=4 * PACK * PASS * piece + skip)
 
         w1_raw = [[over_piece([P, PACK, PASS], F32, f"w1_raw{b}{a}", KP * b + a) for a in range(KP)] for b in range(HP)]
-        cd_all = kept([P, HP, PACK], F32, "cd_all")
-        cd_sb = [cd_all[:, b, :] for b in range(HP)]
-        cd_root = kept([P, HP * PACK], F32, "cd_root")
-        guess = kept([P, HP * PACK], F32, "guess")
-        inverse = kept([P, HP * PACK], F32, "inverse")
-        quotient = kept([P, HP * PACK], F32, "quotient")
+        cd_all = kept([P, HP, 2 * PACK], F32, "cd_all")
+        cd_sb = [cd_all[:, b, 0:PACK] for b in range(HP)]
+        cd_root = kept([P, HP, PACK], F32, "cd_root")
+        guess = kept([P, HP, PACK], F32, "guess")
+        inverse = kept([P, HP, PACK], F32, "inverse")
+        quotient = kept([P, HP, PACK], F32, "quotient")
         psum_banks = [psum.tile([P, HALF], F32, name=f"bank{i}") for i in range(2 * ROTA)]
         w4_w = kept([P, HP, 2 * N], U8, "w4_w")
         w4_s = kept([P, HP, N], U8, "w4_s")
@@ -78,7 +78,6 @@ def tile_list_contact_drag_store_kernel(
 
         load_w1(0, 0)
         nc.sync.dma_start(pick[:], offs)
-        nc.sync.dma_start(place[:], offs2)
         for i in range(4 * KP):
             if i == 3:
                 load_tab(0)
@@ -86,7 +85,7 @@ def tile_list_contact_drag_store_kernel(
             nc.sync.dma_start(tab_s[4 * a + r : P : 32, :].bitcast(I32), tab_scales[a, r:16:4, :].bitcast(I32))
         load_w1(0, 1)
         load_tab(1)
-        nc.sync.dma_start(cd_all[:], cd.rearrange("(b p t) -> p b t", p=P, t=PACK))
+        nc.sync.dma_start(cd_all[:, :, 0:PACK], cd.rearrange("(b p t) -> p b t", p=P, t=PACK))
         for b in range(1, HP):
             for a in range(KP):
                 load_w1(b, a)
@@ -96,6 +95,7 @@ def tile_list_contact_drag_store_kernel(
                 w4_scales[:, 4 * q : 4 * q + 4, :].rearrange("a r n -> r a n").bitcast(I32),
             )
         nc.sync.dma_start(w4_w[:].bitcast(I32), w4_words.rearrange("a p c -> p a c").bitcast(I32))
+        nc.sync.dma_start(place[:], offs2)
         nc.sync.dma_start(wgo_sb[:], wgo)
 
         v_w = [[kept([P, HALF], U32, f"v_w{g}{a}") for a in range(KP)] for g in range(HALVES)]
@@ -109,7 +109,7 @@ def tile_list_contact_drag_store_kernel(
             entries = pick[:, (HALF * g + lo) // 16 : (HALF * g + hi) // 16]
             nc.vector.tensor_copy(v_s[g][:, lo:hi], tab_s[:].indirect(entries))
 
-        cd_flat = cd_all[:].rearrange("p b t -> p (b t)")
+        cd_flat = cd_all[:, :, 0:PACK]
         nc.scalar.activation(guess[:], cd_flat, ACT.Sqrt)
 
         w1_bf, w1_w, w1_s = {}, {}, {}
@@ -223,7 +223,7 @@ def tile_list_contact_drag_store_kernel(
             for e in range(2):
                 t = 2 * u + e
                 nc.scalar.activation(
-                    squares[:, u, :, e], bank[:, e, :], ACT.Square, scale=cd_root[:, PACK * b + t : PACK * b + t + 1]
+                    squares[:, u, :, e], bank[:, e, :], ACT.Square, scale=cd_root[:, b, t : t + 1]
                 )
             nc.scalar.activation(
                 signs[:, u, :, :].rearrange("p (c i) e -> p c e i", i=2),
@@ -305,13 +305,13 @@ def tile_list_contact_drag_store_kernel(
         quantise_w1(0, 1)
         gather_words(0, 1, 0, HALF // 2)
         gather_words(0, 1, HALF // 2, HALF)
-        nc.vector.reciprocal(inverse[:], guess[:])
         gather_words(1, 1, 0, WIDE)
-        nc.vector.scalar_tensor_tensor(quotient[:], cd_flat, 0.5, inverse[:], MULT, MULT)
+        nc.vector.reciprocal(inverse[:], guess[:])
 
         drag(0, 0, 0)
-        nc.vector.scalar_tensor_tensor(cd_root[:], guess[:], 0.5, quotient[:], MULT, ADD)
+        nc.vector.scalar_tensor_tensor(quotient[:], cd_flat, 0.5, inverse[:], MULT, MULT)
         drag(0, 0, 1)
+        nc.vector.scalar_tensor_tensor(cd_root[:], guess[:], 0.5, quotient[:], MULT, ADD)
         magnitude(0, 0, 2)
         round_shared(1, 0)
         multiply(0, 0, 2)

@@ -25,9 +25,16 @@ HP = H // PASS
 NT = N // P
 HALF = 512
 HALVES = S // HALF
+QUARTER = 256
 TOK = 128
-WIDE = 256
-ROTA = 4
+BANKS = 8
+GROUP = 16
+QUADRANT = 32
+PIECE_BYTES = 4 * PACK * PASS
+ROUNDED_BYTES = 2 * PACK * PASS
+WALK = 4
+SCALES_AHEAD = 3
+LATE_BANKS = (4, 6, 7)
 
 
 def tile_list_contact_drag_store_kernel(
@@ -43,22 +50,21 @@ def tile_list_contact_drag_store_kernel(
         def kept(shape, dtype, name):
             return keep.tile(shape, dtype, name=name, align_bytes=64)
 
-        pick = keep.tile([P, S // 16], U16, name="pick")
-        place = keep.tile([P, S // 16], U16, name="place")
+        def over_piece(shape, dtype, name, piece, skip=0):
+            return shared.tile(shape, dtype, name=name, align_bytes=64, offset=PIECE_BYTES * piece + skip)
+
+        pick = keep.tile([P, S // GROUP], U16, name="pick")
+        place = keep.tile([P, S // GROUP], U16, name="place")
         tab_w = [kept([P, T], I32, f"tab_w{a}") for a in range(KP)]
         tab_s = kept([P, T], U8, "tab_s")
-
-        def over_piece(shape, dtype, name, piece, skip=0):
-            return shared.tile(shape, dtype, name=name, align_bytes=64, offset=4 * PACK * PASS * piece + skip)
-
         w1_raw = [[over_piece([P, PACK, PASS], F32, f"w1_raw{b}{a}", KP * b + a) for a in range(KP)] for b in range(HP)]
-        cd_all = kept([P, HP, 2 * PACK], F32, "cd_all")
-        cd_sb = [cd_all[:, b, 0:PACK] for b in range(HP)]
+        cd_padded = kept([P, HP, 2 * PACK], F32, "cd_padded")
+        cd_sb = cd_padded[:, :, 0:PACK]
         cd_root = kept([P, HP, PACK], F32, "cd_root")
         guess = kept([P, HP, PACK], F32, "guess")
         inverse = kept([P, HP, PACK], F32, "inverse")
         quotient = kept([P, HP, PACK], F32, "quotient")
-        psum_banks = [psum.tile([P, HALF], F32, name=f"bank{i}") for i in range(2 * ROTA)]
+        psum_banks = [psum.tile([P, HALF], F32, name=f"bank{i}") for i in range(BANKS)]
         w4_w = kept([P, HP, 2 * N], U8, "w4_w")
         w4_s = kept([P, HP, N], U8, "w4_s")
         wgo_sb = kept([P, S], F32, "wgo_sb")
@@ -79,19 +85,19 @@ def tile_list_contact_drag_store_kernel(
         load_w1(0, 0)
         nc.sync.dma_start(pick[:], offs)
         for i in range(4 * KP):
-            if i == 3:
+            if i == SCALES_AHEAD:
                 load_tab(0)
             r, a = divmod(i, KP)
-            nc.sync.dma_start(tab_s[4 * a + r : P : 32, :].bitcast(I32), tab_scales[a, r:16:4, :].bitcast(I32))
+            nc.sync.dma_start(tab_s[4 * a + r : P : QUADRANT, :].bitcast(I32), tab_scales[a, r:16:4, :].bitcast(I32))
         load_w1(0, 1)
         load_tab(1)
-        nc.sync.dma_start(cd_all[:, :, 0:PACK], cd.rearrange("(b p t) -> p b t", p=P, t=PACK))
+        nc.sync.dma_start(cd_sb, cd.rearrange("(b p t) -> p b t", p=P, t=PACK))
         for b in range(1, HP):
             for a in range(KP):
                 load_w1(b, a)
-        for q in range(4):
+        for q in range(P // QUADRANT):
             nc.sync.dma_start(
-                w4_s[32 * q : 32 * q + 4, :, :].bitcast(I32),
+                w4_s[QUADRANT * q : QUADRANT * q + 4, :, :].bitcast(I32),
                 w4_scales[:, 4 * q : 4 * q + 4, :].rearrange("a r n -> r a n").bitcast(I32),
             )
         nc.sync.dma_start(w4_w[:].bitcast(I32), w4_words.rearrange("a p c -> p a c").bitcast(I32))
@@ -101,36 +107,39 @@ def tile_list_contact_drag_store_kernel(
         v_w = [[kept([P, HALF], U32, f"v_w{g}{a}") for a in range(KP)] for g in range(HALVES)]
         v_s = [kept([P, HALF], U8, f"v_s{g}") for g in range(HALVES)]
 
+        def entries(offsets, lo, hi):
+            return offsets[:, lo // GROUP : hi // GROUP]
+
         def gather_words(g, a, lo=0, hi=HALF):
-            entries = pick[:, (HALF * g + lo) // 16 : (HALF * g + hi) // 16]
-            nc.vector.tensor_copy(v_w[g][a][:, lo:hi], tab_w[a][:].bitcast(U32).indirect(entries))
+            picked = entries(pick, HALF * g + lo, HALF * g + hi)
+            nc.vector.tensor_copy(v_w[g][a][:, lo:hi], tab_w[a][:].bitcast(U32).indirect(picked))
 
-        def gather_scales(g, lo=0, hi=HALF):
-            entries = pick[:, (HALF * g + lo) // 16 : (HALF * g + hi) // 16]
-            nc.vector.tensor_copy(v_s[g][:, lo:hi], tab_s[:].indirect(entries))
+        def gather_scales(g):
+            nc.vector.tensor_copy(v_s[g][:], tab_s[:].indirect(entries(pick, HALF * g, HALF * (g + 1))))
 
-        cd_flat = cd_all[:, :, 0:PACK]
-        nc.scalar.activation(guess[:], cd_flat, ACT.Sqrt)
+        nc.scalar.activation(guess[:], cd_sb, ACT.Sqrt)
 
         w1_bf, w1_w, w1_s = {}, {}, {}
-        staging = {(1, 0): (0, 0), (1, 1): (1, 0), (2, 0): (0, 4096), (2, 1): (1, 4096)}
         h_bf, h_w, h_s = {}, {}, {}
         forces = [kept([P, S], F32, f"force{n}") for n in range(NT)]
 
-        def round_w1(b, a, pair, lo, hi, engine_copy):
+        def staging(b, a):
+            return a, ROUNDED_BYTES * (b - 1)
+
+        def round_w1(b, a, pair, engine_copy):
             if (b, a) not in w1_bf:
                 if b == 0:
                     w1_bf[b, a] = kept([P, PACK * PASS], BF16, f"w1_first{a}")
                 else:
-                    w1_bf[b, a] = over_piece([P, PACK * PASS], BF16, f"w1_bf{b}{a}", *staging[b, a])
+                    w1_bf[b, a] = over_piece([P, PACK * PASS], BF16, f"w1_bf{b}{a}", *staging(b, a))
             slots = slice(2 * pair, 2 * pair + 2)
             src = w1_raw[b][a][:].rearrange("p j (m t) -> p m j t", t=PACK)
             dst = w1_bf[b, a][:].rearrange("p (t m j) -> p m j t", t=PACK, j=PACK)
-            engine_copy(dst[:, lo:hi, :, slots], src[:, lo:hi, :, slots])
+            engine_copy(dst[:, :, :, slots], src[:, :, :, slots])
 
         def round_shared(b, a):
-            round_w1(b, a, 0, 0, P, nc.vector.tensor_copy)
-            round_w1(b, a, 1, 0, P, nc.scalar.copy)
+            round_w1(b, a, 0, nc.vector.tensor_copy)
+            round_w1(b, a, 1, nc.scalar.copy)
 
         def quantise_w1(b, a):
             w1_w[b, a] = kept([P, PASS], U32, f"w1_w{b}{a}")
@@ -138,13 +147,21 @@ def tile_list_contact_drag_store_kernel(
             nc.vector.quantize_mx(w1_w[b, a][:].bitcast(FP8X4), w1_s[b, a][:], w1_bf[b, a][:])
 
         banks, mags = {}, {}
-        held_by = {(0, 0, 1): staging[1, 0], (0, 0, 3): staging[1, 1], (0, 1, 0): staging[2, 0], (1, 0, 1): staging[2, 1], (1, 0, 3): (2, 0)}
-        bank_of = {(0, 0, 0): 0, (0, 0, 1): 1, (0, 0, 2): 2, (0, 0, 3): 3, (0, 1, 0): 4, (0, 1, 1): 5}
-        bank_of.update({(1, 0, 0): 6, (1, 0, 1): 7, (1, 0, 2): 0, (1, 0, 3): 1, (2, 0, 0): 2, (2, 0, 1): 3, (2, 0, 2): 6, (2, 0, 3): 7})
+        late_piece = KP
+        magnitudes_at = {
+            (0, 0, 1): staging(1, 0),
+            (0, 0, 3): staging(1, 1),
+            (0, 1, 0): staging(2, 0),
+            (1, 0, 1): staging(2, 1),
+            (1, 0, 3): (late_piece, 0),
+        }
+        steps_in_turn = 12
 
         def product(b, g, s, a):
             if a == 0:
-                banks[b, g, s] = psum_banks[bank_of[b, g, s]][:].rearrange("p (t c) -> p t c", t=PACK)
+                i = len(banks)
+                number = i % BANKS if i < steps_in_turn else LATE_BANKS[1 + i - steps_in_turn]
+                banks[b, g, s] = psum_banks[number][:].rearrange("p (t c) -> p t c", t=PACK)
             cols = slice(TOK * s, TOK * (s + 1))
             for t in range(PACK):
                 wcols = slice(P * t, P * (t + 1))
@@ -162,14 +179,14 @@ def tile_list_contact_drag_store_kernel(
             if (b, g, s) not in banks:
                 product(b, g, s, 0)
             product(b, g, s, 1)
-            if (b, g, s) in held_by:
-                mag = over_piece([P, HALF], F32, f"mag{b}{g}{s}", *held_by[b, g, s])[:]
+            if (b, g, s) in magnitudes_at:
+                mag = over_piece([P, HALF], F32, f"mag{b}{g}{s}", *magnitudes_at[b, g, s])[:]
             else:
                 mag = ring.tile([P, HALF], F32, name="mag", bufs=4)[:]
             mags[b, g, s] = mag.rearrange("p (t c) -> p t c", t=PACK)
             for t in range(PACK):
                 nc.scalar.activation(
-                    mags[b, g, s][:, t, :], banks[b, g, s][:, t, :], ACT.Abs, scale=cd_sb[b][:, t : t + 1]
+                    mags[b, g, s][:, t, :], banks[b, g, s][:, t, :], ACT.Abs, scale=cd_sb[:, b, t : t + 1]
                 )
 
         def h_tile(b, g):
@@ -180,9 +197,9 @@ def tile_list_contact_drag_store_kernel(
         def multiply(b, g, s):
             dst = h_tile(b, g)[:, PACK * TOK * s : PACK * TOK * (s + 1)]
             nc.vector.tensor_tensor(
-                dst.rearrange("p (c i t) -> p c t i", i=4, t=PACK),
-                banks[b, g, s].rearrange("p t (c i) -> p c t i", i=4),
-                mags[b, g, s].rearrange("p t (c i) -> p c t i", i=4),
+                dst.rearrange("p (c i t) -> p c t i", i=WALK, t=PACK),
+                banks[b, g, s].rearrange("p t (c i) -> p c t i", i=WALK),
+                mags[b, g, s].rearrange("p t (c i) -> p c t i", i=WALK),
                 MULT,
             )
 
@@ -190,23 +207,17 @@ def tile_list_contact_drag_store_kernel(
             magnitude(b, g, s)
             multiply(b, g, s)
 
-        halves = {}
-
+        factors = {}
         taken = []
 
         def next_bank():
-            taken.append(psum_banks[(4, 6, 7)[len(taken) % 3]])
+            taken.append(psum_banks[LATE_BANKS[len(taken) % len(LATE_BANKS)]])
             return taken[-1]
 
         def sign_bank(b, q, u):
             g, s = divmod(q, 2)
-            cols = slice(WIDE * s, WIDE * (s + 1))
-            if u == 0:
-                halves[b, q] = (
-                    ring.tile([P, 2, WIDE, 2], BF16, name="squares", bufs=3),
-                    ring.tile([P, 2, WIDE, 2], BF16, name="signs", bufs=3),
-                )
-            squares, signs = halves[b, q]
+            cols = slice(QUARTER * s, QUARTER * (s + 1))
+            squares, signs = factors[b, q]
             bank = next_bank()[:].rearrange("p (e c) -> p e c", e=2)
             for e in range(2):
                 wcols = slice(P * (2 * u + e), P * (2 * u + e + 1))
@@ -222,23 +233,17 @@ def tile_list_contact_drag_store_kernel(
                     )
             for e in range(2):
                 t = 2 * u + e
-                nc.scalar.activation(
-                    squares[:, u, :, e], bank[:, e, :], ACT.Square, scale=cd_root[:, b, t : t + 1]
-                )
+                nc.scalar.activation(squares[:, u, :, e], bank[:, e, :], ACT.Square, scale=cd_root[:, b, t : t + 1])
             nc.scalar.activation(
                 signs[:, u, :, :].rearrange("p (c i) e -> p c e i", i=2),
                 bank.rearrange("p e (c i) -> p c e i", i=2),
                 ACT.Sign,
             )
 
-        def sign_unit(b, q):
-            sign_bank(b, q, 0)
-            sign_bank(b, q, 1)
-
         def sign_product(b, q):
             g, s = divmod(q, 2)
-            squares, signs = halves[b, q]
-            dst = h_tile(b, g)[:, PACK * WIDE * s : PACK * WIDE * (s + 1)]
+            squares, signs = factors[b, q]
+            dst = h_tile(b, g)[:, PACK * QUARTER * s : PACK * QUARTER * (s + 1)]
             nc.vector.tensor_tensor(
                 dst.rearrange("p (c u e) -> p c u e", u=2, e=2),
                 squares[:].rearrange("p u c e -> p c u e"),
@@ -249,7 +254,7 @@ def tile_list_contact_drag_store_kernel(
         def quantise_h(b, g, lo=0, hi=HALF):
             if (b, g) not in h_w:
                 if (b, g) == (0, 1):
-                    h_w[b, g] = over_piece([P, HALF], U32, "h_w01", 2, 1024)
+                    h_w[b, g] = over_piece([P, HALF], U32, "h_w01", late_piece, 4 * QUARTER)
                 else:
                     h_w[b, g] = kept([P, HALF], U32, f"h_w{b}{g}")
                 h_s[b, g] = kept([P, HALF], U8, f"h_s{b}{g}")
@@ -257,44 +262,54 @@ def tile_list_contact_drag_store_kernel(
                 h_w[b, g][:, lo:hi].bitcast(FP8X4), h_s[b, g][:, lo:hi], h_bf[b, g][:, PACK * lo : PACK * hi]
             )
 
-        def project(g, n, y_bank, order, lo=0, hi=HALF):
+        def quantise_quarter(b, q):
+            g, s = divmod(q, 2)
+            quantise_h(b, g, QUARTER * s, QUARTER * (s + 1))
+
+        def negate(n, lo, hi):
+            g, first = divmod(lo, HALF)
+            y_bank = next_bank()
             width = HALF if hi - lo == HALF else TOK
-            passes = [(b, c) for b in order for c in range(lo, hi, width)]
+            passes = [(b, c) for b in range(HP) for c in range(0, hi - lo, width)]
             for b, c in passes:
+                cols = slice(first + c, first + c + width)
                 nc.tensor.matmul_mx(
-                    y_bank[:, c - lo : c - lo + width],
+                    y_bank[:, c : c + width],
                     lhsT=w4_w[:, b, 2 * P * n : 2 * P * (n + 1)].bitcast(FP4X4),
                     lhsT_scale=w4_s[:, b, P * n : P * (n + 1)],
-                    rhs=h_w[b, g][:, c : c + width].bitcast(FP8X4),
-                    rhs_scale=h_s[b, g][:, c : c + width],
+                    rhs=h_w[b, g][:, cols].bitcast(FP8X4),
+                    rhs_scale=h_s[b, g][:, cols],
                     start=((b, c) == passes[0]),
                     stop=((b, c) == passes[-1]),
                 )
-
-        def negate(n, lo, hi):
-            g = lo // HALF
-            y_bank = next_bank()
-            project(g, n, y_bank, range(HP), lo - HALF * g, hi - HALF * g)
             nc.scalar.activation(forces[n][:, lo:hi], y_bank[:, 0 : hi - lo], ACT.Copy, scale=-1.0)
 
         def scatter(n, lo, hi):
-            places = place[:, lo // 16 : hi // 16]
+            places = entries(place, lo, hi)
             nc.vector.tensor_tensor(pages[n][:].indirect(places), forces[n][:, lo:hi], wgo_sb[:, lo:hi], MULT)
             if hi == S:
                 nc.sync.dma_start(out[P * n : P * (n + 1), :], pages[n][:])
 
         def deliver(n, q, count=1):
-            negate(n, WIDE * q, WIDE * (q + count))
-            scatter(n, WIDE * q, WIDE * (q + count))
+            negate(n, QUARTER * q, QUARTER * (q + count))
+            scatter(n, QUARTER * q, QUARTER * (q + count))
 
-        def quantise_quarter(b, q):
-            g, s = divmod(q, 2)
-            quantise_h(b, g, WIDE * s, WIDE * (s + 1))
+        def sign_unit(b, q, between, after=None):
+            factors[b, q] = (
+                ring.tile([P, 2, QUARTER, 2], BF16, name="squares", bufs=3),
+                ring.tile([P, 2, QUARTER, 2], BF16, name="signs", bufs=3),
+            )
+            for u in range(2):
+                sign_bank(b, q, u)
+            sign_product(b, q)
+            deliver(*between)
+            quantise_quarter(b, q)
+            if after is not None:
+                deliver(*after)
 
-        round_w1(0, 0, 0, 0, P, nc.scalar.copy)
-        round_w1(0, 0, 1, 0, P, nc.scalar.copy)
-        round_w1(0, 1, 0, 0, P, nc.scalar.copy)
-        round_w1(0, 1, 1, 0, P, nc.scalar.copy)
+        for a in range(KP):
+            for pair in range(2):
+                round_w1(0, a, pair, nc.scalar.copy)
         gather_words(0, 0)
         gather_scales(0)
         quantise_w1(0, 0)
@@ -303,13 +318,13 @@ def tile_list_contact_drag_store_kernel(
         gather_words(1, 0)
         gather_scales(1)
         quantise_w1(0, 1)
-        gather_words(0, 1, 0, HALF // 2)
-        gather_words(0, 1, HALF // 2, HALF)
-        gather_words(1, 1, 0, WIDE)
+        gather_words(0, 1, 0, QUARTER)
+        gather_words(0, 1, QUARTER, HALF)
+        gather_words(1, 1, 0, QUARTER)
         nc.vector.reciprocal(inverse[:], guess[:])
 
         drag(0, 0, 0)
-        nc.vector.scalar_tensor_tensor(quotient[:], cd_flat, 0.5, inverse[:], MULT, MULT)
+        nc.vector.scalar_tensor_tensor(quotient[:], cd_sb, 0.5, inverse[:], MULT, MULT)
         drag(0, 0, 1)
         nc.vector.scalar_tensor_tensor(cd_root[:], guess[:], 0.5, quotient[:], MULT, ADD)
         magnitude(0, 0, 2)
@@ -324,6 +339,7 @@ def tile_list_contact_drag_store_kernel(
         magnitude(0, 1, 1)
         quantise_w1(1, 1)
         multiply(0, 1, 0)
+
         magnitude(1, 0, 0)
         round_shared(2, 0)
         multiply(0, 1, 1)
@@ -338,37 +354,27 @@ def tile_list_contact_drag_store_kernel(
         quantise_w1(2, 1)
         multiply(1, 0, 3)
         quantise_h(1, 0)
-        v_late = over_piece([P, WIDE], U32, "v_late", 2, 0)
-        nc.vector.tensor_copy(v_late[:], tab_w[1][:].bitcast(U32).indirect(pick[:, (HALF + WIDE) // 16 : S // 16]))
+
+        v_late = over_piece([P, QUARTER], U32, "v_late", late_piece)
+        nc.vector.tensor_copy(v_late[:], tab_w[1][:].bitcast(U32).indirect(entries(pick, S - QUARTER, S)))
         drag(2, 0, 0)
         quantise_quarter(0, 2)
         drag(2, 0, 1)
         quantise_quarter(2, 0)
         drag(2, 0, 2)
-        negate(0, 0, WIDE)
+        negate(0, 0, QUARTER)
         drag(2, 0, 3)
-        scatter(0, 0, WIDE)
+        scatter(0, 0, QUARTER)
         quantise_quarter(2, 1)
-
-        def finish(unit, cover=None, after=None):
-            sign_product(*unit)
-            if cover is not None:
-                deliver(*cover)
-            quantise_quarter(*unit)
-            if after is not None:
-                deliver(*after)
-
         deliver(1, 0)
-        sign_unit(1, 2)
-        finish((1, 2), (0, 1), (2, 0, 2))
-        sign_unit(2, 2)
-        finish((2, 2), (1, 1))
-        sign_unit(0, 3)
-        finish((0, 3), (3, 0, 2))
-        sign_unit(1, 3)
-        finish((1, 3), (0, 2))
-        sign_unit(2, 3)
-        finish((2, 3), (1, 2), (2, 2))
-        for n in range(NT - 1):
+
+        sign_unit(1, 2, between=(0, 1), after=(2, 0, 2))
+        sign_unit(2, 2, between=(1, 1))
+        sign_unit(0, 3, between=(3, 0))
+        sign_unit(1, 3, between=(3, 1))
+        sign_unit(2, 3, between=(0, 2), after=(1, 2))
+
+        for n in range(NT // 2):
             deliver(n, 3)
-        deliver(NT - 1, 2, 2)
+        for n in range(NT // 2, NT):
+            deliver(n, 2, 2)

@@ -15,7 +15,6 @@ FP8X4 = mybir.dt.float8_e4m3fn_x4
 FP4X4 = mybir.dt.float4_e2m1fn_x4
 ACT = mybir.ActivationFunctionType
 MULT = mybir.AluOpType.mult
-ADD = mybir.AluOpType.add
 
 P = 128
 PACK = 4
@@ -23,18 +22,21 @@ PASS = P * PACK
 KP = K // PASS
 HP = H // PASS
 NT = N // P
-HALF = 512
-HALVES = S // HALF
-QUARTER = 256
-TOK = 128
+CHUNK = 256
+CHUNKS = S // CHUNK
+STEP = 128
+BANK = 512
 BANKS = 8
+EARLY_BANKS = (0, 1, 2, 3, 4, 5, 6, 7, 6, 0, 1, 2, 3, 0)
+LATE_BANKS = (4, 5, 7, 3)
 GROUP = 16
 QUADRANT = 32
-PIECE_BYTES = 4 * PACK * PASS
-ROUNDED_BYTES = 2 * PACK * PASS
+PAIR = 2 * P
 WALK = 4
 SCALES_AHEAD = 3
-LATE_BANKS = (4, 6, 7)
+PIECE_BYTES = 4 * PACK * PASS
+MAG_BYTES = 4 * BANK
+WORDS_BYTES = 4 * CHUNK
 
 
 def tile_list_contact_drag_store_kernel(
@@ -50,21 +52,21 @@ def tile_list_contact_drag_store_kernel(
         def kept(shape, dtype, name):
             return keep.tile(shape, dtype, name=name, align_bytes=64)
 
-        def over_piece(shape, dtype, name, piece, skip=0):
-            return shared.tile(shape, dtype, name=name, align_bytes=64, offset=PIECE_BYTES * piece + skip)
+        def placed(shape, dtype, name, offset):
+            return shared.tile(shape, dtype, name=name, align_bytes=64, offset=offset)
+
+        def piece_at(b, a):
+            return PIECE_BYTES * (KP * b + a)
 
         pick = keep.tile([P, S // GROUP], U16, name="pick")
         place = keep.tile([P, S // GROUP], U16, name="place")
         tab_w = [kept([P, T], I32, f"tab_w{a}") for a in range(KP)]
         tab_s = kept([P, T], U8, "tab_s")
-        w1_raw = [[over_piece([P, PACK, PASS], F32, f"w1_raw{b}{a}", KP * b + a) for a in range(KP)] for b in range(HP)]
+        w1_raw = [[placed([P, PACK, PASS], F32, f"w1_raw{b}{a}", piece_at(b, a)) for a in range(KP)] for b in range(HP)]
         cd_padded = kept([P, HP, 2 * PACK], F32, "cd_padded")
         cd_sb = cd_padded[:, :, 0:PACK]
         cd_root = kept([P, HP, PACK], F32, "cd_root")
-        guess = kept([P, HP, PACK], F32, "guess")
-        inverse = kept([P, HP, PACK], F32, "inverse")
-        quotient = kept([P, HP, PACK], F32, "quotient")
-        psum_banks = [psum.tile([P, HALF], F32, name=f"bank{i}") for i in range(BANKS)]
+        psum_banks = [psum.tile([P, BANK], F32, name=f"bank{i}") for i in range(BANKS)]
         w4_w = kept([P, HP, 2 * N], U8, "w4_w")
         w4_s = kept([P, HP, N], U8, "w4_s")
         wgo_sb = kept([P, S], F32, "wgo_sb")
@@ -104,133 +106,126 @@ def tile_list_contact_drag_store_kernel(
         nc.sync.dma_start(place[:], offs2)
         nc.sync.dma_start(wgo_sb[:], wgo)
 
-        v_w = [[kept([P, HALF], U32, f"v_w{g}{a}") for a in range(KP)] for g in range(HALVES)]
-        v_s = [kept([P, HALF], U8, f"v_s{g}") for g in range(HALVES)]
-
-        def entries(offsets, lo, hi):
-            return offsets[:, lo // GROUP : hi // GROUP]
-
-        def gather_words(g, a, lo=0, hi=HALF):
-            picked = entries(pick, HALF * g + lo, HALF * g + hi)
-            nc.vector.tensor_copy(v_w[g][a][:, lo:hi], tab_w[a][:].bitcast(U32).indirect(picked))
-
-        def gather_scales(g):
-            nc.vector.tensor_copy(v_s[g][:], tab_s[:].indirect(entries(pick, HALF * g, HALF * (g + 1))))
-
-        nc.scalar.activation(guess[:], cd_sb, ACT.Sqrt)
-
-        w1_bf, w1_w, w1_s = {}, {}, {}
-        h_bf, h_w, h_s = {}, {}, {}
-        forces = [kept([P, S], F32, f"force{n}") for n in range(NT)]
-
-        def staging(b, a):
-            return a, ROUNDED_BYTES * (b - 1)
-
-        def round_w1(b, a, pair, engine_copy):
-            if (b, a) not in w1_bf:
-                if b == 0:
-                    w1_bf[b, a] = kept([P, PACK * PASS], BF16, f"w1_first{a}")
-                else:
-                    w1_bf[b, a] = over_piece([P, PACK * PASS], BF16, f"w1_bf{b}{a}", *staging(b, a))
-            slots = slice(2 * pair, 2 * pair + 2)
-            src = w1_raw[b][a][:].rearrange("p j (m t) -> p m j t", t=PACK)
-            dst = w1_bf[b, a][:].rearrange("p (t m j) -> p m j t", t=PACK, j=PACK)
-            engine_copy(dst[:, :, :, slots], src[:, :, :, slots])
-
-        def round_shared(b, a):
-            round_w1(b, a, 0, nc.vector.tensor_copy)
-            round_w1(b, a, 1, nc.scalar.copy)
-
-        def quantise_w1(b, a):
-            w1_w[b, a] = kept([P, PASS], U32, f"w1_w{b}{a}")
-            w1_s[b, a] = kept([P, PASS], U8, f"w1_s{b}{a}")
-            nc.vector.quantize_mx(w1_w[b, a][:].bitcast(FP8X4), w1_s[b, a][:], w1_bf[b, a][:])
-
-        banks, mags = {}, {}
-        late_piece = KP
-        magnitudes_at = {
-            (0, 0, 1): staging(1, 0),
-            (0, 0, 3): staging(1, 1),
-            (0, 1, 0): staging(2, 0),
-            (1, 0, 1): staging(2, 1),
-            (1, 0, 3): (late_piece, 0),
-        }
-        steps_in_turn = 12
-
-        def product(b, g, s, a):
-            if a == 0:
-                i = len(banks)
-                number = i % BANKS if i < steps_in_turn else LATE_BANKS[1 + i - steps_in_turn]
-                banks[b, g, s] = psum_banks[number][:].rearrange("p (t c) -> p t c", t=PACK)
-            cols = slice(TOK * s, TOK * (s + 1))
-            for t in range(PACK):
-                wcols = slice(P * t, P * (t + 1))
-                nc.tensor.matmul_mx(
-                    banks[b, g, s][:, t, :],
-                    lhsT=w1_w[b, a][:, wcols].bitcast(FP8X4),
-                    lhsT_scale=w1_s[b, a][:, wcols],
-                    rhs=v_w[g][a][:, cols].bitcast(FP8X4),
-                    rhs_scale=v_s[g][4 * a : P, cols],
-                    start=(a == 0 and t == 0),
-                    stop=(a == KP - 1 and t == PACK - 1),
-                )
-
-        def magnitude(b, g, s):
-            if (b, g, s) not in banks:
-                product(b, g, s, 0)
-            product(b, g, s, 1)
-            if (b, g, s) in magnitudes_at:
-                mag = over_piece([P, HALF], F32, f"mag{b}{g}{s}", *magnitudes_at[b, g, s])[:]
-            else:
-                mag = ring.tile([P, HALF], F32, name="mag", bufs=4)[:]
-            mags[b, g, s] = mag.rearrange("p (t c) -> p t c", t=PACK)
-            for t in range(PACK):
-                nc.scalar.activation(
-                    mags[b, g, s][:, t, :], banks[b, g, s][:, t, :], ACT.Abs, scale=cd_sb[:, b, t : t + 1]
-                )
-
-        def h_tile(b, g):
-            if (b, g) not in h_bf:
-                h_bf[b, g] = kept([P, PACK * HALF], BF16, f"h_bf{b}{g}")
-            return h_bf[b, g]
-
-        def multiply(b, g, s):
-            dst = h_tile(b, g)[:, PACK * TOK * s : PACK * TOK * (s + 1)]
-            nc.vector.tensor_tensor(
-                dst.rearrange("p (c i t) -> p c t i", i=WALK, t=PACK),
-                banks[b, g, s].rearrange("p t (c i) -> p c t i", i=WALK),
-                mags[b, g, s].rearrange("p t (c i) -> p c t i", i=WALK),
-                MULT,
-            )
-
-        def drag(b, g, s):
-            magnitude(b, g, s)
-            multiply(b, g, s)
-
-        factors = {}
         taken = []
 
         def next_bank():
-            taken.append(psum_banks[LATE_BANKS[len(taken) % len(LATE_BANKS)]])
+            i = len(taken)
+            number = EARLY_BANKS[i] if i < len(EARLY_BANKS) else LATE_BANKS[(i - len(EARLY_BANKS)) % len(LATE_BANKS)]
+            taken.append(psum_banks[number])
             return taken[-1]
 
-        def sign_bank(b, q, u):
-            g, s = divmod(q, 2)
-            cols = slice(QUARTER * s, QUARTER * (s + 1))
-            squares, signs = factors[b, q]
+        def entries(offsets, c, count=1):
+            return offsets[:, CHUNK * c // GROUP : CHUNK * (c + count) // GROUP]
+
+        v_first = kept([P, S], U32, "v_first")
+        v_s = kept([P, S], U8, "v_s")
+        v_second = {}
+
+        def gather_first(c, count):
+            cols = slice(CHUNK * c, CHUNK * (c + count))
+            nc.vector.tensor_copy(v_first[:, cols], tab_w[0][:].bitcast(U32).indirect(entries(pick, c, count)))
+
+        def gather_scales(c, count):
+            cols = slice(CHUNK * c, CHUNK * (c + count))
+            nc.vector.tensor_copy(v_s[:, cols], tab_s[:].indirect(entries(pick, c, count)))
+
+        def gather_second(c, tile):
+            v_second[c] = tile
+            nc.vector.tensor_copy(tile[:], tab_w[1][:].bitcast(U32).indirect(entries(pick, c)))
+
+        def v_words(a, c, lo, hi):
+            return v_first[:, CHUNK * c + lo : CHUNK * c + hi] if a == 0 else v_second[c][:, lo:hi]
+
+        w1_w = {}
+
+        def new_w1(b, a, at=None):
+            name = f"w1_w{b}{a}"
+            w1_w[b, a] = kept([P, PASS], U32, name) if at is None else placed([P, PASS], U32, name, at)
+
+        for b, a in ((0, 0), (0, 1), (1, 1), (2, 0), (2, 1)):
+            new_w1(b, a)
+        w1_s = {(b, a): kept([P, PASS], U8, f"w1_s{b}{a}") for b in range(HP) for a in range(KP)}
+        rounded = {}
+
+        def pair_views(b, a, u, dst):
+            src = w1_raw[b][a][:].rearrange("p j (m t) -> p m t j", t=PACK)[:, :, 2 * u : 2 * u + 2, :]
+            return dst.rearrange("p (e m j) -> p m e j", e=2, j=PACK), src
+
+        def round_on_scalar(b, a, u, dst):
+            rounded[b, a, u] = dst
+            to, src = pair_views(b, a, u, dst)
+            nc.scalar.copy(to.rearrange("p m e j -> p m j e"), src.rearrange("p m e j -> p m j e"))
+
+        def round_on_vector(b, a, u, dst):
+            rounded[b, a, u] = dst
+            to, src = pair_views(b, a, u, dst)
+            nc.vector.tensor_copy(to.rearrange("p m e j -> p m j e"), src.rearrange("p m e j -> p m j e"))
+
+        def quantise_pair(b, a, u):
+            cols = slice(PAIR * u, PAIR * (u + 1))
+            nc.vector.quantize_mx(w1_w[b, a][:, cols].bitcast(FP8X4), w1_s[b, a][:, cols], rounded[b, a, u])
+
+        banks, mags, h_bf, h_w, h_s, factors, forces = {}, {}, {}, {}, {}, {}, {}
+
+        def first_pass(dst, b, t, a, c, lo, hi, start, stop):
+            wcols = slice(P * t, P * (t + 1))
+            nc.tensor.matmul_mx(
+                dst,
+                lhsT=w1_w[b, a][:, wcols].bitcast(FP8X4),
+                lhsT_scale=w1_s[b, a][:, wcols],
+                rhs=v_words(a, c, lo, hi).bitcast(FP8X4),
+                rhs_scale=v_s[4 * a : P, CHUNK * c + lo : CHUNK * c + hi],
+                start=start,
+                stop=stop,
+            )
+
+        def products(b, c, s, a):
+            if a == 0:
+                banks[b, c, s] = next_bank()[:].rearrange("p (t c) -> p t c", t=PACK)
+            for t in range(PACK):
+                first, last = (a == 0 and t == 0), (a == KP - 1 and t == PACK - 1)
+                first_pass(banks[b, c, s][:, t, :], b, t, a, c, STEP * s, STEP * (s + 1), first, last)
+
+        def magnitude(b, c, s, at=None):
+            if (b, c, s) not in banks:
+                products(b, c, s, 0)
+            products(b, c, s, 1)
+            if at is None:
+                mag = ring.tile([P, BANK], F32, name="mag", bufs=4)
+            else:
+                mag = placed([P, BANK], F32, f"mag{b}{c}{s}", at)
+            mags[b, c, s] = mag[:].rearrange("p (t c) -> p t c", t=PACK)
+            for t in range(PACK):
+                nc.scalar.activation(
+                    mags[b, c, s][:, t, :], banks[b, c, s][:, t, :], ACT.Abs, scale=cd_sb[:, b, t : t + 1]
+                )
+
+        def h_tile(b, c):
+            if (b, c) not in h_bf:
+                h_bf[b, c] = kept([P, PACK * CHUNK], BF16, f"h_bf{b}{c}")
+            return h_bf[b, c]
+
+        def multiply(b, c, s):
+            dst = h_tile(b, c)[:, PACK * STEP * s : PACK * STEP * (s + 1)]
+            nc.vector.tensor_tensor(
+                dst.rearrange("p (c i t) -> p c t i", i=WALK, t=PACK),
+                banks[b, c, s].rearrange("p t (c i) -> p c t i", i=WALK),
+                mags[b, c, s].rearrange("p t (c i) -> p c t i", i=WALK),
+                MULT,
+            )
+
+        def sign_bank(b, c, u, squares_at=None):
+            if u == 0:
+                if squares_at is None:
+                    squares = ring.tile([P, 2, CHUNK, 2], BF16, name="squares", bufs=3)
+                else:
+                    squares = placed([P, 2, CHUNK, 2], BF16, f"squares{b}{c}", squares_at)
+                factors[b, c] = (squares, ring.tile([P, 2, CHUNK, 2], BF16, name="signs", bufs=3))
+            squares, signs = factors[b, c]
             bank = next_bank()[:].rearrange("p (e c) -> p e c", e=2)
             for e in range(2):
-                wcols = slice(P * (2 * u + e), P * (2 * u + e + 1))
                 for a in range(KP):
-                    nc.tensor.matmul_mx(
-                        bank[:, e, :],
-                        lhsT=w1_w[b, a][:, wcols].bitcast(FP8X4),
-                        lhsT_scale=w1_s[b, a][:, wcols],
-                        rhs=(v_late[:] if (a, q) == (1, 3) else v_w[g][a][:, cols]).bitcast(FP8X4),
-                        rhs_scale=v_s[g][4 * a : P, cols],
-                        start=(a == 0),
-                        stop=(a == KP - 1),
-                    )
+                    first_pass(bank[:, e, :], b, 2 * u + e, a, c, 0, CHUNK, a == 0, a == KP - 1)
             for e in range(2):
                 t = 2 * u + e
                 nc.scalar.activation(squares[:, u, :, e], bank[:, e, :], ACT.Square, scale=cd_root[:, b, t : t + 1])
@@ -240,141 +235,135 @@ def tile_list_contact_drag_store_kernel(
                 ACT.Sign,
             )
 
-        def sign_product(b, q):
-            g, s = divmod(q, 2)
-            squares, signs = factors[b, q]
-            dst = h_tile(b, g)[:, PACK * QUARTER * s : PACK * QUARTER * (s + 1)]
+        def sign_product(b, c):
+            squares, signs = factors[b, c]
             nc.vector.tensor_tensor(
-                dst.rearrange("p (c u e) -> p c u e", u=2, e=2),
+                h_tile(b, c)[:].rearrange("p (c u e) -> p c u e", u=2, e=2),
                 squares[:].rearrange("p u c e -> p c u e"),
                 signs[:].rearrange("p u c e -> p c u e"),
                 MULT,
             )
 
-        def quantise_h(b, g, lo=0, hi=HALF):
-            if (b, g) not in h_w:
-                if (b, g) == (0, 1):
-                    h_w[b, g] = over_piece([P, HALF], U32, "h_w01", late_piece, 4 * QUARTER)
-                else:
-                    h_w[b, g] = kept([P, HALF], U32, f"h_w{b}{g}")
-                h_s[b, g] = kept([P, HALF], U8, f"h_s{b}{g}")
-            nc.vector.quantize_mx(
-                h_w[b, g][:, lo:hi].bitcast(FP8X4), h_s[b, g][:, lo:hi], h_bf[b, g][:, PACK * lo : PACK * hi]
-            )
+        def quantise_h(b, c, at=None):
+            if at is None:
+                h_w[b, c] = kept([P, CHUNK], U32, f"h_w{b}{c}")
+            else:
+                h_w[b, c] = placed([P, CHUNK], U32, f"h_w{b}{c}", at)
+            h_s[b, c] = kept([P, CHUNK], U8, f"h_s{b}{c}")
+            nc.vector.quantize_mx(h_w[b, c][:].bitcast(FP8X4), h_s[b, c][:], h_bf[b, c][:])
 
-        def quantise_quarter(b, q):
-            g, s = divmod(q, 2)
-            quantise_h(b, g, QUARTER * s, QUARTER * (s + 1))
-
-        def negate(n, lo, hi):
-            g, first = divmod(lo, HALF)
+        def deliver(n, c, count=1, at=None):
             y_bank = next_bank()
-            width = HALF if hi - lo == HALF else TOK
-            passes = [(b, c) for b in range(HP) for c in range(0, hi - lo, width)]
-            for b, c in passes:
-                cols = slice(first + c, first + c + width)
+            passes = [(b, i) for b in range(HP) for i in range(count)]
+            for b, i in passes:
                 nc.tensor.matmul_mx(
-                    y_bank[:, c : c + width],
+                    y_bank[:, CHUNK * i : CHUNK * (i + 1)],
                     lhsT=w4_w[:, b, 2 * P * n : 2 * P * (n + 1)].bitcast(FP4X4),
                     lhsT_scale=w4_s[:, b, P * n : P * (n + 1)],
-                    rhs=h_w[b, g][:, cols].bitcast(FP8X4),
-                    rhs_scale=h_s[b, g][:, cols],
-                    start=((b, c) == passes[0]),
-                    stop=((b, c) == passes[-1]),
+                    rhs=h_w[b, c + i][:].bitcast(FP8X4),
+                    rhs_scale=h_s[b, c + i][:],
+                    start=((b, i) == passes[0]),
+                    stop=((b, i) == passes[-1]),
                 )
-            nc.scalar.activation(forces[n][:, lo:hi], y_bank[:, 0 : hi - lo], ACT.Copy, scale=-1.0)
-
-        def scatter(n, lo, hi):
-            places = entries(place, lo, hi)
-            nc.vector.tensor_tensor(pages[n][:].indirect(places), forces[n][:, lo:hi], wgo_sb[:, lo:hi], MULT)
-            if hi == S:
+            width = CHUNK * count
+            if at is None:
+                force = kept([P, width], F32, f"force{n}{c}")
+            else:
+                force = placed([P, width], F32, f"force{n}{c}", at)
+            forces[n, c] = force
+            nc.scalar.activation(force[:], y_bank[:, 0:width], ACT.Copy, scale=-1.0)
+            weights = wgo_sb[:, CHUNK * c : CHUNK * c + width]
+            nc.vector.tensor_tensor(pages[n][:].indirect(entries(place, c, count)), force[:], weights, MULT)
+            if c + count == CHUNKS:
                 nc.sync.dma_start(out[P * n : P * (n + 1), :], pages[n][:])
 
-        def deliver(n, q, count=1):
-            negate(n, QUARTER * q, QUARTER * (q + count))
-            scatter(n, QUARTER * q, QUARTER * (q + count))
+        nc.scalar.activation(cd_root[:], cd_sb, ACT.Sqrt)
 
-        def sign_unit(b, q, between, after=None):
-            factors[b, q] = (
-                ring.tile([P, 2, QUARTER, 2], BF16, name="squares", bufs=3),
-                ring.tile([P, 2, QUARTER, 2], BF16, name="signs", bufs=3),
-            )
+        head = [kept([P, PACK * PASS], BF16, f"w1_head{a}") for a in range(KP)]
+        for a in range(KP):
             for u in range(2):
-                sign_bank(b, q, u)
-            sign_product(b, q)
-            deliver(*between)
-            quantise_quarter(b, q)
+                round_on_scalar(0, a, u, head[a][:, PACK * PAIR * u : PACK * PAIR * (u + 1)])
+        gather_first(0, 2)
+        gather_scales(0, 2)
+        nc.vector.quantize_mx(w1_w[0, 0][:].bitcast(FP8X4), w1_s[0, 0][:], head[0][:])
+        for c in range(2):
+            for s in range(2):
+                products(0, c, s, 0)
+        gather_first(2, 2)
+        gather_scales(2, 2)
+        nc.vector.quantize_mx(w1_w[0, 1][:].bitcast(FP8X4), w1_s[0, 1][:], head[1][:])
+        for c in range(CHUNKS):
+            gather_second(c, kept([P, CHUNK], U32, f"v_second{c}"))
+
+        def drag(b, c, s, at=None):
+            magnitude(b, c, s, at)
+            multiply(b, c, s)
+
+        def round_shared(b, a):
+            stage = kept([P, PACK * PASS], BF16, f"w1_bf{b}{a}")
+            round_on_vector(b, a, 1, stage[:, PACK * PAIR : 2 * PACK * PAIR])
+            round_on_scalar(b, a, 0, stage[:, 0 : PACK * PAIR])
+            return stage
+
+        def quantise_whole(b, a, stage):
+            nc.vector.quantize_mx(w1_w[b, a][:].bitcast(FP8X4), w1_s[b, a][:], stage[:])
+
+        last, spare = piece_at(2, 1), piece_at(0, 0)
+        new_w1(1, 0)
+        magnitude(0, 0, 0)
+        magnitude(0, 0, 1)
+        stage = round_shared(1, 0)
+        multiply(0, 0, 0)
+        multiply(0, 0, 1)
+        quantise_whole(1, 0, stage)
+        drag(0, 1, 0)
+        drag(0, 1, 1)
+        stage = round_shared(1, 1)
+        magnitude(0, 2, 0)
+        quantise_h(0, 0)
+        quantise_whole(1, 1, stage)
+        stage = round_shared(2, 0)
+        multiply(0, 2, 0)
+        magnitude(0, 2, 1)
+        quantise_whole(2, 0, stage)
+        multiply(0, 2, 1)
+        stage = round_shared(2, 1)
+        quantise_h(0, 1, at=last + 2 * MAG_BYTES)
+        quantise_whole(2, 1, stage)
+        drag(1, 0, 0, at=last)
+        drag(1, 0, 1, at=last + MAG_BYTES)
+        sign_bank(1, 1, 0)
+        quantise_h(1, 0)
+        for s in range(2):
+            products(2, 0, s, 0)
+        drag(2, 0, 0)
+        drag(2, 0, 1, at=spare)
+        quantise_h(0, 2, at=spare)
+        quantise_h(2, 0)
+        drag(2, 1, 0)
+        drag(2, 1, 1)
+        sign_bank(1, 1, 1)
+        quantise_h(2, 1)
+        sign_product(1, 1)
+        deliver(0, 0)
+        quantise_h(1, 1)
+        deliver(1, 0)
+        deliver(2, 0)
+
+        def unit(b, c, behind, after=None):
+            for u in range(2):
+                sign_bank(b, c, u)
+            sign_product(b, c)
+            deliver(*behind)
+            quantise_h(b, c)
             if after is not None:
                 deliver(*after)
 
-        for a in range(KP):
-            for pair in range(2):
-                round_w1(0, a, pair, nc.scalar.copy)
-        gather_words(0, 0)
-        gather_scales(0)
-        quantise_w1(0, 0)
-        for s in range(HALF // TOK):
-            product(0, 0, s, 0)
-        gather_words(1, 0)
-        gather_scales(1)
-        quantise_w1(0, 1)
-        gather_words(0, 1, 0, QUARTER)
-        gather_words(0, 1, QUARTER, HALF)
-        gather_words(1, 1, 0, QUARTER)
-        nc.vector.reciprocal(inverse[:], guess[:])
-
-        drag(0, 0, 0)
-        nc.vector.scalar_tensor_tensor(quotient[:], cd_sb, 0.5, inverse[:], MULT, MULT)
-        drag(0, 0, 1)
-        nc.vector.scalar_tensor_tensor(cd_root[:], guess[:], 0.5, quotient[:], MULT, ADD)
-        magnitude(0, 0, 2)
-        round_shared(1, 0)
-        multiply(0, 0, 2)
-        magnitude(0, 0, 3)
-        quantise_w1(1, 0)
-        multiply(0, 0, 3)
-        magnitude(0, 1, 0)
-        round_shared(1, 1)
-        quantise_h(0, 0)
-        magnitude(0, 1, 1)
-        quantise_w1(1, 1)
-        multiply(0, 1, 0)
-
-        magnitude(1, 0, 0)
-        round_shared(2, 0)
-        multiply(0, 1, 1)
-        multiply(1, 0, 0)
-        magnitude(1, 0, 1)
-        quantise_w1(2, 0)
-        multiply(1, 0, 1)
-        magnitude(1, 0, 2)
-        round_shared(2, 1)
-        multiply(1, 0, 2)
-        magnitude(1, 0, 3)
-        quantise_w1(2, 1)
-        multiply(1, 0, 3)
-        quantise_h(1, 0)
-
-        v_late = over_piece([P, QUARTER], U32, "v_late", late_piece)
-        nc.vector.tensor_copy(v_late[:], tab_w[1][:].bitcast(U32).indirect(entries(pick, S - QUARTER, S)))
-        drag(2, 0, 0)
-        quantise_quarter(0, 2)
-        drag(2, 0, 1)
-        quantise_quarter(2, 0)
-        drag(2, 0, 2)
-        negate(0, 0, QUARTER)
-        drag(2, 0, 3)
-        scatter(0, 0, QUARTER)
-        quantise_quarter(2, 1)
-        deliver(1, 0)
-
-        sign_unit(1, 2, between=(0, 1), after=(2, 0, 2))
-        sign_unit(2, 2, between=(1, 1))
-        sign_unit(0, 3, between=(3, 0))
-        sign_unit(1, 3, between=(3, 1))
-        sign_unit(2, 3, between=(0, 2), after=(1, 2))
-
-        for n in range(NT // 2):
+        unit(1, 2, behind=(3, 0), after=(0, 1))
+        unit(2, 2, behind=(1, 1), after=(2, 1))
+        unit(0, 3, behind=(3, 1))
+        unit(1, 3, behind=(0, 2))
+        unit(2, 3, behind=(1, 2), after=(2, 2))
+        for n in range(NT - 1):
             deliver(n, 3)
-        for n in range(NT // 2, NT):
-            deliver(n, 2, 2)
+        deliver(NT - 1, 2, 2)

@@ -34,7 +34,6 @@ QUADRANT = 32
 PAIR = 2 * P
 WALK = 4
 SCALES_AHEAD = 3
-PIECE_BYTES = 4 * PACK * PASS
 MAG_BYTES = 4 * BANK
 WORDS_BYTES = 4 * CHUNK
 
@@ -55,14 +54,13 @@ def tile_list_contact_drag_store_kernel(
         def placed(shape, dtype, name, offset):
             return shared.tile(shape, dtype, name=name, align_bytes=64, offset=offset)
 
-        def piece_at(b, a):
-            return PIECE_BYTES * (KP * b + a)
-
         pick = keep.tile([P, S // GROUP], U16, name="pick")
         place = keep.tile([P, S // GROUP], U16, name="place")
         tab_w = [kept([P, T], I32, f"tab_w{a}") for a in range(KP)]
         tab_s = kept([P, T], U8, "tab_s")
-        w1_raw = [[placed([P, PACK, PASS], F32, f"w1_raw{b}{a}", piece_at(b, a)) for a in range(KP)] for b in range(HP)]
+        loads = [(0, 0, PASS), (1, 0, PASS), (0, PASS, 2 * PASS), (1, PASS, PASS + PAIR), (1, H - PAIR, PAIR)]
+        starts = [sum(4 * PACK * width for a, first, width in loads[:i]) for i in range(len(loads))]
+        w1_raw = [placed([P, PACK, width], F32, f"w1_raw{i}", starts[i]) for i, (a, first, width) in enumerate(loads)]
         cd_padded = kept([P, HP, 2 * PACK], F32, "cd_padded")
         cd_sb = cd_padded[:, :, 0:PACK]
         cd_root = kept([P, HP, PACK], F32, "cd_root")
@@ -77,26 +75,30 @@ def tile_list_contact_drag_store_kernel(
             nc.vector.memset(page[:].bitcast(I32), 0)
         nc.vector.memset(w4_s[:].bitcast(I32), 0)
 
-        def load_w1(b, a):
-            rows = w1[PASS * a : PASS * (a + 1), PASS * b : PASS * (b + 1)]
-            nc.sync.dma_start(w1_raw[b][a][:], rows.rearrange("(p j) c -> p j c", j=PACK))
+        def load_w1(i):
+            a, first, width = loads[i]
+            rows = w1[PASS * a : PASS * (a + 1), first : first + width]
+            nc.sync.dma_start(w1_raw[i][:], rows.rearrange("(p j) c -> p j c", j=PACK))
+
+        def load_cd(lo, hi):
+            nc.sync.dma_start(cd_sb[:, lo:hi, :], cd[PASS * lo : PASS * hi].rearrange("(b p t) -> p b t", p=P, t=PACK))
 
         def load_tab(a):
             nc.sync.dma_start(tab_w[a][:], tab_words[a].rearrange("p t i -> p (t i)").bitcast(I32))
 
-        load_w1(0, 0)
+        load_w1(0)
         nc.sync.dma_start(pick[:], offs)
         for i in range(4 * KP):
             if i == SCALES_AHEAD:
                 load_tab(0)
             r, a = divmod(i, KP)
             nc.sync.dma_start(tab_s[4 * a + r : P : QUADRANT, :].bitcast(I32), tab_scales[a, r:16:4, :].bitcast(I32))
-        load_w1(0, 1)
+        load_w1(1)
         load_tab(1)
-        nc.sync.dma_start(cd_sb, cd.rearrange("(b p t) -> p b t", p=P, t=PACK))
-        for b in range(1, HP):
-            for a in range(KP):
-                load_w1(b, a)
+        load_cd(0, 1)
+        for i in range(2, len(loads)):
+            load_w1(i)
+        load_cd(1, HP)
         for q in range(P // QUADRANT):
             nc.sync.dma_start(
                 w4_s[QUADRANT * q : QUADRANT * q + 4, :, :].bitcast(I32),
@@ -136,34 +138,26 @@ def tile_list_contact_drag_store_kernel(
         def v_words(a, c, lo, hi):
             return v_first[:, CHUNK * c + lo : CHUNK * c + hi] if a == 0 else v_second[c][:, lo:hi]
 
-        w1_w = {}
-
-        def new_w1(b, a, at=None):
-            name = f"w1_w{b}{a}"
-            w1_w[b, a] = kept([P, PASS], U32, name) if at is None else placed([P, PASS], U32, name, at)
-
-        for b, a in ((0, 0), (0, 1), (1, 1), (2, 0), (2, 1)):
-            new_w1(b, a)
+        w1_w = {(b, a): kept([P, PASS], U32, f"w1_w{b}{a}") for b in range(HP) for a in range(KP)}
         w1_s = {(b, a): kept([P, PASS], U8, f"w1_s{b}{a}") for b in range(HP) for a in range(KP)}
-        rounded = {}
+        stages = {}
 
-        def pair_views(b, a, u, dst):
-            src = w1_raw[b][a][:].rearrange("p j (m t) -> p m t j", t=PACK)[:, :, 2 * u : 2 * u + 2, :]
-            return dst.rearrange("p (e m j) -> p m e j", e=2, j=PACK), src
+        def round_part(engine_copy, b, a, u, lo=0, hi=PASS):
+            if (b, a) not in stages:
+                stages[b, a] = kept([P, PACK * PASS], BF16, f"w1_bf{b}{a}")
+            column = PASS * b + lo
+            i = max(i for i, (at, first, width) in enumerate(loads) if at == a and first <= column)
+            src = w1_raw[i][:, :, column - loads[i][1] : column - loads[i][1] + hi - lo]
+            src = src.rearrange("p j (m t) -> p m j t", t=PACK)[:, :, :, 2 * u : 2 * u + 2]
+            dst = stages[b, a][:].rearrange("p (t m j) -> p m j t", t=PACK, j=PACK)
+            engine_copy(dst[:, lo // PACK : hi // PACK, :, 2 * u : 2 * u + 2], src)
 
-        def round_on_scalar(b, a, u, dst):
-            rounded[b, a, u] = dst
-            to, src = pair_views(b, a, u, dst)
-            nc.scalar.copy(to.rearrange("p m e j -> p m j e"), src.rearrange("p m e j -> p m j e"))
+        def round_shared(b, a, lo=0, hi=PASS):
+            round_part(nc.vector.tensor_copy, b, a, 1, lo, hi)
+            round_part(nc.scalar.copy, b, a, 0, lo, hi)
 
-        def round_on_vector(b, a, u, dst):
-            rounded[b, a, u] = dst
-            to, src = pair_views(b, a, u, dst)
-            nc.vector.tensor_copy(to.rearrange("p m e j -> p m j e"), src.rearrange("p m e j -> p m j e"))
-
-        def quantise_pair(b, a, u):
-            cols = slice(PAIR * u, PAIR * (u + 1))
-            nc.vector.quantize_mx(w1_w[b, a][:, cols].bitcast(FP8X4), w1_s[b, a][:, cols], rounded[b, a, u])
+        def quantise_w1(b, a):
+            nc.vector.quantize_mx(w1_w[b, a][:].bitcast(FP8X4), w1_s[b, a][:], stages[b, a][:])
 
         banks, mags, h_bf, h_w, h_s, factors, forces = {}, {}, {}, {}, {}, {}, {}
 
@@ -277,21 +271,20 @@ def tile_list_contact_drag_store_kernel(
             if c + count == CHUNKS:
                 nc.sync.dma_start(out[P * n : P * (n + 1), :], pages[n][:])
 
-        nc.scalar.activation(cd_root[:], cd_sb, ACT.Sqrt)
+        nc.scalar.activation(cd_root[:, 0:1, :], cd_sb[:, 0:1, :], ACT.Sqrt)
 
-        head = [kept([P, PACK * PASS], BF16, f"w1_head{a}") for a in range(KP)]
         for a in range(KP):
             for u in range(2):
-                round_on_scalar(0, a, u, head[a][:, PACK * PAIR * u : PACK * PAIR * (u + 1)])
+                round_part(nc.scalar.copy, 0, a, u)
         gather_first(0, 2)
         gather_scales(0, 2)
-        nc.vector.quantize_mx(w1_w[0, 0][:].bitcast(FP8X4), w1_s[0, 0][:], head[0][:])
+        quantise_w1(0, 0)
         for c in range(2):
             for s in range(2):
                 products(0, c, s, 0)
         gather_first(2, 2)
         gather_scales(2, 2)
-        nc.vector.quantize_mx(w1_w[0, 1][:].bitcast(FP8X4), w1_s[0, 1][:], head[1][:])
+        quantise_w1(0, 1)
         for c in range(CHUNKS):
             gather_second(c, kept([P, CHUNK], U32, f"v_second{c}"))
 
@@ -299,39 +292,27 @@ def tile_list_contact_drag_store_kernel(
             magnitude(b, c, s, at)
             multiply(b, c, s)
 
-        def round_shared(b, a):
-            stage = kept([P, PACK * PASS], BF16, f"w1_bf{b}{a}")
-            round_on_vector(b, a, 1, stage[:, PACK * PAIR : 2 * PACK * PAIR])
-            round_on_scalar(b, a, 0, stage[:, 0 : PACK * PAIR])
-            return stage
-
-        def quantise_whole(b, a, stage):
-            nc.vector.quantize_mx(w1_w[b, a][:].bitcast(FP8X4), w1_s[b, a][:], stage[:])
-
-        last, spare = piece_at(2, 1), piece_at(0, 0)
-        new_w1(1, 0)
-        magnitude(0, 0, 0)
-        magnitude(0, 0, 1)
-        stage = round_shared(1, 0)
-        multiply(0, 0, 0)
-        multiply(0, 0, 1)
-        quantise_whole(1, 0, stage)
-        drag(0, 1, 0)
-        drag(0, 1, 1)
-        stage = round_shared(1, 1)
-        magnitude(0, 2, 0)
+        spare, earlier, last = starts[0], starts[-2], starts[-1]
+        for c in range(2):
+            for s in range(2):
+                drag(0, c, s)
+        round_shared(1, 0)
+        round_shared(2, 0)
+        quantise_w1(1, 0)
         quantise_h(0, 0)
-        quantise_whole(1, 1, stage)
-        stage = round_shared(2, 0)
-        multiply(0, 2, 0)
+        quantise_w1(2, 0)
+        drag(0, 2, 0)
         magnitude(0, 2, 1)
-        quantise_whole(2, 0, stage)
+        round_shared(1, 1)
         multiply(0, 2, 1)
-        stage = round_shared(2, 1)
-        quantise_h(0, 1, at=last + 2 * MAG_BYTES)
-        quantise_whole(2, 1, stage)
+        round_shared(2, 1, 0, PAIR)
+        quantise_w1(1, 1)
+        round_shared(2, 1, PAIR, PASS)
+        quantise_h(0, 1, at=earlier)
+        quantise_w1(2, 1)
         drag(1, 0, 0, at=last)
         drag(1, 0, 1, at=last + MAG_BYTES)
+        nc.scalar.activation(cd_root[:, 1:HP, :], cd_sb[:, 1:HP, :], ACT.Sqrt)
         sign_bank(1, 1, 0)
         quantise_h(1, 0)
         for s in range(2):

@@ -27,8 +27,8 @@ CHUNKS = S // CHUNK
 STEP = 128
 BANK = 512
 BANKS = 8
-EARLY_BANKS = (0, 1, 2, 3, 4, 5, 6, 7, 6, 0, 1, 2, 3, 0)
-LATE_BANKS = (4, 5, 7, 3)
+EARLY_BANKS = (0, 1, 2, 3, 4, 5, 6, 7, 6, 0, 1, 2, 3, 4, 5, 4, 4, 5, 4)
+LATE_BANKS = (3, 7, 5, 4)
 GROUP = 16
 QUADRANT = 32
 PAIR = 2 * P
@@ -58,7 +58,7 @@ def tile_list_contact_drag_store_kernel(
         place = keep.tile([P, S // GROUP], U16, name="place")
         tab_w = [kept([P, T], I32, f"tab_w{a}") for a in range(KP)]
         tab_s = kept([P, T], U8, "tab_s")
-        loads = [(0, 0, PASS), (1, 0, PASS), (0, PASS, 2 * PASS), (1, PASS, PASS + PAIR), (1, H - PAIR, PAIR)]
+        loads = [(0, 0, PASS), (1, 0, PASS), (0, PASS, PASS), (0, 2 * PASS, PASS), (1, PASS, PASS + PAIR), (1, H - PAIR, PAIR)]
         starts = [sum(4 * PACK * width for a, first, width in loads[:i]) for i in range(len(loads))]
         w1_raw = [placed([P, PACK, width], F32, f"w1_raw{i}", starts[i]) for i, (a, first, width) in enumerate(loads)]
         cd_padded = kept([P, HP, 2 * PACK], F32, "cd_padded")
@@ -142,19 +142,23 @@ def tile_list_contact_drag_store_kernel(
         w1_s = {(b, a): kept([P, PASS], U8, f"w1_s{b}{a}") for b in range(HP) for a in range(KP)}
         stages = {}
 
-        def round_part(engine_copy, b, a, u, lo=0, hi=PASS):
+        def round_part(engine_copy, b, a, slots, lo=0, hi=PASS):
             if (b, a) not in stages:
                 stages[b, a] = kept([P, PACK * PASS], BF16, f"w1_bf{b}{a}")
             column = PASS * b + lo
             i = max(i for i, (at, first, width) in enumerate(loads) if at == a and first <= column)
             src = w1_raw[i][:, :, column - loads[i][1] : column - loads[i][1] + hi - lo]
-            src = src.rearrange("p j (m t) -> p m j t", t=PACK)[:, :, :, 2 * u : 2 * u + 2]
+            src = src.rearrange("p j (m t) -> p m j t", t=PACK)[:, :, :, slots]
             dst = stages[b, a][:].rearrange("p (t m j) -> p m j t", t=PACK, j=PACK)
-            engine_copy(dst[:, lo // PACK : hi // PACK, :, 2 * u : 2 * u + 2], src)
+            engine_copy(dst[:, lo // PACK : hi // PACK, :, slots], src)
 
         def round_shared(b, a, lo=0, hi=PASS):
-            round_part(nc.vector.tensor_copy, b, a, 1, lo, hi)
-            round_part(nc.scalar.copy, b, a, 0, lo, hi)
+            round_part(nc.vector.tensor_copy, b, a, slice(2, 4), lo, hi)
+            round_part(nc.scalar.copy, b, a, slice(0, 2), lo, hi)
+
+        def round_on_vector(b, a, lo=0, hi=PASS):
+            for u in range(2):
+                round_part(nc.vector.tensor_copy, b, a, slice(2 * u, 2 * u + 2), lo, hi)
 
         def quantise_w1(b, a):
             nc.vector.quantize_mx(w1_w[b, a][:].bitcast(FP8X4), w1_s[b, a][:], stages[b, a][:])
@@ -194,9 +198,10 @@ def tile_list_contact_drag_store_kernel(
                     mags[b, c, s][:, t, :], banks[b, c, s][:, t, :], ACT.Abs, scale=cd_sb[:, b, t : t + 1]
                 )
 
-        def h_tile(b, c):
+        def h_tile(b, c, at=None):
             if (b, c) not in h_bf:
-                h_bf[b, c] = kept([P, PACK * CHUNK], BF16, f"h_bf{b}{c}")
+                shape, name = [P, PACK * CHUNK], f"h_bf{b}{c}"
+                h_bf[b, c] = kept(shape, BF16, name) if at is None else placed(shape, BF16, name, at)
             return h_bf[b, c]
 
         def multiply(b, c, s):
@@ -246,8 +251,9 @@ def tile_list_contact_drag_store_kernel(
             h_s[b, c] = kept([P, CHUNK], U8, f"h_s{b}{c}")
             nc.vector.quantize_mx(h_w[b, c][:].bitcast(FP8X4), h_s[b, c][:], h_bf[b, c][:])
 
-        def deliver(n, c, count=1, at=None):
-            y_bank = next_bank()
+        def deliver(n, c, count=1, y_bank=None):
+            if y_bank is None:
+                y_bank = next_bank()
             passes = [(b, i) for b in range(HP) for i in range(count)]
             for b, i in passes:
                 nc.tensor.matmul_mx(
@@ -260,10 +266,7 @@ def tile_list_contact_drag_store_kernel(
                     stop=((b, i) == passes[-1]),
                 )
             width = CHUNK * count
-            if at is None:
-                force = kept([P, width], F32, f"force{n}{c}")
-            else:
-                force = placed([P, width], F32, f"force{n}{c}", at)
+            force = kept([P, width], F32, f"force{n}{c}")
             forces[n, c] = force
             nc.scalar.activation(force[:], y_bank[:, 0:width], ACT.Copy, scale=-1.0)
             weights = wgo_sb[:, CHUNK * c : CHUNK * c + width]
@@ -275,7 +278,7 @@ def tile_list_contact_drag_store_kernel(
 
         for a in range(KP):
             for u in range(2):
-                round_part(nc.scalar.copy, 0, a, u)
+                round_part(nc.scalar.copy, 0, a, slice(2 * u, 2 * u + 2))
         gather_first(0, 2)
         gather_scales(0, 2)
         quantise_w1(0, 0)
@@ -292,26 +295,31 @@ def tile_list_contact_drag_store_kernel(
             magnitude(b, c, s, at)
             multiply(b, c, s)
 
-        spare, earlier, last = starts[0], starts[-2], starts[-1]
-        for c in range(2):
-            for s in range(2):
-                drag(0, c, s)
+        spare, last = starts[0], starts[-1]
+        magnitude(0, 0, 0)
+        magnitude(0, 0, 1)
         round_shared(1, 0)
-        round_shared(2, 0)
-        quantise_w1(1, 0)
+        multiply(0, 0, 0)
+        multiply(0, 0, 1)
         quantise_h(0, 0)
+        round_on_vector(2, 0)
+        quantise_w1(1, 0)
+        drag(0, 1, 0)
         quantise_w1(2, 0)
-        drag(0, 2, 0)
+        drag(0, 1, 1)
+        magnitude(0, 2, 0)
         magnitude(0, 2, 1)
         round_shared(1, 1)
-        multiply(0, 2, 1)
-        round_shared(2, 1, 0, PAIR)
-        quantise_w1(1, 1)
+        round_on_vector(2, 1, 0, PAIR)
         round_shared(2, 1, PAIR, PASS)
-        quantise_h(0, 1, at=earlier)
+        quantise_w1(1, 1)
         quantise_w1(2, 1)
-        drag(1, 0, 0, at=last)
-        drag(1, 0, 1, at=last + MAG_BYTES)
+        h_tile(0, 2, at=last)
+        multiply(0, 2, 0)
+        multiply(0, 2, 1)
+        drag(1, 0, 0)
+        drag(1, 0, 1)
+        quantise_h(0, 1, at=last + MAG_BYTES)
         nc.scalar.activation(cd_root[:, 1:HP, :], cd_sb[:, 1:HP, :], ACT.Sqrt)
         sign_bank(1, 1, 0)
         quantise_h(1, 0)
@@ -323,12 +331,12 @@ def tile_list_contact_drag_store_kernel(
         quantise_h(2, 0)
         drag(2, 1, 0)
         drag(2, 1, 1)
-        sign_bank(1, 1, 1)
         quantise_h(2, 1)
-        sign_product(1, 1)
         deliver(0, 0)
-        quantise_h(1, 1)
         deliver(1, 0)
+        sign_bank(1, 1, 1)
+        sign_product(1, 1)
+        quantise_h(1, 1)
         deliver(2, 0)
 
         def unit(b, c, behind, after=None):
@@ -340,11 +348,20 @@ def tile_list_contact_drag_store_kernel(
             if after is not None:
                 deliver(*after)
 
-        unit(1, 2, behind=(3, 0), after=(0, 1))
+        sign_bank(1, 2, 0)
+        deliver(3, 0)
+        sign_bank(1, 2, 1)
+        sign_product(1, 2)
+        deliver(0, 1)
+        quantise_h(1, 2)
         unit(2, 2, behind=(1, 1), after=(2, 1))
         unit(0, 3, behind=(3, 1))
-        unit(1, 3, behind=(0, 2))
-        unit(2, 3, behind=(1, 2), after=(2, 2))
+        unit(1, 3, behind=(0, 2), after=(1, 2))
+        sign_bank(2, 3, 0)
+        sign_bank(2, 3, 1)
+        sign_product(2, 3)
+        quantise_h(2, 3)
+        deliver(2, 2, y_bank=taken[-1])
         for n in range(NT - 1):
             deliver(n, 3)
         deliver(NT - 1, 2, 2)

@@ -27,8 +27,8 @@ CHUNKS = S // CHUNK
 STEP = 128
 BANK = 512
 BANKS = 8
-EARLY_BANKS = (0, 1, 2, 3, 4, 5, 6, 7, 6, 0, 1, 2, 3, 4, 5, 4, 4, 5, 4)
-LATE_BANKS = (3, 7, 5, 4)
+EARLY_BANKS = (0, 1, 2, 3, 4, 5, 6, 7, 6, 0, 1, 2, 3, 0)
+LATE_BANKS = (4, 5, 7, 3)
 GROUP = 16
 QUADRANT = 32
 PAIR = 2 * P
@@ -58,7 +58,7 @@ def tile_list_contact_drag_store_kernel(
         place = keep.tile([P, S // GROUP], U16, name="place")
         tab_w = [kept([P, T], I32, f"tab_w{a}") for a in range(KP)]
         tab_s = kept([P, T], U8, "tab_s")
-        loads = [(0, 0, PASS), (1, 0, PASS), (0, PASS, PASS), (0, 2 * PASS, PASS), (1, PASS, PASS + PAIR), (1, H - PAIR, PAIR)]
+        loads = [(0, 0, PASS), (1, 0, PASS), (0, PASS, PASS), (1, PASS, PASS), (0, 2 * PASS, PASS), (1, 2 * PASS, PAIR), (1, H - PAIR, PAIR)]
         starts = [sum(4 * PACK * width for a, first, width in loads[:i]) for i in range(len(loads))]
         w1_raw = [placed([P, PACK, width], F32, f"w1_raw{i}", starts[i]) for i, (a, first, width) in enumerate(loads)]
         cd_padded = kept([P, HP, 2 * PACK], F32, "cd_padded")
@@ -295,31 +295,30 @@ def tile_list_contact_drag_store_kernel(
             magnitude(b, c, s, at)
             multiply(b, c, s)
 
-        spare, last = starts[0], starts[-1]
+        spare, earlier, last = starts[0], starts[-2], starts[-1]
         magnitude(0, 0, 0)
         magnitude(0, 0, 1)
         round_shared(1, 0)
         multiply(0, 0, 0)
         multiply(0, 0, 1)
-        quantise_h(0, 0)
-        round_on_vector(2, 0)
         quantise_w1(1, 0)
         drag(0, 1, 0)
-        quantise_w1(2, 0)
-        drag(0, 1, 1)
-        magnitude(0, 2, 0)
-        magnitude(0, 2, 1)
+        magnitude(0, 1, 1)
         round_shared(1, 1)
-        round_on_vector(2, 1, 0, PAIR)
-        round_shared(2, 1, PAIR, PASS)
+        multiply(0, 1, 1)
+        quantise_h(0, 0)
         quantise_w1(1, 1)
-        quantise_w1(2, 1)
-        h_tile(0, 2, at=last)
+        magnitude(0, 2, 0)
+        round_shared(2, 0)
         multiply(0, 2, 0)
-        multiply(0, 2, 1)
-        drag(1, 0, 0)
-        drag(1, 0, 1)
-        quantise_h(0, 1, at=last + MAG_BYTES)
+        round_on_vector(2, 1, 0, PAIR)
+        quantise_w1(2, 0)
+        round_shared(2, 1, PAIR, PASS)
+        quantise_h(0, 1, at=earlier)
+        quantise_w1(2, 1)
+        drag(0, 2, 1, at=last - WORDS_BYTES)
+        drag(1, 0, 0, at=last + WORDS_BYTES)
+        drag(1, 0, 1, at=last + 3 * WORDS_BYTES)
         nc.scalar.activation(cd_root[:, 1:HP, :], cd_sb[:, 1:HP, :], ACT.Sqrt)
         sign_bank(1, 1, 0)
         quantise_h(1, 0)
@@ -331,12 +330,12 @@ def tile_list_contact_drag_store_kernel(
         quantise_h(2, 0)
         drag(2, 1, 0)
         drag(2, 1, 1)
-        quantise_h(2, 1)
-        deliver(0, 0)
-        deliver(1, 0)
         sign_bank(1, 1, 1)
+        quantise_h(2, 1)
         sign_product(1, 1)
+        deliver(0, 0)
         quantise_h(1, 1)
+        deliver(1, 0)
         deliver(2, 0)
 
         def unit(b, c, behind, after=None):
@@ -348,20 +347,11 @@ def tile_list_contact_drag_store_kernel(
             if after is not None:
                 deliver(*after)
 
-        sign_bank(1, 2, 0)
-        deliver(3, 0)
-        sign_bank(1, 2, 1)
-        sign_product(1, 2)
-        deliver(0, 1)
-        quantise_h(1, 2)
+        unit(1, 2, behind=(3, 0), after=(0, 1))
         unit(2, 2, behind=(1, 1), after=(2, 1))
         unit(0, 3, behind=(3, 1))
-        unit(1, 3, behind=(0, 2), after=(1, 2))
-        sign_bank(2, 3, 0)
-        sign_bank(2, 3, 1)
-        sign_product(2, 3)
-        quantise_h(2, 3)
-        deliver(2, 2, y_bank=taken[-1])
+        unit(1, 3, behind=(0, 2))
+        unit(2, 3, behind=(1, 2), after=(2, 2))
         for n in range(NT - 1):
             deliver(n, 3)
         deliver(NT - 1, 2, 2)

@@ -27,8 +27,8 @@ CHUNKS = S // CHUNK
 STEP = 128
 BANK = 512
 BANKS = 8
-EARLY_BANKS = (0, 1, 2, 3, 4, 5, 6, 7, 6, 0, 1, 2, 3, 0)
-LATE_BANKS = (4, 5, 7, 3)
+EARLY_BANKS = (0, 1, 2, 3, 4, 5, 6, 7, 6, 0, 1, 2, 3, 4, 5, 4, 4, 5, 4)
+LATE_BANKS = (3, 7, 5, 4)
 GROUP = 16
 QUADRANT = 32
 PAIR = 2 * P
@@ -131,9 +131,11 @@ def tile_list_contact_drag_store_kernel(
             cols = slice(CHUNK * c, CHUNK * (c + count))
             nc.vector.tensor_copy(v_s[:, cols], tab_s[:].indirect(entries(pick, c, count)))
 
-        def gather_second(c, tile):
-            v_second[c] = tile
-            nc.vector.tensor_copy(tile[:], tab_w[1][:].bitcast(U32).indirect(entries(pick, c)))
+        def gather_second(c, lo=0, hi=CHUNK):
+            if c not in v_second:
+                v_second[c] = kept([P, CHUNK], U32, f"v_second{c}")
+            picked = pick[:, (CHUNK * c + lo) // GROUP : (CHUNK * c + hi) // GROUP]
+            nc.vector.tensor_copy(v_second[c][:, lo:hi], tab_w[1][:].bitcast(U32).indirect(picked))
 
         def v_words(a, c, lo, hi):
             return v_first[:, CHUNK * c + lo : CHUNK * c + hi] if a == 0 else v_second[c][:, lo:hi]
@@ -160,8 +162,9 @@ def tile_list_contact_drag_store_kernel(
             for u in range(2):
                 round_part(nc.vector.tensor_copy, b, a, slice(2 * u, 2 * u + 2), lo, hi)
 
-        def quantise_w1(b, a):
-            nc.vector.quantize_mx(w1_w[b, a][:].bitcast(FP8X4), w1_s[b, a][:], stages[b, a][:])
+        def quantise_w1(b, a, lo=0, hi=PASS):
+            rounded = stages[b, a][:, PACK * lo : PACK * hi]
+            nc.vector.quantize_mx(w1_w[b, a][:, lo:hi].bitcast(FP8X4), w1_s[b, a][:, lo:hi], rounded)
 
         banks, mags, h_bf, h_w, h_s, factors, forces = {}, {}, {}, {}, {}, {}, {}
 
@@ -287,15 +290,17 @@ def tile_list_contact_drag_store_kernel(
                 products(0, c, s, 0)
         gather_first(2, 2)
         gather_scales(2, 2)
+        gather_second(0, 0, STEP)
         quantise_w1(0, 1)
-        for c in range(CHUNKS):
-            gather_second(c, kept([P, CHUNK], U32, f"v_second{c}"))
+        gather_second(0, STEP, CHUNK)
+        for c in range(1, CHUNKS):
+            gather_second(c)
 
         def drag(b, c, s, at=None):
             magnitude(b, c, s, at)
             multiply(b, c, s)
 
-        spare, earlier, last = starts[0], starts[-2], starts[-1]
+        last = starts[-1]
         magnitude(0, 0, 0)
         magnitude(0, 0, 1)
         round_shared(1, 0)
@@ -311,31 +316,33 @@ def tile_list_contact_drag_store_kernel(
         magnitude(0, 2, 0)
         round_shared(2, 0)
         multiply(0, 2, 0)
+        magnitude(0, 2, 1)
         round_on_vector(2, 1, 0, PAIR)
-        quantise_w1(2, 0)
+        multiply(0, 2, 1)
+        drag(1, 0, 0)
         round_shared(2, 1, PAIR, PASS)
-        quantise_h(0, 1, at=earlier)
-        quantise_w1(2, 1)
-        drag(0, 2, 1, at=last - WORDS_BYTES)
-        drag(1, 0, 0, at=last + WORDS_BYTES)
-        drag(1, 0, 1, at=last + 3 * WORDS_BYTES)
+        quantise_w1(2, 0)
+        quantise_w1(2, 1, PAIR, PASS)
+        quantise_w1(2, 1, 0, PAIR)
+        quantise_h(0, 1, at=last)
+        quantise_h(0, 2, at=last + WORDS_BYTES)
+        drag(1, 0, 1, at=last + MAG_BYTES)
         nc.scalar.activation(cd_root[:, 1:HP, :], cd_sb[:, 1:HP, :], ACT.Sqrt)
         sign_bank(1, 1, 0)
         quantise_h(1, 0)
         for s in range(2):
             products(2, 0, s, 0)
         drag(2, 0, 0)
-        drag(2, 0, 1, at=spare)
-        quantise_h(0, 2, at=spare)
+        drag(2, 0, 1)
         quantise_h(2, 0)
         drag(2, 1, 0)
         drag(2, 1, 1)
-        sign_bank(1, 1, 1)
         quantise_h(2, 1)
-        sign_product(1, 1)
         deliver(0, 0)
-        quantise_h(1, 1)
         deliver(1, 0)
+        sign_bank(1, 1, 1)
+        sign_product(1, 1)
+        quantise_h(1, 1)
         deliver(2, 0)
 
         def unit(b, c, behind, after=None):
@@ -347,7 +354,12 @@ def tile_list_contact_drag_store_kernel(
             if after is not None:
                 deliver(*after)
 
-        unit(1, 2, behind=(3, 0), after=(0, 1))
+        sign_bank(1, 2, 0)
+        deliver(3, 0)
+        sign_bank(1, 2, 1)
+        sign_product(1, 2)
+        deliver(0, 1)
+        quantise_h(1, 2)
         unit(2, 2, behind=(1, 1), after=(2, 1))
         unit(0, 3, behind=(3, 1))
         unit(1, 3, behind=(0, 2))

@@ -48,16 +48,16 @@ def tile_list_contact_drag_store_kernel(
         ring = ctx.enter_context(tc.tile_pool(name="ring", bufs=4))
         psum = ctx.enter_context(tc.psum_pool(name="psum", bufs=1))
 
-        def kept(shape, dtype, name):
-            return keep.tile(shape, dtype, name=name, align_bytes=64)
+        def kept(shape, dtype, name, align=64):
+            return keep.tile(shape, dtype, name=name, align_bytes=align)
 
         def placed(shape, dtype, name, offset):
-            return shared.tile(shape, dtype, name=name, align_bytes=64, offset=offset)
+            return shared.tile(shape, dtype, name=name, align_bytes=256, offset=offset)
 
         pick = keep.tile([P, S // GROUP], U16, name="pick")
         place = keep.tile([P, S // GROUP], U16, name="place")
-        tab_w = [kept([P, T], I32, f"tab_w{a}") for a in range(KP)]
-        tab_s = kept([P, T], U8, "tab_s")
+        tab_w = [kept([P, T], I32, f"tab_w{a}", 256) for a in range(KP)]
+        tab_s = kept([P, T], U8, "tab_s", 256)
         loads = [(0, 0, PASS), (1, 0, PASS), (0, PASS, PASS), (1, PASS, PASS), (0, 2 * PASS, PASS), (1, 2 * PASS, PAIR), (1, H - PAIR, PAIR)]
         starts = [sum(4 * PACK * width for a, first, width in loads[:i]) for i in range(len(loads))]
         w1_raw = [placed([P, PACK, width], F32, f"w1_raw{i}", starts[i]) for i, (a, first, width) in enumerate(loads)]
@@ -65,10 +65,10 @@ def tile_list_contact_drag_store_kernel(
         cd_sb = cd_padded[:, :, 0:PACK]
         cd_root = kept([P, HP, PACK], F32, "cd_root")
         psum_banks = [psum.tile([P, BANK], F32, name=f"bank{i}") for i in range(BANKS)]
-        w4_w = kept([P, HP, 2 * N], U8, "w4_w")
+        w4_w = kept([P, HP, 2 * N], U8, "w4_w", 256)
         w4_s = kept([P, HP, N], U8, "w4_s")
-        wgo_sb = kept([P, S], F32, "wgo_sb")
-        pages = [kept([P, T2], F32, f"page{n}") for n in range(NT)]
+        wgo_sb = kept([P, S], F32, "wgo_sb", 256)
+        pages = [kept([P, T2], F32, f"page{n}", 256) for n in range(NT)]
 
         nc.vector.memset(tab_s[:].bitcast(I32), 0)
         for page in pages:
@@ -274,8 +274,11 @@ def tile_list_contact_drag_store_kernel(
             nc.scalar.activation(force[:], y_bank[:, 0:width], ACT.Copy, scale=-1.0)
             weights = wgo_sb[:, CHUNK * c : CHUNK * c + width]
             nc.vector.tensor_tensor(pages[n][:].indirect(entries(place, c, count)), force[:], weights, MULT)
-            if c + count == CHUNKS:
+            if c + count == CHUNKS and n < NT - 1:
                 nc.sync.dma_start(out[P * n : P * (n + 1), :], pages[n][:])
+            elif c + count == CHUNKS:
+                for queue, cols in ((nc.sync, slice(0, T2 // 2)), (nc.scalar, slice(T2 // 2, T2))):
+                    queue.dma_start(out[P * n : P * (n + 1), cols], pages[n][:, cols])
 
         nc.scalar.activation(cd_root[:, 0:1, :], cd_sb[:, 0:1, :], ACT.Sqrt)
 

@@ -86,11 +86,11 @@ def tile_list_contact_drag_store_kernel(
         def load_tab(a):
             nc.sync.dma_start(tab_w[a][:], tab_words[a].rearrange("p t i -> p (t i)").bitcast(I32))
 
-        load_w1(0)
+        load_tab(0)
         nc.sync.dma_start(pick[:], offs)
         for i in range(4 * KP):
             if i == SCALES_AHEAD:
-                load_tab(0)
+                load_w1(0)
             r, a = divmod(i, KP)
             nc.sync.dma_start(tab_s[4 * a + r : P : QUADRANT, :].bitcast(I32), tab_scales[a, r:16:4, :].bitcast(I32))
         load_w1(1)
@@ -143,10 +143,12 @@ def tile_list_contact_drag_store_kernel(
         w1_w = {(b, a): kept([P, PASS], U32, f"w1_w{b}{a}") for b in range(HP) for a in range(KP)}
         w1_s = {(b, a): kept([P, PASS], U8, f"w1_s{b}{a}") for b in range(HP) for a in range(KP)}
         stages = {}
+        held_at = starts[-1] + 4 * PACK * PAIR
 
         def round_part(engine_copy, b, a, slots, lo=0, hi=PASS):
             if (b, a) not in stages:
-                stages[b, a] = kept([P, PACK * PASS], BF16, f"w1_bf{b}{a}")
+                shape, name = [P, PACK * PASS], f"w1_bf{b}{a}"
+                stages[b, a] = placed(shape, BF16, name, held_at) if (b, a) == (1, 0) else kept(shape, BF16, name)
             column = PASS * b + lo
             i = max(i for i, (at, first, width) in enumerate(loads) if at == a and first <= column)
             src = w1_raw[i][:, :, column - loads[i][1] : column - loads[i][1] + hi - lo]
@@ -282,19 +284,17 @@ def tile_list_contact_drag_store_kernel(
 
         nc.scalar.activation(cd_root[:, 0:1, :], cd_sb[:, 0:1, :], ACT.Sqrt)
 
-        for a in range(KP):
-            for u in range(2):
-                round_part(nc.scalar.copy, 0, a, slice(2 * u, 2 * u + 2))
-        gather_first(0, 2)
-        gather_scales(0, 2)
+        for u in range(2):
+            round_part(nc.scalar.copy, 0, 0, slice(2 * u, 2 * u + 2))
+        gather_first(0, CHUNKS)
+        gather_scales(0, CHUNKS)
+        round_shared(0, 1)
         quantise_w1(0, 0)
         for c in range(2):
             for s in range(2):
                 products(0, c, s, 0)
-        gather_first(2, 2)
-        gather_scales(2, 2)
-        gather_second(0, 0, STEP)
         quantise_w1(0, 1)
+        gather_second(0, 0, STEP)
         gather_second(0, STEP, CHUNK)
         for c in range(1, CHUNKS):
             gather_second(c)
@@ -304,11 +304,11 @@ def tile_list_contact_drag_store_kernel(
             multiply(b, c, s)
 
         last = starts[-1]
-        magnitude(0, 0, 0)
+        magnitude(0, 0, 0, at=held_at)
         magnitude(0, 0, 1)
-        round_shared(1, 0)
         multiply(0, 0, 0)
         multiply(0, 0, 1)
+        round_shared(1, 0)
         quantise_w1(1, 0)
         drag(0, 1, 0)
         magnitude(0, 1, 1)

@@ -27,7 +27,7 @@ CHUNKS = S // CHUNK
 STEP = 128
 BANK = 512
 BANKS = 8
-EARLY_BANKS = (0, 1, 2, 3, 4, 5, 6, 7, 6, 0, 1, 2, 3, 4, 5, 4, 4, 5, 4)
+EARLY_BANKS = (0, 1, 2, 3, 4, 5, 6, 7, 0, 1, 2, 3, 4, 0, 5, 4, 4, 5, 4)
 LATE_BANKS = (3, 7, 5, 4)
 GROUP = 16
 QUADRANT = 32
@@ -57,23 +57,24 @@ def tile_list_contact_drag_store_kernel(
         pick = keep.tile([P, S // GROUP], U16, name="pick")
         place = keep.tile([P, S // GROUP], U16, name="place")
         tab_w = [kept([P, T], I32, f"tab_w{a}", 256) for a in range(KP)]
-        tab_s = kept([P, T], U8, "tab_s", 256)
         loads = [(0, 0, PASS), (1, 0, PASS), (0, PASS, PASS), (1, PASS, PASS), (0, 2 * PASS, PASS), (1, 2 * PASS, PAIR), (1, H - PAIR, PAIR)]
         starts = [sum(4 * PACK * width for a, first, width in loads[:i]) for i in range(len(loads))]
         w1_raw = [placed([P, PACK, width], F32, f"w1_raw{i}", starts[i]) for i, (a, first, width) in enumerate(loads)]
+        held_at = starts[-1] + 4 * PACK * PAIR
+        scales_at = held_at + 2 * PACK * PASS
+        tab_s = placed([P, T], U8, "tab_s", scales_at)
         cd_padded = kept([P, HP, 2 * PACK], F32, "cd_padded")
         cd_sb = cd_padded[:, :, 0:PACK]
         cd_root = kept([P, HP, PACK], F32, "cd_root")
         psum_banks = [psum.tile([P, BANK], F32, name=f"bank{i}") for i in range(BANKS)]
         w4_w = kept([P, HP, 2 * N], U8, "w4_w", 256)
-        w4_s = kept([P, HP, N], U8, "w4_s")
+        w4_s = placed([P, HP, N], U8, "w4_s", scales_at)
         wgo_sb = kept([P, S], F32, "wgo_sb", 256)
         pages = [kept([P, T2], F32, f"page{n}", 256) for n in range(NT)]
 
-        nc.vector.memset(tab_s[:].bitcast(I32), 0)
+        nc.gpsimd.memset(tab_s[:].bitcast(I32), 0)
         for page in pages:
             nc.vector.memset(page[:].bitcast(I32), 0)
-        nc.vector.memset(w4_s[:].bitcast(I32), 0)
 
         def load_w1(i):
             a, first, width = loads[i]
@@ -99,14 +100,16 @@ def tile_list_contact_drag_store_kernel(
         for i in range(2, len(loads)):
             load_w1(i)
         load_cd(1, HP)
-        for q in range(P // QUADRANT):
-            nc.sync.dma_start(
-                w4_s[QUADRANT * q : QUADRANT * q + 4, :, :].bitcast(I32),
-                w4_scales[:, 4 * q : 4 * q + 4, :].rearrange("a r n -> r a n").bitcast(I32),
-            )
-        nc.sync.dma_start(w4_w[:].bitcast(I32), w4_words.rearrange("a p c -> p a c").bitcast(I32))
-        nc.sync.dma_start(place[:], offs2)
-        nc.sync.dma_start(wgo_sb[:], wgo)
+
+        def load_rest():
+            for q in range(P // QUADRANT):
+                nc.sync.dma_start(
+                    w4_s[QUADRANT * q : QUADRANT * q + 4, :, :].bitcast(I32),
+                    w4_scales[:, 4 * q : 4 * q + 4, :].rearrange("a r n -> r a n").bitcast(I32),
+                )
+            nc.sync.dma_start(w4_w[:].bitcast(I32), w4_words.rearrange("a p c -> p a c").bitcast(I32))
+            nc.sync.dma_start(place[:], offs2)
+            nc.sync.dma_start(wgo_sb[:], wgo)
 
         taken = []
 
@@ -143,7 +146,6 @@ def tile_list_contact_drag_store_kernel(
         w1_w = {(b, a): kept([P, PASS], U32, f"w1_w{b}{a}") for b in range(HP) for a in range(KP)}
         w1_s = {(b, a): kept([P, PASS], U8, f"w1_s{b}{a}") for b in range(HP) for a in range(KP)}
         stages = {}
-        held_at = starts[-1] + 4 * PACK * PAIR
 
         def round_part(engine_copy, b, a, slots, lo=0, hi=PASS):
             if (b, a) not in stages:
@@ -288,6 +290,7 @@ def tile_list_contact_drag_store_kernel(
             round_part(nc.scalar.copy, 0, 0, slice(2 * u, 2 * u + 2))
         gather_first(0, CHUNKS)
         gather_scales(0, CHUNKS)
+        load_rest()
         round_shared(0, 1)
         quantise_w1(0, 0)
         for c in range(2):
@@ -331,7 +334,6 @@ def tile_list_contact_drag_store_kernel(
         quantise_h(0, 2, at=last + WORDS_BYTES)
         drag(1, 0, 1, at=last + MAG_BYTES)
         nc.scalar.activation(cd_root[:, 1:HP, :], cd_sb[:, 1:HP, :], ACT.Sqrt)
-        sign_bank(1, 1, 0)
         quantise_h(1, 0)
         for s in range(2):
             products(2, 0, s, 0)
@@ -342,6 +344,7 @@ def tile_list_contact_drag_store_kernel(
         drag(2, 1, 1)
         quantise_h(2, 1)
         deliver(0, 0)
+        sign_bank(1, 1, 0)
         deliver(1, 0)
         sign_bank(1, 1, 1)
         sign_product(1, 1)

from contextlib import ExitStack

import concourse.mybir as mybir

K, H, N, T, S, T2 = 1024, 1536, 512, 2048, 1024, 2048
FLOPS = 2 * S * H * (K + N)

F32 = mybir.dt.float32
BF16 = mybir.dt.bfloat16
I32 = mybir.dt.int32
U32 = mybir.dt.uint32
U16 = mybir.dt.uint16
U8 = mybir.dt.uint8
FP8X4 = mybir.dt.float8_e4m3fn_x4
FP4X4 = mybir.dt.float4_e2m1fn_x4
ACT = mybir.ActivationFunctionType
MULT = mybir.AluOpType.mult

P = 128
PACK = 4
PASS = P * PACK
KP = K // PASS
HP = H // PASS
NT = N // P
CHUNK = 256
CHUNKS = S // CHUNK
STEP = 128
BANK = 512
BANKS = 8
EARLY_BANKS = (0, 1, 2, 3, 4, 5, 6, 7, 0, 1, 2, 3, 4, 0, 5, 4, 4, 5, 4)
LATE_BANKS = (3, 7, 5, 4)
GROUP = 16
QUADRANT = 32
PAIR = 2 * P
WALK = 4
SCALES_AHEAD = 3
MAG_BYTES = 4 * BANK
WORDS_BYTES = 4 * CHUNK


def tile_list_contact_drag_store_kernel(
    tc, tab_words, tab_scales, offs, w1, cd, w4_words, w4_scales, offs2, wgo, out
):
    nc = tc.nc
    with ExitStack() as ctx:
        keep = ctx.enter_context(tc.tile_pool(name="keep", bufs=1))
        shared = ctx.enter_context(tc.tile_pool(name="shared", bufs=1))
        ring = ctx.enter_context(tc.tile_pool(name="ring", bufs=4))
        psum = ctx.enter_context(tc.psum_pool(name="psum", bufs=1))

        def kept(shape, dtype, name, align=64):
            return keep.tile(shape, dtype, name=name, align_bytes=align)

        def placed(shape, dtype, name, offset):
            return shared.tile(shape, dtype, name=name, align_bytes=256, offset=offset)

        pick = keep.tile([P, S // GROUP], U16, name="pick")
        place = keep.tile([P, S // GROUP], U16, name="place")
        tab_w = [kept([P, T], I32, f"tab_w{a}", 256) for a in range(KP)]
        loads = [(0, 0, PASS), (1, 0, PASS), (0, PASS, PASS), (1, PASS, PASS), (0, 2 * PASS, PASS), (1, 2 * PASS, PAIR), (1, H - PAIR, PAIR)]
        starts = [sum(4 * PACK * width for a, first, width in loads[:i]) for i in range(len(loads))]
        w1_raw = [placed([P, PACK, width], F32, f"w1_raw{i}", starts[i]) for i, (a, first, width) in enumerate(loads)]
        held_at = starts[-1] + 4 * PACK * PAIR
        scales_at = held_at + 2 * PACK * PASS
        tab_s = placed([P, T], U8, "tab_s", scales_at)
        cd_padded = kept([P, HP, 2 * PACK], F32, "cd_padded")
        cd_sb = cd_padded[:, :, 0:PACK]
        cd_root = kept([P, HP, PACK], F32, "cd_root")
        psum_banks = [psum.tile([P, BANK], F32, name=f"bank{i}") for i in range(BANKS)]
        w4_w = kept([P, HP, 2 * N], U8, "w4_w", 256)
        w4_s = placed([P, HP, N], U8, "w4_s", scales_at)
        wgo_sb = kept([P, S], F32, "wgo_sb", 256)
        pages = [kept([P, T2], F32, f"page{n}", 256) for n in range(NT)]

        nc.gpsimd.memset(tab_s[:].bitcast(I32), 0)
        for page in pages:
            nc.vector.memset(page[:].bitcast(I32), 0)

        def load_w1(i):
            a, first, width = loads[i]
            rows = w1[PASS * a : PASS * (a + 1), first : first + width]
            nc.sync.dma_start(w1_raw[i][:], rows.rearrange("(p j) c -> p j c", j=PACK))

        def load_cd(lo, hi):
            nc.sync.dma_start(cd_sb[:, lo:hi, :], cd[PASS * lo : PASS * hi].rearrange("(b p t) -> p b t", p=P, t=PACK))

        def load_tab(a):
            nc.sync.dma_start(tab_w[a][:], tab_words[a].rearrange("p t i -> p (t i)").bitcast(I32))

        load_tab(0)
        nc.sync.dma_start(pick[:], offs)
        for i in range(4 * KP):
            if i == SCALES_AHEAD:
                load_w1(0)
            r, a = divmod(i, KP)
            nc.sync.dma_start(tab_s[4 * a + r : P : QUADRANT, :].bitcast(I32), tab_scales[a, r:16:4, :].bitcast(I32))
        load_w1(1)
        load_tab(1)
        load_cd(0, 1)
        for i in range(2, len(loads)):
            load_w1(i)
        load_cd(1, HP)

        def load_rest():
            for q in range(P // QUADRANT):
                nc.sync.dma_start(
                    w4_s[QUADRANT * q : QUADRANT * q + 4, :, :].bitcast(I32),
                    w4_scales[:, 4 * q : 4 * q + 4, :].rearrange("a r n -> r a n").bitcast(I32),
                )
            nc.sync.dma_start(w4_w[:].bitcast(I32), w4_words.rearrange("a p c -> p a c").bitcast(I32))
            nc.sync.dma_start(place[:], offs2)
            nc.sync.dma_start(wgo_sb[:], wgo)

        taken = []

        def next_bank():
            i = len(taken)
            number = EARLY_BANKS[i] if i < len(EARLY_BANKS) else LATE_BANKS[(i - len(EARLY_BANKS)) % len(LATE_BANKS)]
            taken.append(psum_banks[number])
            return taken[-1]

        def entries(offsets, c, count=1):
            return offsets[:, CHUNK * c // GROUP : CHUNK * (c + count) // GROUP]

        v_first = kept([P, S], U32, "v_first")
        v_s = kept([P, S], U8, "v_s")
        v_second = {}

        def gather_first(c, count):
            cols = slice(CHUNK * c, CHUNK * (c + count))
            nc.vector.tensor_copy(v_first[:, cols], tab_w[0][:].bitcast(U32).indirect(entries(pick, c, count)))

        def gather_scales(c, count):
            cols = slice(CHUNK * c, CHUNK * (c + count))
            nc.vector.tensor_copy(v_s[:, cols], tab_s[:].indirect(entries(pick, c, count)))

        def gather_second(c, lo=0, hi=CHUNK):
            if c not in v_second:
                v_second[c] = kept([P, CHUNK], U32, f"v_second{c}")
            picked = pick[:, (CHUNK * c + lo) // GROUP : (CHUNK * c + hi) // GROUP]
            nc.vector.tensor_copy(v_second[c][:, lo:hi], tab_w[1][:].bitcast(U32).indirect(picked))

        def v_words(a, c, lo, hi):
            return v_first[:, CHUNK * c + lo : CHUNK * c + hi] if a == 0 else v_second[c][:, lo:hi]

        w1_w = {(b, a): kept([P, PASS], U32, f"w1_w{b}{a}") for b in range(HP) for a in range(KP)}
        w1_s = {(b, a): kept([P, PASS], U8, f"w1_s{b}{a}") for b in range(HP) for a in range(KP)}
        stages = {}

        def round_part(engine_copy, b, a, slots, lo=0, hi=PASS):
            if (b, a) not in stages:
                shape, name = [P, PACK * PASS], f"w1_bf{b}{a}"
                stages[b, a] = placed(shape, BF16, name, held_at) if (b, a) == (1, 0) else kept(shape, BF16, name)
            column = PASS * b + lo
            i = max(i for i, (at, first, width) in enumerate(loads) if at == a and first <= column)
            src = w1_raw[i][:, :, column - loads[i][1] : column - loads[i][1] + hi - lo]
            src = src.rearrange("p j (m t) -> p m j t", t=PACK)[:, :, :, slots]
            dst = stages[b, a][:].rearrange("p (t m j) -> p m j t", t=PACK, j=PACK)
            engine_copy(dst[:, lo // PACK : hi // PACK, :, slots], src)

        def round_shared(b, a, lo=0, hi=PASS):
            round_part(nc.vector.tensor_copy, b, a, slice(2, 4), lo, hi)
            round_part(nc.scalar.copy, b, a, slice(0, 2), lo, hi)

        def round_on_vector(b, a, lo=0, hi=PASS):
            for u in range(2):
                round_part(nc.vector.tensor_copy, b, a, slice(2 * u, 2 * u + 2), lo, hi)

        def quantise_w1(b, a, lo=0, hi=PASS):
            rounded = stages[b, a][:, PACK * lo : PACK * hi]
            nc.vector.quantize_mx(w1_w[b, a][:, lo:hi].bitcast(FP8X4), w1_s[b, a][:, lo:hi], rounded)

        banks, mags, h_bf, h_w, h_s, factors, forces = {}, {}, {}, {}, {}, {}, {}

        def first_pass(dst, b, t, a, c, lo, hi, start, stop):
            wcols = slice(P * t, P * (t + 1))
            nc.tensor.matmul_mx(
                dst,
                lhsT=w1_w[b, a][:, wcols].bitcast(FP8X4),
                lhsT_scale=w1_s[b, a][:, wcols],
                rhs=v_words(a, c, lo, hi).bitcast(FP8X4),
                rhs_scale=v_s[4 * a : P, CHUNK * c + lo : CHUNK * c + hi],
                start=start,
                stop=stop,
            )

        def products(b, c, s, a):
            if a == 0:
                banks[b, c, s] = next_bank()[:].rearrange("p (t c) -> p t c", t=PACK)
            for t in range(PACK):
                first, last = (a == 0 and t == 0), (a == KP - 1 and t == PACK - 1)
                first_pass(banks[b, c, s][:, t, :], b, t, a, c, STEP * s, STEP * (s + 1), first, last)

        def magnitude(b, c, s, at=None):
            if (b, c, s) not in banks:
                products(b, c, s, 0)
            products(b, c, s, 1)
            if at is None:
                mag = ring.tile([P, BANK], F32, name="mag", bufs=4)
            else:
                mag = placed([P, BANK], F32, f"mag{b}{c}{s}", at)
            mags[b, c, s] = mag[:].rearrange("p (t c) -> p t c", t=PACK)
            for t in range(PACK):
                nc.scalar.activation(
                    mags[b, c, s][:, t, :], banks[b, c, s][:, t, :], ACT.Abs, scale=cd_sb[:, b, t : t + 1]
                )

        def h_tile(b, c, at=None):
            if (b, c) not in h_bf:
                shape, name = [P, PACK * CHUNK], f"h_bf{b}{c}"
                h_bf[b, c] = kept(shape, BF16, name) if at is None else placed(shape, BF16, name, at)
            return h_bf[b, c]

        def multiply(b, c, s):
            dst = h_tile(b, c)[:, PACK * STEP * s : PACK * STEP * (s + 1)]
            nc.vector.tensor_tensor(
                dst.rearrange("p (c i t) -> p c t i", i=WALK, t=PACK),
                banks[b, c, s].rearrange("p t (c i) -> p c t i", i=WALK),
                mags[b, c, s].rearrange("p t (c i) -> p c t i", i=WALK),
                MULT,
            )

        def sign_bank(b, c, u, squares_at=None):
            if u == 0:
                if squares_at is None:
                    squares = ring.tile([P, 2, CHUNK, 2], BF16, name="squares", bufs=3)
                else:
                    squares = placed([P, 2, CHUNK, 2], BF16, f"squares{b}{c}", squares_at)
                factors[b, c] = (squares, ring.tile([P, 2, CHUNK, 2], BF16, name="signs", bufs=3))
            squares, signs = factors[b, c]
            bank = next_bank()[:].rearrange("p (e c) -> p e c", e=2)
            for e in range(2):
                for a in range(KP):
                    first_pass(bank[:, e, :], b, 2 * u + e, a, c, 0, CHUNK, a == 0, a == KP - 1)
            for e in range(2):
                t = 2 * u + e
                nc.scalar.activation(squares[:, u, :, e], bank[:, e, :], ACT.Square, scale=cd_root[:, b, t : t + 1])
            nc.scalar.activation(
                signs[:, u, :, :].rearrange("p (c i) e -> p c e i", i=2),
                bank.rearrange("p e (c i) -> p c e i", i=2),
                ACT.Sign,
            )

        def sign_product(b, c):
            squares, signs = factors[b, c]
            nc.vector.tensor_tensor(
                h_tile(b, c)[:].rearrange("p (c u e) -> p c u e", u=2, e=2),
                squares[:].rearrange("p u c e -> p c u e"),
                signs[:].rearrange("p u c e -> p c u e"),
                MULT,
            )

        def quantise_h(b, c, at=None):
            if at is None:
                h_w[b, c] = kept([P, CHUNK], U32, f"h_w{b}{c}")
            else:
                h_w[b, c] = placed([P, CHUNK], U32, f"h_w{b}{c}", at)
            h_s[b, c] = kept([P, CHUNK], U8, f"h_s{b}{c}")
            nc.vector.quantize_mx(h_w[b, c][:].bitcast(FP8X4), h_s[b, c][:], h_bf[b, c][:])

        def deliver(n, c, count=1, y_bank=None):
            if y_bank is None:
                y_bank = next_bank()
            passes = [(b, i) for b in range(HP) for i in range(count)]
            for b, i in passes:
                nc.tensor.matmul_mx(
                    y_bank[:, CHUNK * i : CHUNK * (i + 1)],
                    lhsT=w4_w[:, b, 2 * P * n : 2 * P * (n + 1)].bitcast(FP4X4),
                    lhsT_scale=w4_s[:, b, P * n : P * (n + 1)],
                    rhs=h_w[b, c + i][:].bitcast(FP8X4),
                    rhs_scale=h_s[b, c + i][:],
                    start=((b, i) == passes[0]),
                    stop=((b, i) == passes[-1]),
                )
            width = CHUNK * count
            force = kept([P, width], F32, f"force{n}{c}")
            forces[n, c] = force
            nc.scalar.activation(force[:], y_bank[:, 0:width], ACT.Copy, scale=-1.0)
            weights = wgo_sb[:, CHUNK * c : CHUNK * c + width]
            nc.vector.tensor_tensor(pages[n][:].indirect(entries(place, c, count)), force[:], weights, MULT)
            if c + count == CHUNKS and n < NT - 1:
                nc.sync.dma_start(out[P * n : P * (n + 1), :], pages[n][:])
            elif c + count == CHUNKS:
                for queue, cols in ((nc.sync, slice(0, T2 // 2)), (nc.scalar, slice(T2 // 2, T2))):
                    queue.dma_start(out[P * n : P * (n + 1), cols], pages[n][:, cols])

        nc.scalar.activation(cd_root[:, 0:1, :], cd_sb[:, 0:1, :], ACT.Sqrt)

        for u in range(2):
            round_part(nc.scalar.copy, 0, 0, slice(2 * u, 2 * u + 2))
        gather_first(0, CHUNKS)
        gather_scales(0, CHUNKS)
        load_rest()
        round_shared(0, 1)
        quantise_w1(0, 0)
        for c in range(2):
            for s in range(2):
                products(0, c, s, 0)
        quantise_w1(0, 1)
        gather_second(0, 0, STEP)
        gather_second(0, STEP, CHUNK)
        for c in range(1, CHUNKS):
            gather_second(c)

        def drag(b, c, s, at=None):
            magnitude(b, c, s, at)
            multiply(b, c, s)

        last = starts[-1]
        magnitude(0, 0, 0, at=held_at)
        magnitude(0, 0, 1)
        multiply(0, 0, 0)
        multiply(0, 0, 1)
        round_shared(1, 0)
        quantise_w1(1, 0)
        drag(0, 1, 0)
        magnitude(0, 1, 1)
        round_shared(1, 1)
        multiply(0, 1, 1)
        quantise_h(0, 0)
        quantise_w1(1, 1)
        magnitude(0, 2, 0)
        round_shared(2, 0)
        multiply(0, 2, 0)
        magnitude(0, 2, 1)
        round_on_vector(2, 1, 0, PAIR)
        multiply(0, 2, 1)
        drag(1, 0, 0)
        round_shared(2, 1, PAIR, PASS)
        quantise_w1(2, 0)
        quantise_w1(2, 1, PAIR, PASS)
        quantise_w1(2, 1, 0, PAIR)
        quantise_h(0, 1, at=last)
        quantise_h(0, 2, at=last + WORDS_BYTES)
        drag(1, 0, 1, at=last + MAG_BYTES)
        nc.scalar.activation(cd_root[:, 1:HP, :], cd_sb[:, 1:HP, :], ACT.Sqrt)
        quantise_h(1, 0)
        for s in range(2):
            products(2, 0, s, 0)
        drag(2, 0, 0)
        drag(2, 0, 1)
        quantise_h(2, 0)
        drag(2, 1, 0)
        drag(2, 1, 1)
        quantise_h(2, 1)
        deliver(0, 0)
        sign_bank(1, 1, 0)
        deliver(1, 0)
        sign_bank(1, 1, 1)
        sign_product(1, 1)
        quantise_h(1, 1)
        deliver(2, 0)

        def unit(b, c, behind, after=None):
            for u in range(2):
                sign_bank(b, c, u)
            sign_product(b, c)
            deliver(*behind)
            quantise_h(b, c)
            if after is not None:
                deliver(*after)

        sign_bank(1, 2, 0)
        deliver(3, 0)
        sign_bank(1, 2, 1)
        sign_product(1, 2)
        deliver(0, 1)
        quantise_h(1, 2)
        unit(2, 2, behind=(1, 1), after=(2, 1))
        unit(0, 3, behind=(3, 1))
        unit(1, 3, behind=(0, 2))
        unit(2, 3, behind=(1, 2), after=(2, 2))
        for n in range(NT - 1):
            deliver(n, 3)
        deliver(NT - 1, 2, 2)
